import numpy as np, ml_dtypes
CORES = [48,51,52,55]
N = 4
BF = ml_dtypes.bfloat16
W, C, M, V, D, Q = 4096, 256, 3, 5, 1, 9
LM = 127
def parts(rng):
    return (rng.integers(0, 256, (N, 8, 16, W)), rng.integers(0, W, (N, 8, 16, C)), rng.integers(0, 256, (N, 8, 16, C)),
            rng.integers(0, 16, (N, 8, 16, 1)), rng.integers(48, 81, (N, 8, 16, 1)))
def pack(x, f, z, w, lm):
    return {"rock": x.reshape(N, 128, W).astype(np.float32).astype(BF), "front": np.ascontiguousarray(f.reshape(N, 128, C)).astype(np.int32),
            "vein": z.reshape(N, 128, C).astype(np.float32).astype(BF), "w": w.reshape(N, 128, 1).astype(np.int32), "lim": lm.reshape(N, 128, 1).astype(np.int32)}
def setup_inputs(rng):
    return pack(*parts(rng))
def setup_inputs_alike(rng):
    x, f, z, w, lm = parts(rng); lm = rng.integers(10, 41, (N, 8, 16, 1)); rec = rng.integers(100, 156, (N, 8, 16, 4))
    x = np.take_along_axis(rec, rng.integers(0, 4, (N, 8, 1, W)), 3)
    far = lm + rng.choice(np.array([-1, 0, 0, 0, 1, 2, 3, 4]), (N, 8, 16, C))
    z = np.take_along_axis(rec, rng.integers(0, 4, (N, 8, 1, C)), 3) + rng.choice(np.array([-1, 1]), (N, 8, 16, C)) * far
    f[:, ::2] = rng.choice(np.array([0, W - 1, W // 2, 3]), (N, 4, 16, C))
    f[:, 1] = f[:, 1][..., rng.integers(0, 4, C)]
    return pack(x, f, z, w, lm)
def setup_inputs_corners(rng):
    x, f, z, w, lm = parts(rng); end = np.array([0, 1, 14, 15]); P = C // 2; h = np.arange(P)
    for a in range(N):
        o = [int(b) for b in rng.permutation(8)]
        for g in range(8):
            v = o[g]
            if v == 0:
                lm[a, g] = 0; w[a, g] = 0
            elif v == 1:
                lm[a, g] = LM; w[a, g] = 15
            elif v in (2, 3, 4):
                x[a, g] = rng.integers(200, 256, (16, W)); z[a, g] = rng.integers(0, 61, (16, C)); lm[a, g] = rng.integers(0, 101, (16, 1))
                s = np.arange(16)[:, None] * (W // 32) + rng.integers(0, W // 32, (16, P)); j = rng.integers(W // 2, W, (16, P))
                if v == 2:
                    k = rng.choice(end, P); l = rng.choice(end, P); k[:16] = np.repeat(end, 4); l[:16] = np.tile(end, 4)
                    s[np.maximum(l, rng.integers(0, 16, P)), h] = s[l, h]
                    j[k, h] = (s[l, h] & -8) + rng.integers(0, 8, P)
                    j[np.maximum(k, rng.integers(0, 16, P)), h] = j[k, h]
                if v == 4:
                    s[:] = W - 1; j[:] = W - 1; s[:, :P // 2] = 0; j[:, :P // 2] = 0
                    s[1:, P // 2:3 * P // 4] = W - 21; j[1:, P // 2:3 * P // 4] = W - 3
                f[a, g][:, 0::2] = s; f[a, g][:, 1::2] = j
            elif v == 5:
                r = rng.integers(64, 192, (16, 1)); x[a, g] = r; lm[a, g] = 0
                off = np.argsort(rng.random((16, C)), axis=0) >= rng.integers(Q - 2, Q + 2, C)[None, :]
                z[a, g] = r + np.where(off, rng.choice(np.array([-40, -4, 4, 40]), (16, C)), 0)
            elif v == 6:
                f[a, g] = (W - 1) * rng.integers(0, 2, (16, C)); w[a, g] = 15 * rng.integers(0, 2, (16, 1)); lm[a, g] = LM * rng.integers(0, 2, (16, 1))
            else:
                w[a, g, 0] = 15; w[a, g, 1] = 1; z[a, g][:, ::2] = 0; z[a, g, 0, ::2] = 136; z[a, g, 1, ::2] = 7; f[a, g][:, ::4] = W - 1
                for i, n, u, m in ((2, W - 3, 2037, 0), (6, W - 15, 2039, 2)):
                    z[a, g, 0, i::8] = 135; z[a, g, 1, i::8] = u - 2025; f[a, g][:, i::8] = n
                    x[a, g][:, (((n * (2 * u + 1)) >> (5 + m)) + n + 613 * m + 37 * np.arange(16)) & (W - 1)] = z[a, g][:, i][:, None]
    return pack(x, f, z, w, lm)
def setup_inputs_ends(rng):
    x, f, z, w, lm = parts(rng)
    x = 255 * np.where(rng.random((N, 8, 1, W)) < 0.4, rng.integers(0, 2, (N, 8, 1, W)), rng.integers(0, 2, (N, 8, 16, W)))
    z = 255 * np.where(rng.random((N, 8, 1, C)) < 0.4, rng.integers(0, 2, (N, 8, 1, C)), rng.integers(0, 2, (N, 8, 16, C)))
    f = (W - 1) * rng.integers(0, 2, f.shape); w = 15 * rng.integers(0, 2, w.shape); lm = LM * rng.integers(0, 2, lm.shape)
    for a, g in ((N - 1, 7), (0, 0)):
        w[a, g] = 15; z[a, g][:, [0, C - 2, C - 1]] = 255; z[a, g][:, [3, C - 3]] = 0
        z[a, g][:, [5, C - 4]] = rng.permutation(np.array([255] * 9 + [26] + [0] * 6))[:, None]
        f[a, g, 15][[0, 3, 5, C - 4, C - 3, C - 2, C - 1]] = W - 1
        for u in ((16 * 15 * 255) & 2047, 0):
            x[a, g][:, ((((W - 1) * (2 * u + 1)) >> (5 + np.arange(M))) + W - 1 + 613 * np.arange(M) + 37 * 15) & (W - 1)] = 0
    return pack(x, f, z, w, lm)
def setup_inputs_full(rng):
    x, f, z, w, lm = parts(rng); P = C // 2; h = np.arange(P); n = W // C
    b = int(rng.integers(0, N)); g = int(rng.integers(0, 8)); rest = [q for q in range(N) if q not in (b, (b - D) % N)]; a = rest[int(rng.integers(0, len(rest)))]
    for q in range(N):
        if q != a:
            x[q, g] = rng.integers(200, 256, (16, W)); z[q, g] = rng.integers(0, 61, (16, C)); lm[q, g] = 0
            f[q, g] = n * rng.permutation(C)[None, :] + rng.integers(0, n, (16, C))
    i = np.array([P - 1, 0, P // 2])[:int(rng.integers(1, 4))]
    f[b, g, 15, 2 * i + 1] = (f[b, g, rng.integers(0, 16, len(i)), 2 * i] & -8) + rng.integers(0, 8, len(i))
    x[a] = rng.integers(200, 256, (8, 16, W)); z[a] = rng.integers(0, 61, (8, 16, C)); lm[a] = rng.integers(80, 121, (8, 16, 1))
    k = rng.integers(0, 16, (8, P)); l = rng.integers(0, 16, (8, P)); gr = np.arange(8)[:, None]; fa = f[a]
    fa[gr, k, 2 * h + 1] = (fa[gr, l, 2 * h] & -8) + rng.integers(0, 8, (8, P))
    o = [int(c) for c in rng.permutation(8)]
    f[a, o[0]] = 0; w[a, o[0]] = 0
    f[a, o[1]] = W - 1; w[a, o[1]] = 0; w[a, o[1], 0] = W >> 9; z[a, o[1], 0] = 32
    return pack(x, f, z, w, lm)
def setup_inputs_spread(rng):
    x = np.minimum((np.exp2(8 * rng.random((N, 8, 1, W))) * rng.random((N, 8, 16, W))).astype(np.int64), 255)
    z = np.minimum((np.exp2(8 * rng.random((N, 8, 1, C))) * rng.random((N, 8, 16, C))).astype(np.int64), 255)
    f = np.minimum((W * rng.random((N, 8, 16, C)) ** 3).astype(np.int64), W - 1)
    return pack(x, f, z, rng.integers(0, 16, (N, 8, 16, 1)), np.minimum((128 * rng.random((N, 8, 16, 1)) ** 2).astype(np.int64), LM))
def check_inputs(d):
    bad = []
    for k, hi in (("rock", 255), ("front", W - 1), ("vein", 255), ("w", 15), ("lim", LM)):
        v = np.asarray(d[k]).astype(np.float64)
        if not (np.min(v) >= 0 and np.max(v) <= hi): bad.append("range of " + k)
        elif np.any(v != np.floor(v)): bad.append("whole numbers in " + k)
    return bad
def reference(rock, front, vein, w, lim):
    x = rock.astype(np.float32).astype(np.int64).reshape(N, 8, 16, W)
    f = front.astype(np.int64).reshape(N, 8, 16, C)
    z = vein.astype(np.float32).astype(np.int64).reshape(N, 8, 16, C)
    wt = w.astype(np.int64).reshape(N, 8, 16, 1); lm = lim.astype(np.int64).reshape(N, 8, 16, 1)
    place = np.arange(16)[:, None]; ci = np.arange(C); met = np.zeros(N, np.int64)
    for t in range(V):
        if t > 0:
            f = np.roll(f, D, axis=0); z = np.roll(z, D, axis=0)
        u = np.add.reduce(wt * z, axis=2) & 2047
        dig = np.add.reduce(z, axis=2) & 15
        top = (lm + (met & 3)[:, None, None, None])[..., None]
        for m in range(M):
            c = (((f * (2 * u[:, :, None, :] + 1)) >> (5 + m)) + f + 613 * m + 37 * place) & (W - 1)
            v = np.take_along_axis(x, c.reshape(N, 8, 1, 16 * C), 3).reshape(N, 8, 16, 16, C)
            dif = np.abs(v - z[:, :, :, None, :])
            score = np.add.reduce(dif, axis=2); near = np.count_nonzero(dif <= top, axis=2)
            if m == 0:
                bs, bc, bn = score, c, near
            else:
                less = score < bs; bs = np.where(less, score, bs); bc = np.where(less, c, bc); bn = np.where(less, near, bn)
        f = np.where(bn >= Q, bc, f)
        sen = ci[((ci >> t) & 1) == 0]; jun = sen + (1 << t)
        fs = f[..., sen]; fj = f[..., jun]
        eq = ((fj[:, :, :, None, :] >> 3) == (fs[:, :, None, :, :] >> 3)).reshape(N, 8, 256, C // 2)
        meet = np.any(eq, axis=2)[:, :, None, :]; first = np.argmax(eq, axis=2)[:, :, None, :]
        k = first >> 4; l = first & 15
        met = np.count_nonzero(meet, axis=(1, 2, 3))
        src = place - l + k
        ns = np.where(meet & (place > l) & (src <= 15), np.take_along_axis(fj, np.minimum(np.maximum(src, 0), 15), 2), fs)
        nj = np.where(meet & (place >= k), (((fj * fs) >> 5) + fj + u[..., jun][:, :, None, :]) & (W - 1), fj)
        f = f.copy(); f[..., sen] = ns; f[..., jun] = nj
        e = np.take_along_axis(f, dig[:, :, None, :], 2)
        old = np.take_along_axis(x, e, 3)
        lo = np.full((N, 8, W), C)
        np.minimum.at(lo, (np.arange(N)[:, None, None], np.arange(8)[None, :, None], e[:, :, 0]), np.broadcast_to(ci, (N, 8, C)))
        zl = np.take_along_axis(z, np.minimum(lo, C - 1)[:, :, None, :], 3)
        x = np.where((lo < C)[:, :, None, :], np.maximum(x - (zl >> 2), 0), x)
        z = (z + old) >> 1
    return {"yx": x.reshape(N, 128, W).astype(np.float32).astype(BF), "yf": f.reshape(N, 128, C).astype(np.float32), "yz": z.reshape(N, 128, C).astype(np.float32).astype(BF)}

@@ -1,0 +1,657 @@
+import comms_topo
+from concourse.mybir import AluOpType as A, AxisListType, ActivationFunctionType as F
+
+W, C, V, Q = 4096, 256, 5, 9
+H = 128
+TRASH = W
+VPART = [64, 64, 64]
+
+SCRATCH = {}
+BUF = {}
+PLACE = {}
+POOL = {"bfloat16": ["PoolB", 0], "float16": ["PoolH", 0], "float32": ["PoolF", 0], "int32": ["PoolI", 0], "uint16": ["PoolU", 0]}
+SEMAPHORES = ["cV", "cS", "cP", "cG", "loc"]
+
+
+def _sb(name, cols, dt):
+    BUF[name] = ("sbuf", [128] + (cols if isinstance(cols, list) else [cols]), dt)
+    if isinstance(cols, list):
+        SCRATCH[name] = BUF[name]
+        return
+    step = 8 if dt in ("float32", "int32") else 16
+    p = POOL[dt]
+    PLACE[name] = (p[0], p[1])
+    p[1] += (cols + step - 1) // step * step
+    SCRATCH[p[0]] = ("sbuf", [128, p[1]], dt)
+
+
+def _declare():
+    b, h, f, i, u = "bfloat16", "float16", "float32", "int32", "uint16"
+    _sb("X", W + C, b)
+    _sb("vein0", C, b); _sb("front0", C, i); _sb("w0", 1, i); _sb("lim0", 1, i)
+    _sb("PI", 1, i); _sb("CI", 128, i); _sb("C15", 128, i); _sb("CG", 128, i)
+    _sb("ci", 32, i)
+    _sb("cf", 64, f)
+    _sb("OHK", 16, f)
+    for n in ("BDb", "Ib", "NIb", "W2", "S256", "LT", "LT0", "KBD", "BD64", "BD0"):
+        _sb(n, 128, b)
+    _sb("IND", 8, b); _sb("IND128", 8, b); _sb("HC", 64, b); _sb("RB", 64, b)
+    _sb("BDh", 128, h); _sb("NIh", 128, h); _sb("WI", 160, h); _sb("WC", 160, i)
+    _sb("BL", 16 * 128, h); _sb("PW", 8 * 128, b)
+    _sb("RM", 7 * 128, h); _sb("CC", 7 * 8, h); _sb("PM", 5 * 128, h)
+    _sb("REP", 16 * H, b); _sb("REPI", 16 * H, i)
+    _sb("SC0", 64, b); _sb("TRI", [8, 16], b); _sb("ONE", 128, f)
+    _sb("TRC", 16, f); _sb("TRI0", 16, i)
+    for k in range(2):
+        s = str(k)
+        for t in range(V):
+            _sb("Z%d%d" % (t, k), H, b); _sb("TB%d%d" % (t, k), 4 * H, h)
+        for t in range(V - 1):
+            _sb("SN%d%d" % (t, k), H, h); _sb("SZ%d%d" % (t, k), H, b)
+        _sb("VI" + s, 2 * H, i); _sb("VS" + s, 2 * H, i); _sb("MS" + s, H, b); _sb("NK" + s, 3 * H, f)
+        _sb("QI" + s, 3 * H, i); _sb("QS" + s, 3 * H, i); _sb("OF" + s, 3 * H, u); _sb("ZR" + s, 16 * H, b); _sb("ZT" + s, H, b); _sb("NZT" + s, H, b)
+        _sb("U32" + s, 64, f); _sb("ZQ" + s, H, h)
+        _sb("K0" + s, H, f); _sb("K1" + s, H, f); _sb("KI" + s, H, i); _sb("YI" + s, H, i); _sb("OK" + s, H, i)
+        _sb("MK" + s, 4 * H, b); _sb("PR" + s, 4 * H, h)
+        _sb("GS" + s, 64, h); _sb("JR" + s, 256, h); _sb("NF" + s, H, f); _sb("FC" + s, H, h); _sb("EQ" + s, 1024, b)
+        _sb("M12" + s, H, b); _sb("OH" + s, 64, b); _sb("MM" + s, H, b); _sb("P12" + s, H, b); _sb("TP" + s, 64, b)
+        _sb("MS1" + s, 64, b); _sb("MS2" + s, 64, b)
+        _sb("DM" + s, 64, f); _sb("DS" + s, 64, f); _sb("DO" + s, 4, u); _sb("TAB" + s, 2048, f)
+        _sb("J32" + s, 64, f); _sb("JQ" + s, 64, i); _sb("JT" + s, 64, i); _sb("NEW" + s, H, f)
+        _sb("PA" + s, H, h); _sb("PB" + s, H, h); _sb("CNT" + s, 1, f)
+        _sb("FS" + s, H, h); _sb("ETF" + s, H, h); _sb("EMP" + s, H, h); _sb("EMN" + s, H, h); _sb("EC" + s, H, h)
+        _sb("EPF" + s, 8, f); _sb("YO" + s, 8, u); _sb("ECL" + s, 8, f); _sb("YB" + s, H, b); _sb("ZH" + s, H, h)
+        _sb("ED" + s, [8, H], b); _sb("FLG" + s, H, b); _sb("DTM" + s, H, h); _sb("T1" + s, 8, f); _sb("T2" + s, 8, f)
+        _sb("SO" + s, 8, u); _sb("NX" + s, H, b)
+    _sb("EX", [8, H], b)
+    _sb("EI", 2, i); _sb("TOP", 1, f); _sb("YF", C, f); _sb("YZ", C, b)
+    for k in range(3):
+        _sb("D%d" % k, 16 * H, b); _sb("G%d" % k, 16 * H, b); _sb("L%d" % k, 16 * H, b)
+    for k in range(8):
+        SCRATCH["B%d" % k] = BUF["B%d" % k] = ("psum", [128, 512], "float32")
+    for t in range(1, V):
+        for k in range(2):
+            SEMAPHORES.append("an%d%d" % (t, k)); SEMAPHORES.append("az%d%d" % (t, k))
+    for k in range(20):
+        SEMAPHORES.append("d%d" % k)
+
+
+_declare()
+
+CY = 0.00083
+FIX = {"V": 0.06, "S": 0.10, "P": 0.03, "G": 0.15, "Y": 0.1, "A": 0.1}
+LAT = 0.08
+
+
+class _Nothing:
+    pass
+
+
+def _graph():
+    return {"ops": [], "acc": {}, "bank": {}}
+
+
+def _add(gr, q, cost, fn, R, Wr, sem=None):
+    ops = gr["ops"]; n = len(ops); deps = set()
+    for w, regs in ((False, R), (True, Wr)):
+        for (name, a, b) in regs:
+            if BUF.get(name, ("",))[0] == "psum":
+                ep = gr["bank"].setdefault(name, [None, [], []])
+                if ep[0] != q:
+                    ep[2] = ep[1]; ep[1] = []; ep[0] = q
+                for o in ep[2]:
+                    deps.add(o[0])
+                for o in ep[1]:
+                    if o[1] < b and a < o[2] and (w or o[3]):
+                        deps.add(o[0])
+                ep[1].append((n, a, b, w))
+            else:
+                lst = gr["acc"].setdefault(name, [])
+                keep = []
+                for o in lst:
+                    if o[1] < b and a < o[2] and (w or o[3]):
+                        deps.add(o[0])
+                        if w and a <= o[1] and o[2] <= b and o[0] != n:
+                            continue
+                    keep.append(o)
+                keep.append((n, a, b, w))
+                gr["acc"][name] = keep
+    deps.discard(n)
+    ops.append({"q": q, "cost": cost, "fn": fn, "deps": sorted(deps), "sem": sem})
+    return n
+
+
+def _order(ops):
+    n = len(ops); succ = [[] for _ in ops]; need = [0] * n
+    for i, o in enumerate(ops):
+        need[i] = len(o["deps"])
+        for d in o["deps"]:
+            succ[d].append(i)
+    pr = [0.0] * n
+    for i in range(n - 1, -1, -1):
+        pr[i] = ops[i]["cost"] + max([pr[s] + LAT for s in succ[i]] or [0.0])
+    free = {}; fin = [0.0] * n; est = [0.0] * n; out = []
+    ready = {}
+    for i in range(n):
+        if need[i] == 0:
+            ready.setdefault(ops[i]["q"], []).append(i)
+    while any(ready.values()):
+        best = None
+        for q, lst in ready.items():
+            if not lst:
+                continue
+            f = free.get(q, 0.0)
+            t0 = min(max(f, est[i]) for i in lst)
+            c = max((i for i in lst if max(f, est[i]) <= t0 + 0.04), key=lambda i: pr[i])
+            st = max(f, est[c])
+            if best is None or st < best[0]:
+                best = (st, c, q)
+        st, c, q = best
+        ready[q].remove(c)
+        dur = ops[c]["cost"]
+        hold = dur
+        if ops[c]["sem"] is not None:
+            hold = FIX.get(q, 0.1)
+        free[q] = st + hold if q != "A" else 0.0
+        fin[c] = st + dur
+        ops[c]["start"] = st; ops[c]["fin"] = fin[c]
+        out.append(c)
+        for s in succ[c]:
+            need[s] -= 1
+            est[s] = max(est[s], fin[c] + LAT)
+            if need[s] == 0:
+                ready.setdefault(ops[s]["q"], []).append(s)
+    return out
+
+
+def rank_program(g, core, T, topo):
+    rank = T.rank_of(core)
+    if rank is None:
+        return
+    nxt = T.cores[(rank + 1) % len(T.cores)]
+    gr = _graph()
+    vec, sca, ten, syn = g.vector, g.scalar, g.tensor, g.sync
+
+    def sl(n, a=0, b=None, st=None):
+        p, o = PLACE.get(n, (n, 0))
+        b = BUF[n][1][1] if b is None else b
+        return T[p][:, o + a:o + b:st] if st else T[p][:, o + a:o + b]
+
+    def ap(r):
+        return sl(*r)
+
+    def full(n):
+        return (n, 0, BUF[n][1][1])
+
+    def reg(r):
+        return (r[0], r[1], r[2])
+
+    def cnt(r):
+        return (r[2] - r[1] + (r[3] if len(r) > 3 else 1) - 1) // (r[3] if len(r) > 3 else 1)
+
+    def two(*rs):
+        return all(BUF[r[0]][2] in ("bfloat16", "float16", "uint16") for r in rs)
+
+    def vc(cy):
+        return FIX["V"] + max(64, cy) * CY
+
+    def scal(s):
+        return [reg(s)] if isinstance(s, tuple) else []
+
+    def sv(s):
+        return ap(s) if isinstance(s, tuple) else s
+
+    def tc(o, i):
+        _add(gr, "V", vc(cnt(i) * (0.5 if two(o, i) else 1)), lambda: vec.tensor_copy(out=ap(o), in_=ap(i)), [reg(i)], [reg(o)])
+
+    def ts(o, i, s1, op0, s2=None, op1=None):
+        def fn():
+            if op1 is None:
+                return vec.tensor_scalar(out=ap(o), in0=ap(i), scalar1=sv(s1), scalar2=None, op0=op0)
+            return vec.tensor_scalar(out=ap(o), in0=ap(i), scalar1=sv(s1), scalar2=sv(s2), op0=op0, op1=op1)
+        _add(gr, "V", vc(cnt(i) * (0.5 if two(o, i) else 1)), fn, [reg(i)] + scal(s1) + scal(s2), [reg(o)])
+
+    def tt(o, i, j, op):
+        ps = "psum" in (BUF[i[0]][0], BUF[j[0]][0])
+        _add(gr, "V", vc(cnt(i) * (1 if ps else 2)), lambda: vec.tensor_tensor(out=ap(o), in0=ap(i), in1=ap(j), op=op),
+             [reg(i), reg(j)], [reg(o)])
+
+    def act(o, i, func=F.Identity, bias=None, scale=None):
+        def fn():
+            kw = {}
+            if bias is not None:
+                kw["bias"] = sv(bias)
+            if scale is not None:
+                kw["scale"] = sv(scale)
+            return sca.activation(out=ap(o), in_=ap(i), func=func, **kw)
+        _add(gr, "S", FIX["S"] + cnt(i) * CY, fn, [reg(i)] + scal(bias) + scal(scale), [reg(o)])
+
+    def mm(lst):
+        def fn():
+            x = None
+            for o, l, r, s, e in lst:
+                x = ten.matmul(ap(o), ap(l), ap(r), s, e)
+            return x
+        c = FIX["P"]; R = []; Wr = []
+        for o, l, r, s, e in lst:
+            c += max(min(64, cnt(l)), cnt(r)) * CY * (4 if BUF[l[0]][2] == "float32" else 1)
+            R += [reg(l), reg(r)]; Wr.append(reg(o))
+        lo = min(x[1] for x in Wr); hi = max(x[2] for x in Wr)
+        _add(gr, "P", c, fn, sorted(set(R)), [(Wr[0][0], lo, hi)])
+
+    dn = [0]
+
+    def load(q, o, src):
+        s = "d%d" % dn[0]; dn[0] += 1
+        eng = {"Y": syn, "S": sca}[q]
+        byts = cnt(o) * 128 * 2
+        _add(gr, q, 2.0 + byts / 150000.0, lambda: eng.dma_start(ap(o), src), [], [reg(o)], sem=s)
+
+    def store(q, dst, i):
+        s = "d%d" % dn[0]; dn[0] += 1
+        eng = {"Y": syn, "S": sca}[q]
+        _add(gr, q, 2.0 + cnt(i) * 256 / 150000.0, lambda: eng.dma_start(dst, ap(i)), [reg(i)], [], sem=s)
+
+    load("Y", full("vein0"), T.vein[:]); load("S", full("front0"), T.front[:])
+    load("Y", full("w0"), T.w[:]); load("S", full("lim0"), T.lim[:])
+    for k in range(4):
+        load("YS"[k & 1], ("X", k * 1024, (k + 1) * 1024), T.rock[:, k * 1024:(k + 1) * 1024])
+
+    def iota(name, pattern, base, cm, cols):
+        _add(gr, "G", 0.15 + 2 * cols * CY, lambda: g.iota(sl(name), pattern, base, cm), [], [full(name)])
+
+    iota("PI", [[1, 1]], 0, 1, 1); iota("CI", [[1, 128]], 0, 0, 128); iota("WC", [[1, 160]], -16, 0, 160)
+    iota("TRI0", [[16, 16]], TRASH, 0, 16)
+    iota("REPI", [[1, 128], [0, 16]], 0, 0, 2048)
+    nc = [0]
+
+    def col():
+        nc[0] += 1
+        return ("cf", nc[0] - 1, nc[0])
+    ni = [0]
+
+    def icol():
+        ni[0] += 1
+        return ("ci", ni[0] - 1, ni[0])
+    PI, CI, C15, CG = full("PI"), full("CI"), full("C15"), full("CG")
+    PF = col(); tc(PF, PI)
+    k_i, g_i = icol(), icol()
+    ts(k_i, PI, 15, A.bitwise_and); ts(g_i, PI, 4, A.arith_shift_right)
+    KF, GF = col(), col(); tc(KF, k_i); tc(GF, g_i)
+    ts(CG, CI, 4, A.arith_shift_right); ts(C15, CI, 15, A.bitwise_and)
+    BDb, BDh, Ib, NIb, NIh = full("BDb"), full("BDh"), full("Ib"), full("NIb"), full("NIh")
+    ts(BDb, CG, GF, A.is_equal); tc(BDh, BDb)
+    ts(Ib, CI, PF, A.is_equal); ts(NIb, Ib, -1.0, A.mult)
+    ts(full("WI"), full("WC"), PF, A.is_equal); Ih = ("WI", 16, 144)
+    ts(NIh, Ih, -1.0, A.mult)
+    WF, LF = col(), col(); tc(WF, full("w0")); tc(LF, full("lim0"))
+    W2, S256 = full("W2"), full("S256")
+    ts(W2, BDb, WF, A.mult, 2.0, A.mult); ts(S256, BDb, 256.0, A.mult)
+    KS = col(); ts(KS, KF, 256.0, A.mult, 1.0, A.add)
+    NKC = []
+    for m in range(3):
+        c = col(); NKC.append(c); sc = float(1 << (5 + m))
+        ts(c, KF, 37.0 * sc, A.mult, (613 * m + 2048) * sc - 8388608.0, A.add)
+    TOP = full("TOP"); tc(TOP, LF)
+    ts(full("REP"), full("REPI"), PF, A.is_equal)
+    IND, IND128 = full("IND"), full("IND128")
+    ts(IND, ("CI", 0, 8), GF, A.is_equal); ts(IND128, IND, 128.0, A.mult)
+    OHK = full("OHK"); ts(OHK, ("CI", 0, 16), KF, A.is_equal)
+
+    def BL(l):
+        return ("BL", l * 128, l * 128 + 128)
+
+    def PW(j):
+        return ("PW", j * 128, j * 128 + 128)
+    for l in range(16):
+        ts(BL(l), BDh, ("OHK", l, l + 1), A.mult)
+    for j in range(8):
+        ts(PW(j), Ib, float(1 << j), A.mult)
+    LT, LT0 = full("LT"), full("LT0")
+    ts(LT0, C15, KF, A.is_gt, 4.0, A.mult); tt(LT0, LT0, BDb, A.mult); tt(LT, LT0, Ib, A.subtract)
+    BD0 = full("BD0"); ts(BD0, BDb, ("OHK", 0, 1), A.mult)
+    KBD, BD64 = full("KBD"), full("BD64")
+    ts(KBD, BDb, KF, A.mult, 64.0, A.mult); ts(BD64, BDb, 64.0, A.mult)
+    HC = full("HC"); ts(HC, ("CI", 0, 64), 0.0625, A.mult)
+    P16, P15c = col(), col()
+    ts(P16, KF, 0.0, A.mult, 65536.0, A.add)
+    for b in range(4):
+        x, y = icol(), col()
+        ts(x, k_i, b, A.arith_shift_right, 1, A.bitwise_and)
+        ts(y, x, 2.0 ** -(1 << b) - 1.0, A.mult, 1.0, A.add)
+        tt(P16, P16, y, A.mult)
+    ts(P15c, P16, 0.5, A.mult)
+    M2C = col(); ts(M2C, KF, -64.0, A.mult, 64.0 * 31 + 63, A.add)
+    RB = full("RB"); ts(RB, ("C15", 0, 64), KF, A.is_equal)
+    SC0 = full("SC0"); ts(SC0, ("C15", 0, 64), 0.0, A.not_equal)
+    for c in range(8):
+        _add(gr, "V", vc(16), lambda c=c: vec.tensor_scalar(out=T.TRI[:, c, :], in0=sl("C15", 0, 16), scalar1=ap(KF), scalar2=None, op0=A.is_gt),
+             [("C15", 0, 16), KF], [("TRI", c, c + 1)])
+    ts(full("TRC"), full("TRI0"), KF, A.add)
+    _add(gr, "V", vc(128), lambda: vec.memset(sl("ONE"), 1.0), [], [full("ONE")])
+    for k in range(2):
+        _add(gr, "V", vc(2048), lambda k=k: vec.memset(sl("TAB%d" % k), 0.0), [], [full("TAB%d" % k)])
+
+    def RM(s):
+        return ("RM", s * 128, s * 128 + 128)
+
+    def CC(s):
+        return ("CC", s * 8, s * 8 + 8)
+
+    def PM(s):
+        return ("PM", (s - 1) * 128, s * 128)
+    rot_i = icol(); rot_h = icol(); lo_i = icol()
+    for s in (0, 1, 6, 2, 5, 3, 4):
+        rf, lf, hf = col(), col(), col()
+        if s == 0:
+            ts(rot_i, PI, 0.0, A.add)
+        else:
+            ts(rot_i, PI, float(1 << s), A.mult); ts(rot_i, rot_i, 127, A.bitwise_and)
+            ts(rot_h, PI, 7 - s, A.arith_shift_right); tt(rot_i, rot_i, rot_h, A.add)
+        tc(rf, rot_i); ts(lo_i, rot_i, 15, A.bitwise_and); tc(lf, lo_i)
+        ts(lo_i, rot_i, 4, A.arith_shift_right); tc(hf, lo_i)
+        ts(RM(s), C15, lf, A.is_equal); ts(CC(s), ("CI", 0, 8), hf, A.is_equal)
+        if 1 <= s <= 5:
+            ts(PM(s), CI, rf, A.is_equal)
+
+    for k in range(2):
+        for p in range(2):
+            ts(("TB0%d" % k, 384 + 64 * p, 448 + 64 * p), ("front0", k * H + p, (k + 1) * H, 2), -2048.0, A.add)
+            act(("Z0%d" % k, 64 * p, 64 * p + 64), ("vein0", k * H + p, (k + 1) * H, 2))
+
+    def view(h, t):
+        s = str(h)
+        return lambda n, a=None, b=None, st=None: ((n + s,) + ((0, BUF[n + s][1][1]) if a is None else ((a, b) if st is None else (a, b, st))))
+
+    BU, BM, BS0, BS1 = "B6", "B7", "B4", "B5"
+    BK = ["B2", "B3"]
+
+    def numbers(h, t):
+        v = view(h, t)
+        Z = full("Z%d%d" % (t, h)); tb = "TB%d%d" % (t, h); NCt = (tb, 384, 512)
+        mm([((BU, 256, 384), Ih, NCt, True, True)])
+        act((BU, 384, 512), (BU, 256, 384), bias=None, scale=None) if False else None
+        for m in range(3):
+            act(v("NK", m * H, m * H + H), (BU, 256, 384), F.Identity, NKC[m], float(1 << (5 + m)))
+        mm([((BU, 0, 128), W2, Z, True, True), ((BU, 128, 256), S256, Z, True, True)])
+        ts(v("VI"), (BU, 0, 256), 1.0, A.add); ts(v("VS"), v("VI"), 4095, A.bitwise_and)
+        ts((BU, 384, 512), (BU, 256, 384), 2048.0, A.add)
+        tt((BU, 0, 128), (BU, 384, 512), v("VS", 0, 128), A.mult)
+        for m in range(3):
+            o = (m * H, m * H + H)
+            tt(v("QI", *o), (BU, 0, 128), v("NK", *o), A.add)
+            ts(v("QS", *o), v("QI", *o), 5 + m, A.arith_shift_right, 4095, A.bitwise_and)
+            tc(v("OF", *o), v("QS", *o))
+        bk = "B%d" % (dbank[0] & 1); dbank[0] += 1
+        mm([((bk, 0, 128), Z, Ib, True, True)])
+        act(v("ZT"), (bk, 0, 128)); act(v("NZT"), (bk, 0, 128), scale=-1.0)
+        for a in range(0, 16 * max(VPART), 512):
+            bk = "B%d" % (dbank[0] & 1); dbank[0] += 1
+            mm([((bk, 0, 512), v("ZT"), ("REP", a, a + 512), True, True)])
+            act(v("ZR", a, a + 512), (bk, 0, 512))
+        ts((tb, 0, 384), v("OF"), -2048.0, A.add)
+        ts(v("MS"), v("VS", 128, 256), KS, A.is_equal)
+        ts(v("U32"), v("VS", 64, 128), 16.0, A.mult, -16.0 - 8388608.0, A.add)
+        ts(v("ZQ"), Z, 0.25, A.mult, 1031.625, A.add)
+
+    unit = [0]
+    dbank = [0]
+
+    def scores(h, t):
+        v = view(h, t); zr = "ZR%d" % h
+        for m in range(3):
+            u = unit[0] % 3; unit[0] += 1
+            D, G, L = "D%d" % u, "G%d" % u, "L%d" % u
+            nv = VPART[m]
+            of = "OF%d" % h
+            XW = ("X", 0, W)
+
+            def vg(a, b, m=m, D=D):
+                _add(gr, "V", 0.05 + 1.5 * CY * 16 * (b - a), lambda: vec.tensor_tensor(
+                    out=sl(D, 16 * a, 16 * b), in0=sl("X", 0, W).indirect(sl(of, m * H + a, m * H + b)), in1=sl(zr, 16 * a, 16 * b), op=A.subtract),
+                    [XW, (of, m * H + a, m * H + b), (zr, 16 * a, 16 * b)], [(D, 16 * a, 16 * b)])
+
+            def sg(a, b, m=m, G=G):
+                _add(gr, "S", 0.065 + 1.5 * CY * 16 * (b - a), lambda: sca.activation(
+                    out=sl(G, 16 * a, 16 * b), in_=sl("X", 0, W).indirect(sl(of, m * H + a, m * H + b)), func=F.Identity),
+                    [XW, (of, m * H + a, m * H + b)], [(G, 16 * a, 16 * b)])
+            for a in range(0, nv, 32):
+                vg(a, a + 32)
+            for a in range(nv, H, 32):
+                sg(a, a + 32)
+            for a in range(nv, H, 32):
+                bk = "B%d" % (dbank[0] & 1); dbank[0] += 1
+
+                r = (16 * a, 16 * a + 512)
+                mm([((bk, 0, 512), v("NZT"), ("REP",) + r, True, False), ((bk, 0, 512), Ib, (G,) + r, False, True)])
+                act((D, 16 * a, 16 * a + 512), (bk, 0, 512), F.Abs)
+            for a in range(0, nv, 32):
+                act((D, 16 * a, 16 * a + 512), (D, 16 * a, 16 * a + 512), F.Abs)
+            for a in range(0, H, 64):
+                r = (16 * a, 16 * a + 1024)
+                ts((L,) + r, (D,) + r, TOP, A.is_le, 2.0 * m + 0.4375, A.add)
+            for k0 in range(0, 16, 8):
+                mm([x for k in range(k0, k0 + 8) for x in (
+                    ((BK[h], m * H + k, m * H + 128, 16), (D, k, 2048, 16), IND128, True, False),
+                    ((BK[h], m * H + k, m * H + 128, 16), (L, k, 2048, 16), IND, False, True))])
+
+    def choose(h, t):
+        v = view(h, t); B = BK[h]; tb = "TB%d%d" % (t, h)
+        act(v("K0"), (B, 0, 128))
+        tt(v("K1"), v("K0"), (B, 128, 256), A.min)
+        tt(v("KI"), v("K1"), (B, 256, 384), A.min)
+        ts(v("YI"), v("KI"), 4, A.arith_shift_right, 7, A.bitwise_and)
+        ts(v("OK"), v("KI"), 16, A.bitwise_and)
+        for m in range(3):
+            ts(v("MK", m * H, m * H + H), v("YI"), 2.0 * m + 1.0, A.is_equal)
+        ts(v("MK", 384, 512), v("OK"), 0.0, A.is_equal)
+        mm([((BS0, s * H, s * H + H), v("MK", s * H, s * H + H), Ib, True, True) for s in range(4)])
+        tt(v("PR"), (BS0, 0, 512), full(tb), A.mult)
+        mm([((BM, 0, 128), Ih, v("PR", s * H, s * H + H), s == 0, s == 3) for s in range(4)])
+
+    def meet(h, t):
+        v = view(h, t)
+        NPs, NPj, NPa = (BM, 0, 64), (BM, 64, 128), (BM, 0, 128)
+        ts(v("GS"), NPs, 0.125, A.mult, 1287.5625, A.add)
+        ts(v("JR", 0, 64), NPj, 0.125, A.mult, 1287.5625, A.add)
+        tc(v("FC"), NPa)
+        act(v("NF"), NPa, F.Identity, B2048)
+        act(v("J32"), NPj, F.Identity, B65536, 32.0)
+        tc(v("JR", 64, 128), v("JR", 0, 64)); tc(v("JR", 128, 256), v("JR", 0, 128))
+        for x in range(2):
+            bk = (BS0, BS1)[x]
+            mm([((bk, 64 * l, 64 * l + 64), BL(8 * x + l), v("GS"), True, True) for l in range(8)])
+            for y in range(2):
+                tt(v("EQ", 512 * x + 256 * y, 512 * x + 256 * y + 256), (bk, 256 * y, 256 * y + 256), v("JR"), A.is_equal)
+        for x in range(4):
+            lo, hi = max(2, 8 * x), min(31, 8 * x + 8)
+            bk = (BS0, BS1)[x & 1]
+            mm([((bk, 64 * (d - 8 * x), 64 * (d - 8 * x) + 64), ("WI", d, d + 128), v("FC", 64, 128), True, True) for d in range(lo, hi)])
+            act(v("TAB", 64 * lo, 64 * hi), (bk, 64 * (lo - 8 * x), 64 * (hi - 8 * x)))
+        for x in range(2):
+            mm([((BM, 128 + 64 * x, 192 + 64 * x), PW(7 - l), v("EQ", 512 * x + 64 * l, 512 * x + 64 * l + 64), l == 0, l == 7) for l in range(8)])
+        ts(v("M12"), (BM, 128, 256), 0.0, A.is_gt)
+        mm([((BM, 256, 320), LT, v("M12", 0, 64), True, False), ((BM, 256, 320), LT, v("M12", 64, 128), False, True)])
+        ts(v("OH"), (BM, 256, 320), 0.0, A.is_lt)
+        tt(v("P12", 0, 64), (BM, 128, 192), v("OH"), A.mult)
+        tt(v("P12", 64, 128), (BM, 192, 256), v("OH"), A.mult)
+        mm([((BM, 320, 384), S256, v("P12", 0, 64), True, False), ((BM, 320, 384), BDb, v("P12", 64, 128), False, True)])
+        ts(v("TP"), (BM, 320, 384), P15c, A.is_ge)
+        mm([((BM, 384, 448), KBD, v("OH"), True, False), ((BM, 384, 448), BDb, HC, False, False), ((BM, 384, 448), BD64, v("TP"), False, True)])
+        tt(v("DM"), (BM, 384, 448), RB, A.mult)
+        _add(gr, "V", vc(64), lambda: vec.tensor_tensor_scan(ap(v("DS")), ap(SC0), ap(v("DM")), 0.0, A.mult, A.add), [SC0, v("DM")], [v("DS")])
+        tc(v("DO"), v("DS", 15, 64, 16))
+        do = "DO%d" % h; tab = "TAB%d" % h; new = "NEW%d" % h
+        _add(gr, "S", 0.065 + 64 * 1.5 * CY, lambda: sca.activation(out=sl(new, 0, 64), in_=sl(tab).indirect(sl(do)), func=F.Identity),
+             [full(tab), full(do)], [(new, 0, 64)])
+        ts(v("MS1"), (BM, 320, 384), P16, A.is_ge)
+        ts(v("MS2"), (BM, 384, 448), M2C, A.is_le)
+        tt(v("MM", 0, 64), v("MS1"), v("MS2"), A.mult)
+        ts(v("MM", 64, 128), (BM, 256, 320), 0.0, A.not_equal)
+        tt((BM, 448, 512), v("NF", 64, 128), v("NF", 0, 64), A.mult)
+        tt((BM, 448, 512), (BM, 448, 512), v("U32"), A.add)
+        tt(v("JQ"), (BM, 448, 512), v("J32"), A.add)
+        ts(v("JT"), v("JQ"), 5, A.arith_shift_right, 4095, A.bitwise_and)
+        ts(v("NEW", 64, 128), v("JT"), -2048.0, A.add)
+        tt(v("PB"), v("MM"), v("FC"), A.mult)
+        tt(v("PA", 64, 128), v("NEW", 64, 128), v("MM", 64, 128), A.mult)
+        tt(v("PA", 0, 64), v("NEW", 0, 64), v("MM", 0, 64), A.mult)
+        F2 = (BK[h], 0, 128)
+        mm([(F2, Ih, v("FC"), True, False), (F2, NIh, v("PB"), False, False), (F2, Ih, v("PA"), False, True)])
+        if t < V - 1:
+            _add(gr, "V", vc(64), lambda: vec.tensor_reduce(out=ap(v("CNT")), in_=ap(v("OH")), axis=AxisListType.X, op=A.add), [v("OH")], [v("CNT")])
+
+    def send(name, h, t):
+        src = full("S%s%d%d" % (name, t, h))
+        dst = full("Z%d%d" % (t + 1, h)) if name == "Z" else ("TB%d%d" % (t + 1, h), 384, 512)
+        rid, pid, _ = topo.addr(nxt)
+        en = topo.engines(core, nxt)
+        en = en[:len(en) // 2] if name == "N" else en[len(en) // 2:]
+        msk = sum(1 << e for e in en)
+        rs = "a%s%d%d" % (name.lower(), t + 1, h)
+        NE.append(len(en))
+        x = ("link", 8 * len(NE), 8 * len(NE) + 1)
+        _add(gr, "G", 0.5, lambda: g.remote_dma(ap(dst), ap(src), T.sem[rs], T.sem.loc, pid, rid, msk), [src], [x], sem="loc")
+        _add(gr, "A", 2.5, None, [x], [dst], sem=(rs, len(en)))
+
+    NE = []
+
+    def mine(h, t):
+        v = view(h, t); B = BK[h]; s = t + 1
+        F2, ET, EB, ELp, ELn, DW = (B, 0, 128), (B, 128, 256), (B, 256, 384), (B, 384, 392), (B, 392, 400), (B, 400, 408)
+        Z = full("Z%d%d" % (t, h))
+        tt(v("FS"), F2, v("MS"), A.mult)
+        mm([(ET, v("FS"), BDh, True, True)])
+        tt(v("EMP"), ET, RM(0), A.mult)
+        mm([(ELp, v("EMP"), CC(0), True, True)])
+        if t < V - 1:
+            for p in range(2):
+                tc(("SN%d%d" % (t, h), 64 * p, 64 * p + 64), (B, p, 128, 2))
+            send("N", h, t)
+        else:
+            for q in range(4):
+                act(("YF", h * H + 32 * q, h * H + 32 * q + 32), (B, q, 128, 4), F.Identity, B2048)
+        ts(v("YO"), ELp, 2048.0, A.add)
+        yo = "YO%d" % h; yb = "YB%d" % h
+        _add(gr, "S", 0.065 + 128 * 1.5 * CY, lambda: sca.activation(out=sl(yb), in_=sl("X", 0, W).indirect(sl(yo)), func=F.Identity),
+             [("X", 0, W), full(yo)], [full(yb)])
+        tt(v("EMN"), ET, RM(s), A.mult); tc(v("ETF"), ET); ts(v("EPF"), ELp, 2048.0, A.add)
+        mm([(ELn, v("EMN"), CC(s), True, True), (EB, v("ETF"), PM(s), True, True)])
+        tc(v("ECL"), ELn); tc(v("EC"), EB)
+        mm([((B, 0, 128), Ib, v("YB"), True, False), ((B, 0, 128), Ib, Z, False, True),
+            ((B, 128, 256), Ib, v("YB"), True, False), ((B, 128, 256), NIh, v("ZQ"), False, True)])
+        ts(v("ZH"), (B, 0, 128), 0.5, A.mult, 1031.75, A.add)
+        if t < V - 1:
+            for p in range(2):
+                ts(("SZ%d%d" % (t, h), 64 * p, 64 * p + 64), v("ZH", p, 128, 2), -1032.0, A.add)
+            send("Z", h, t)
+        else:
+            for q in range(4):
+                ts(("YZ", h * H + 32 * q, h * H + 32 * q + 32), v("ZH", q, 128, 4), -1032.0, A.add)
+        act(v("NX"), (B, 128, 256), F.Relu, B1032)
+        ed = "ED%d" % h; ec = "EC%d" % h
+        for c in range(8):
+            _add(gr, "V", vc(64), lambda c=c: vec.tensor_scalar(out=T[ed][:, c, 0:H - 16 * c], in0=sl(ec, 16 * c, H),
+                 scalar1=ap(v("ECL", c, c + 1)), scalar2=None, op0=A.is_equal), [full(ec), v("ECL", c, c + 1)], [(ed, c, c + 1)])
+        if h == 1:
+            for c in range(8):
+                _add(gr, "V", vc(64), lambda c=c: vec.tensor_scalar(out=T.EX[:, c, :], in0=sl(ec),
+                     scalar1=ap(("ECL0", c, c + 1)), scalar2=None, op0=A.is_equal), [full(ec), ("ECL0", c, c + 1)], [("EX", c, c + 1)])
+        _add(gr, "V", vc(256), lambda: vec.tensor_tensor(out=T[ed][:, :, 0:16], in0=T[ed][:, :, 0:16], in1=T.TRI[:], op=A.mult),
+             [(ed, 0, 8), ("TRI", 0, 8)], [(ed, 0, 8)])
+
+        def dup():
+            for c in range(8):
+                x = ten.matmul(T[B][:, 256 + 16 * c:384], ap(BDb), T[ed][:, c, 0:H - 16 * c], c == 0, c == 7 and h == 0)
+            if h == 1:
+                for c in range(8):
+                    x = ten.matmul(T[B][:, 256:384], ap(BDb), T.EX[:, c, :], False, c == 7)
+            return x
+        _add(gr, "P", FIX["P"] + (700 + 1024 * h) * CY, dup, [reg(BDb), (ed, 0, 8)] + ([("EX", 0, 8)] if h else []), [EB])
+        ts(v("FLG"), EB, 0.0, A.is_gt)
+        mm([((B, 0, 128), v("FLG"), BD0, True, True)])
+        tt(v("DTM"), (B, 0, 128), RM(7 - s), A.mult)
+        mm([(DW, v("DTM"), CC(7 - s), True, True)])
+        tt(v("T1"), DW, ("TRC", 8 * h, 8 * h + 8), A.mult)
+        tt(v("T2"), v("T1"), v("EPF"), A.max)
+        tc(v("SO"), v("T2"))
+
+    def carve(h, t):
+        so = "SO%d" % h; nx = "NX%d" % h
+        _add(gr, "V", 0.05 + 128 * 3.5 * CY, lambda: vec.tensor_copy(out=sl("X").indirect(sl(so)), in_=sl(nx)),
+             [full(so), full(nx)], [("X", 0, W + C)])
+
+    def limits():
+        B = BK[1]
+        mm([((B, 408, 409), full("ONE"), full("CNT0"), True, False), ((B, 408, 409), full("ONE"), full("CNT1"), False, True)])
+        tc(("EI", 0, 1), (B, 408, 409)); ts(("EI", 1, 2), ("EI", 0, 1), 3, A.bitwise_and)
+        tt(TOP, ("EI", 1, 2), LF, A.add)
+
+    B2048, B65536, B1032 = col(), col(), col()
+    for c, x in ((B2048, 2048.0), (B65536, 65536.0), (B1032, 1032.0)):
+        ts(c, KF, 0.0, A.mult, x, A.add)
+
+    numbers(0, 0); numbers(1, 0)
+    for t in range(V):
+        scores(0, t); choose(0, t)
+        scores(1, t)
+        meet(0, t); mine(0, t)
+        choose(1, t); meet(1, t); mine(1, t)
+        if t < V - 1:
+            limits()
+        carve(0, t); carve(1, t)
+        if t < V - 1:
+            numbers(0, t + 1); numbers(1, t + 1)
+    store("Y", T.yf[:], full("YF")); store("S", T.yz[:], full("YZ"))
+    for k in range(4):
+        store("YS"[k & 1], T.yx[:, k * 1024:(k + 1) * 1024], ("X", k * 1024, (k + 1) * 1024))
+
+    ops = gr["ops"]
+    seq = _order(ops)
+    eng = {"V": vec, "S": sca, "P": ten, "G": g, "Y": syn}
+    cs = {"V": "cV", "S": "cS", "P": "cP", "G": "cG"}
+    count = {q: 0 for q in eng}
+    seen = {q: {} for q in eng}
+    for c in seq:
+        o = ops[c]; q = o["q"]
+        if q == "A":
+            o["key"] = o["sem"]
+            d = ops[o["deps"][0]] if o["deps"] else None
+            o["vc"] = {}
+            continue
+        S = seen[q]
+        want = {}
+        for d in o["deps"]:
+            k = ops[d].get("key")
+            if k is None:
+                continue
+            if S.get(k[0], 0) < k[1]:
+                want.setdefault(k[0], (0, None))
+                if want[k[0]][0] < k[1]:
+                    want[k[0]] = (k[1], d)
+        for nm, (val, d) in sorted(want.items(), key=lambda kv: -ops[kv[1][1]].get("fin", 0)):
+            if S.get(nm, 0) >= val:
+                continue
+            eng[q].wait_ge(T.sem[nm], val)
+            S[nm] = max(S.get(nm, 0), val)
+            for n2, v2 in ops[d]["vc"].items():
+                S[n2] = max(S.get(n2, 0), v2)
+        x = o["fn"]()
+        o["vc"] = dict(S)
+        if o["sem"] is None:
+            count[q] += 1
+            x.then_inc(T.sem[cs[q]], 1)
+            o["key"] = (cs[q], count[q])
+        elif o["sem"] == "loc":
+            pass
+        else:
+            x.then_inc(T.sem[o["sem"]], 16)
+            o["key"] = (o["sem"], 16)
+    for q in "VSPG":
+        if count[q]:
+            g.wait_ge(T.sem[cs[q]], count[q])
+    for k in range(dn[0]):
+        g.wait_ge(T.sem["d%d" % k], 16)
+    if NE:
+        g.wait_ge(T.sem.loc, sum(NE))
+    return ops

@@ -1,10 +1,13 @@
+import math
 import comms_topo
 from concourse.mybir import AluOpType as A, AxisListType, ActivationFunctionType as F
 
-W, C, V, Q = 4096, 256, 5, 9
+W, C, V = 4096, 256, 5
 H = 128
-TRASH = W
-VPART = [64, 64, 64]
+NV = 80
+NS = H - NV
+ZG = 8
+TMW = 264
 
 SCRATCH = {}
 BUF = {}
@@ -27,68 +30,53 @@ def _sb(name, cols, dt):
 
 def _declare():
     b, h, f, i, u = "bfloat16", "float16", "float32", "int32", "uint16"
-    _sb("X", W + C, b)
-    _sb("vein0", C, b); _sb("front0", C, i); _sb("w0", 1, i); _sb("lim0", 1, i)
-    _sb("PI", 1, i); _sb("CI", 128, i); _sb("C15", 128, i); _sb("CG", 128, i)
-    _sb("ci", 32, i)
-    _sb("cf", 64, f)
-    _sb("OHK", 16, f)
-    for n in ("BDb", "Ib", "NIb", "W2", "S256", "LT", "LT0", "KBD", "BD64", "BD0"):
+    _sb("wl0", 16, i); _sb("wlb", 2, b); _sb("WL", 4, f)
+    _sb("PI", 1, i); _sb("CI", 256, i); _sb("C15", 256, i); _sb("CG", 256, i); _sb("CX", 256, i); _sb("CY", 256, f); _sb("CZ", 256, f)
+    _sb("ci", 32, i); _sb("cf", 64, f)
+    for n in ("BDb", "Ib", "S256", "C2048", "ONES", "DUP0", "DUP1", "T2", "CD"):
         _sb(n, 128, b)
-    _sb("IND", 8, b); _sb("IND128", 8, b); _sb("HC", 64, b); _sb("RB", 64, b)
-    _sb("BDh", 128, h); _sb("NIh", 128, h); _sb("WI", 160, h); _sb("WC", 160, i)
-    _sb("BL", 16 * 128, h); _sb("PW", 8 * 128, b)
-    _sb("RM", 7 * 128, h); _sb("CC", 7 * 8, h); _sb("PM", 5 * 128, h)
-    _sb("REP", 16 * H, b); _sb("REPI", 16 * H, i)
-    _sb("SC0", 64, b); _sb("TRI", [8, 16], b); _sb("ONE", 128, f)
-    _sb("TRC", 16, f); _sb("TRI0", 16, i)
+    for n in ("BDh", "Ih", "NIh", "NI16", "I32", "I16", "ND0", "ND1", "RM"):
+        _sb(n, 128, h)
+    _sb("IND", 8, b); _sb("IND128", 8, b); _sb("CCh", 8, h); _sb("CCB", 8, b)
+    _sb("SH", 15 * 128, h); _sb("EE", 512, h); _sb("LA", 512, b); _sb("CM", 48, b); _sb("CADD", 12, b); _sb("RL", 4, u); _sb("RLI", 48, i)
+    _sb("TM", 2 * TMW, b); _sb("THR", V * 128, b); _sb("RO0", 45, i); _sb("RO1", 45, i); _sb("RO2", 45, i); _sb("RF", 45, f); _sb("WT", 45, f); _sb("TH", 8, f)
+    _sb("TRC", 16, f); _sb("EI", 4, i); _sb("CN", 8, f); _sb("TOP", 2, f)
     for k in range(2):
         s = str(k)
+        _sb("X" + s, W + H, b); _sb("vein" + s, H, b); _sb("front" + s, H, i); _sb("W2" + s, 128, b)
         for t in range(V):
-            _sb("Z%d%d" % (t, k), H, b); _sb("TB%d%d" % (t, k), 4 * H, h)
+            _sb("Z%d%d" % (t, k), H, b); _sb("N%d%d" % (t, k), H, h)
         for t in range(V - 1):
             _sb("SN%d%d" % (t, k), H, h); _sb("SZ%d%d" % (t, k), H, b)
         _sb("VI" + s, 2 * H, i); _sb("VS" + s, 2 * H, i); _sb("MS" + s, H, b); _sb("NK" + s, 3 * H, f)
-        _sb("QI" + s, 3 * H, i); _sb("QS" + s, 3 * H, i); _sb("OF" + s, 3 * H, u); _sb("ZR" + s, 16 * H, b); _sb("ZT" + s, H, b); _sb("NZT" + s, H, b)
-        _sb("U32" + s, 64, f); _sb("ZQ" + s, H, h)
+        _sb("QI" + s, 3 * H, i); _sb("QS" + s, 3 * H, i); _sb("TB" + s, [H, 3], h); _sb("OV" + s, 3 * NV, u); _sb("OS" + s, [NS, 4], u)
+        _sb("ZR" + s, 16 * NV, b); _sb("U16" + s, 64, h); _sb("ZQ" + s, H, h)
+        _sb("D" + s, 48 * NV, b); _sb("A" + s, [H, 48], b); _sb("L" + s, [H, 48], b)
         _sb("K0" + s, H, f); _sb("K1" + s, H, f); _sb("KI" + s, H, i); _sb("YI" + s, H, i); _sb("OK" + s, H, i)
-        _sb("MK" + s, 4 * H, b); _sb("PR" + s, 4 * H, h)
-        _sb("GS" + s, 64, h); _sb("JR" + s, 256, h); _sb("NF" + s, H, f); _sb("FC" + s, H, h); _sb("EQ" + s, 1024, b)
-        _sb("M12" + s, H, b); _sb("OH" + s, 64, b); _sb("MM" + s, H, b); _sb("P12" + s, H, b); _sb("TP" + s, 64, b)
-        _sb("MS1" + s, 64, b); _sb("MS2" + s, 64, b)
-        _sb("DM" + s, 64, f); _sb("DS" + s, 64, f); _sb("DO" + s, 4, u); _sb("TAB" + s, 2048, f)
-        _sb("J32" + s, 64, f); _sb("JQ" + s, 64, i); _sb("JT" + s, 64, i); _sb("NEW" + s, H, f)
-        _sb("PA" + s, H, h); _sb("PB" + s, H, h); _sb("CNT" + s, 1, f)
-        _sb("FS" + s, H, h); _sb("ETF" + s, H, h); _sb("EMP" + s, H, h); _sb("EMN" + s, H, h); _sb("EC" + s, H, h)
-        _sb("EPF" + s, 8, f); _sb("YO" + s, 8, u); _sb("ECL" + s, 8, f); _sb("YB" + s, H, b); _sb("ZH" + s, H, h)
-        _sb("ED" + s, [8, H], b); _sb("FLG" + s, H, b); _sb("DTM" + s, H, h); _sb("T1" + s, 8, f); _sb("T2" + s, 8, f)
-        _sb("SO" + s, 8, u); _sb("NX" + s, H, b)
-    _sb("EX", [8, H], b)
-    _sb("EI", 2, i); _sb("TOP", 1, f); _sb("YF", C, f); _sb("YZ", C, b)
-    for k in range(3):
-        _sb("D%d" % k, 16 * H, b); _sb("G%d" % k, 16 * H, b); _sb("L%d" % k, 16 * H, b)
+        _sb("MK" + s, 3 * H, b); _sb("PR" + s, 4 * H, h)
+        _sb("FC" + s, H, h); _sb("NF" + s, H, f); _sb("G" + s, 256, h); _sb("R" + s, 4, f); _sb("RI" + s, 4, i); _sb("W8" + s, 8, i)
+        _sb("RR" + s, 48, b); _sb("LO" + s, 12, u); _sb("MT" + s, 4, b); _sb("TAB" + s, 1024, f); _sb("MM" + s, H, b)
+        _sb("JA" + s, 64, f); _sb("JQ" + s, 64, i); _sb("JT" + s, 64, i); _sb("PA" + s, H, h); _sb("PB" + s, H, h)
+        _sb("FS" + s, H, h); _sb("EM" + s, H, h); _sb("EC" + s, H, h); _sb("EL" + s, 8, f); _sb("YO" + s, 8, u); _sb("YB" + s, H, b)
+        _sb("ZH" + s, H, h); _sb("NX" + s, 2 * H, b); _sb("ED" + s, 8 * H, b); _sb("DT" + s, H, b); _sb("T1" + s, 16, f); _sb("SO" + s, 16, u)
+        _sb("YF" + s, H, f); _sb("YZ" + s, H, b)
     for k in range(8):
         SCRATCH["B%d" % k] = BUF["B%d" % k] = ("psum", [128, 512], "float32")
     for t in range(1, V):
         for k in range(2):
             SEMAPHORES.append("an%d%d" % (t, k)); SEMAPHORES.append("az%d%d" % (t, k))
-    for k in range(20):
+    for k in range(40):
         SEMAPHORES.append("d%d" % k)
 
 
 _declare()
 
 CY = 0.00083
-FIX = {"V": 0.06, "S": 0.10, "P": 0.03, "G": 0.15, "Y": 0.1, "A": 0.1}
-LAT = 0.08
-
-
-class _Nothing:
-    pass
-
-
-def _graph():
-    return {"ops": [], "acc": {}, "bank": {}}
+GATHER, SCATTER = 1.56, 3.8
+HOLD = {"G": 0.5, "Y": 0.1, "S": 0.1, "A": 0.1}
+LAT = 0.1
+SLACK = 0.04
+LEAD = 0.0
 
 
 def _add(gr, q, cost, fn, R, Wr, sem=None):
@@ -117,7 +105,7 @@ def _add(gr, q, cost, fn, R, Wr, sem=None):
                 keep.append((n, a, b, w))
                 gr["acc"][name] = keep
     deps.discard(n)
-    ops.append({"q": q, "cost": cost, "fn": fn, "deps": sorted(deps), "sem": sem})
+    ops.append({"q": q, "cost": cost, "fn": fn, "deps": sorted(deps), "sem": sem, "lead": gr["lead"], "bulk": gr["bulk"]})
     return n
 
 
@@ -129,7 +117,10 @@ def _order(ops):
             succ[d].append(i)
     pr = [0.0] * n
     for i in range(n - 1, -1, -1):
-        pr[i] = ops[i]["cost"] + max([pr[s] + LAT for s in succ[i]] or [0.0])
+        pr[i] = ops[i]["cost"] + max([pr[s] + LAT for s in succ[i]] + [ops[i]["lead"]]) + 1e3 * ops[i].get("first", 0)
+    for i in range(n):
+        if ops[i]["bulk"]:
+            pr[i] = -float(i)
     free = {}; fin = [0.0] * n; est = [0.0] * n; out = []
     ready = {}
     for i in range(n):
@@ -142,19 +133,17 @@ def _order(ops):
                 continue
             f = free.get(q, 0.0)
             t0 = min(max(f, est[i]) for i in lst)
-            c = max((i for i in lst if max(f, est[i]) <= t0 + 0.04), key=lambda i: pr[i])
+            c = max((i for i in lst if max(f, est[i]) <= t0 + SLACK), key=lambda i: pr[i])
             st = max(f, est[c])
             if best is None or st < best[0]:
                 best = (st, c, q)
         st, c, q = best
         ready[q].remove(c)
         dur = ops[c]["cost"]
-        hold = dur
-        if ops[c]["sem"] is not None:
-            hold = FIX.get(q, 0.1)
+        hold = HOLD[q] if ops[c]["sem"] is not None else dur
         free[q] = st + hold if q != "A" else 0.0
         fin[c] = st + dur
-        ops[c]["start"] = st; ops[c]["fin"] = fin[c]
+        ops[c]["fin"] = fin[c]
         out.append(c)
         for s in succ[c]:
             need[s] -= 1
@@ -169,442 +158,418 @@ def rank_program(g, core, T, topo):
     if rank is None:
         return
     nxt = T.cores[(rank + 1) % len(T.cores)]
-    gr = _graph()
+    gr = {"ops": [], "acc": {}, "bank": {}, "lead": 0.0, "bulk": False}
     vec, sca, ten, syn = g.vector, g.scalar, g.tensor, g.sync
 
-    def sl(n, a=0, b=None, st=None):
+    def r(n, a=0, b=None, st=1, p0=0, p1=128, last=None):
+        return (n, a, BUF[n][1][1] if b is None else b, st, p0, p1, last)
+
+    def part(x, p0, p1):
+        return x[:4] + (p0, p1, x[6])
+
+    def ap(x):
+        n, a, b, st, p0, p1, last = x
+        if len(BUF[n][1]) == 3:
+            if last is None:
+                last = slice(0, BUF[n][1][2])
+            return T[n][p0:p1, a, last] if st == 0 else T[n][p0:p1, a:b, last]
         p, o = PLACE.get(n, (n, 0))
-        b = BUF[n][1][1] if b is None else b
-        return T[p][:, o + a:o + b:st] if st else T[p][:, o + a:o + b]
+        return T[p][p0:p1, o + a:o + b:st] if st > 1 else T[p][p0:p1, o + a:o + b]
 
-    def ap(r):
-        return sl(*r)
+    def reg(x):
+        n, a, b = x[:3]
+        if len(BUF[n][1]) == 3 and n[0] in "AL" and x[6] is not None:
+            m = (x[6].start if isinstance(x[6], slice) else x[6]) // 16
+            return [(n + "_%d" % m, a, b)]
+        if len(BUF[n][1]) == 3 and n[0] in "AL":
+            return [(n + "_%d" % m, a, b) for m in range(3)]
+        if n[:-1] in ("X", "vein", "front", "G", "YF", "YZ"):
+            return [(n + "_%d" % h, a, b) for h in range(2) if x[4] < 64 * h + 64 and 64 * h < x[5]]
+        return [(n, a, b)]
 
-    def full(n):
-        return (n, 0, BUF[n][1][1])
+    def regs(*xs):
+        return sorted(set(y for x in xs if isinstance(x, tuple) for y in reg(x)))
 
-    def reg(r):
-        return (r[0], r[1], r[2])
+    def cnt(x):
+        k = (x[2] - x[1] + max(x[3], 1) - 1) // max(x[3], 1)
+        if len(BUF[x[0]][1]) == 3:
+            k *= BUF[x[0]][1][2] if x[6] is None else (x[6].stop - x[6].start if isinstance(x[6], slice) else 1)
+        return k
 
-    def cnt(r):
-        return (r[2] - r[1] + (r[3] if len(r) > 3 else 1) - 1) // (r[3] if len(r) > 3 else 1)
-
-    def two(*rs):
-        return all(BUF[r[0]][2] in ("bfloat16", "float16", "uint16") for r in rs)
-
-    def vc(cy):
-        return FIX["V"] + max(64, cy) * CY
-
-    def scal(s):
-        return [reg(s)] if isinstance(s, tuple) else []
+    def two(*xs):
+        return all(BUF[x[0]][2] in ("bfloat16", "float16", "uint16") for x in xs)
 
     def sv(s):
         return ap(s) if isinstance(s, tuple) else s
 
+    def src(i, ix):
+        return ap(i).indirect(ap(ix)) if ix else ap(i)
+
+    def vcost(o, i, ix, rate):
+        return 0.05 + cnt(o) * GATHER * CY if ix else max(64, cnt(o) * rate) * CY
+
     def tc(o, i):
-        _add(gr, "V", vc(cnt(i) * (0.5 if two(o, i) else 1)), lambda: vec.tensor_copy(out=ap(o), in_=ap(i)), [reg(i)], [reg(o)])
+        _add(gr, "V", vcost(o, i, None, 0.5 if two(o, i) else 1), lambda: vec.tensor_copy(out=ap(o), in_=ap(i)), regs(i), regs(o))
 
     def ts(o, i, s1, op0, s2=None, op1=None):
         def fn():
             if op1 is None:
                 return vec.tensor_scalar(out=ap(o), in0=ap(i), scalar1=sv(s1), scalar2=None, op0=op0)
             return vec.tensor_scalar(out=ap(o), in0=ap(i), scalar1=sv(s1), scalar2=sv(s2), op0=op0, op1=op1)
-        _add(gr, "V", vc(cnt(i) * (0.5 if two(o, i) else 1)), fn, [reg(i)] + scal(s1) + scal(s2), [reg(o)])
+        _add(gr, "V", vcost(o, i, None, 0.5 if two(o, i) else 1), fn, regs(i, s1, s2), regs(o))
 
-    def tt(o, i, j, op):
+    def tt(o, i, j, op, ix=None):
         ps = "psum" in (BUF[i[0]][0], BUF[j[0]][0])
-        _add(gr, "V", vc(cnt(i) * (1 if ps else 2)), lambda: vec.tensor_tensor(out=ap(o), in0=ap(i), in1=ap(j), op=op),
-             [reg(i), reg(j)], [reg(o)])
+        _add(gr, "V", vcost(o, i, ix, 1 if ps else 2), lambda: vec.tensor_tensor(out=ap(o), in0=src(i, ix), in1=ap(j), op=op),
+             regs(i, j, ix), regs(o))
 
-    def act(o, i, func=F.Identity, bias=None, scale=None):
+    def fill(o, x):
+        _add(gr, "V", vcost(o, o, None, 0.5 if two(o) else 1), lambda: vec.memset(ap(o), x), [], regs(o))
+
+    def act(o, i, func=F.Identity, bias=None, scale=None, ix=None, acc=None, extra=0.0):
         def fn():
             kw = {}
             if bias is not None:
                 kw["bias"] = sv(bias)
             if scale is not None:
                 kw["scale"] = sv(scale)
-            return sca.activation(out=ap(o), in_=ap(i), func=func, **kw)
-        _add(gr, "S", FIX["S"] + cnt(i) * CY, fn, [reg(i)] + scal(bias) + scal(scale), [reg(o)])
+            if acc is not None:
+                kw["accum_out"] = ap(acc)
+            return sca.activation(out=ap(o), in_=src(i, ix), func=func, **kw)
+        c = 0.065 + cnt(o) * GATHER * CY if ix else max(64, cnt(o)) * CY
+        _add(gr, "S", c + extra, fn, regs(i, bias, scale, ix), regs(o, acc))
 
     def mm(lst):
         def fn():
             x = None
-            for o, l, r, s, e in lst:
-                x = ten.matmul(ap(o), ap(l), ap(r), s, e)
+            for o, l, q, s, e in lst:
+                x = ten.matmul(ap(o), ap(l), ap(q), s, e)
             return x
-        c = FIX["P"]; R = []; Wr = []
-        for o, l, r, s, e in lst:
-            c += max(min(64, cnt(l)), cnt(r)) * CY * (4 if BUF[l[0]][2] == "float32" else 1)
-            R += [reg(l), reg(r)]; Wr.append(reg(o))
-        lo = min(x[1] for x in Wr); hi = max(x[2] for x in Wr)
-        _add(gr, "P", c, fn, sorted(set(R)), [(Wr[0][0], lo, hi)])
+        c = sum(max(min(64, cnt(l)), cnt(q)) * CY for o, l, q, s, e in lst)
+        lo = min(x[0][1] for x in lst); hi = max(x[0][2] for x in lst)
+        _add(gr, "P", c, fn, regs(*[x[1] for x in lst], *[x[2] for x in lst]), [(lst[0][0][0], lo, hi)])
+
+    def group(o, *pairs):
+        return [(o, l, q, k == 0, k == len(pairs) - 1) for k, (l, q) in enumerate(pairs)]
+
+    def turned(o, *pairs):
+        out = []
+        for p in range(2):
+            oo = r(o[0], o[1] + 64 * p, o[1] + 64 * p + 64)
+            out += group(oo, *[(l, r(q[0], q[1] + 64 * p, q[1] + 64 * p + 64) if done else r(q[0], q[1] + p, q[2], 2)) for l, q, done in pairs])
+        return out
 
     dn = [0]
 
-    def load(q, o, src):
+    def dma(q, o, i, R, Wr, byts):
         s = "d%d" % dn[0]; dn[0] += 1
         eng = {"Y": syn, "S": sca}[q]
-        byts = cnt(o) * 128 * 2
-        _add(gr, q, 2.0 + byts / 150000.0, lambda: eng.dma_start(ap(o), src), [], [reg(o)], sem=s)
+        _add(gr, q, 2.0 + byts / 150000.0, lambda: eng.dma_start(o(), i()), R, Wr, sem=s)
 
-    def store(q, dst, i):
-        s = "d%d" % dn[0]; dn[0] += 1
-        eng = {"Y": syn, "S": sca}[q]
-        _add(gr, q, 2.0 + cnt(i) * 256 / 150000.0, lambda: eng.dma_start(dst, ap(i)), [reg(i)], [], sem=s)
+    def load(q, o, x, byts, late=False):
+        dma(q, lambda: ap(o), lambda: x, [], regs(o), byts)
+        gr["ops"][-1]["first"] = not late
 
-    load("Y", full("vein0"), T.vein[:]); load("S", full("front0"), T.front[:])
-    load("Y", full("w0"), T.w[:]); load("S", full("lim0"), T.lim[:])
-    for k in range(4):
-        load("YS"[k & 1], ("X", k * 1024, (k + 1) * 1024), T.rock[:, k * 1024:(k + 1) * 1024])
+    def store(q, x, i, byts):
+        dma(q, lambda: x, lambda: ap(i), regs(i), [], byts)
 
-    def iota(name, pattern, base, cm, cols):
-        _add(gr, "G", 0.15 + 2 * cols * CY, lambda: g.iota(sl(name), pattern, base, cm), [], [full(name)])
+    load("S", r("wl0", 0, 1), T.w[:], 512); load("Y", r("wl0", 8, 9), T.lim[:], 512)
+    for s in range(2):
+        rows = slice(64 * s, 64 * s + 64)
+        for h in range(2):
+            load("YS"[h], r("vein%d" % s, p0=64 * h, p1=64 * h + 64), T.vein[rows, H * h:H * h + H], 16384)
+            load("YS"[h], r("front%d" % s, p0=64 * h, p1=64 * h + 64), T.front[rows, H * h:H * h + H], 32768)
+    for s in range(2):
+        for h in range(2):
+            load("Y", r("X%d" % s, 0, W, p0=64 * h, p1=64 * h + 64), T.rock[64 * s:64 * s + 64, :], 524288 * (1 + h + 2 * s), late=True)
 
-    iota("PI", [[1, 1]], 0, 1, 1); iota("CI", [[1, 128]], 0, 0, 128); iota("WC", [[1, 160]], -16, 0, 160)
-    iota("TRI0", [[16, 16]], TRASH, 0, 16)
-    iota("REPI", [[1, 128], [0, 16]], 0, 0, 2048)
-    nc = [0]
+    def iota(x, pattern, base, cm):
+        _add(gr, "G", 0.13 + 2 * cnt(x) * CY, lambda: g.iota(ap(x), pattern, base, cm), [], regs(x))
+
+    PI, CI, C15, CG, CX, CYf, CZ = r("PI"), r("CI"), r("C15"), r("CG"), r("CX"), r("CY"), r("CZ")
+    iota(PI, [[1, 1]], 0, 1); iota(CI, [[1, 256]], 0, 0)
+    nc = [0, 0]
 
     def col():
         nc[0] += 1
-        return ("cf", nc[0] - 1, nc[0])
-    ni = [0]
+        return r("cf", nc[0] - 1, nc[0])
 
     def icol():
-        ni[0] += 1
-        return ("ci", ni[0] - 1, ni[0])
-    PI, CI, C15, CG = full("PI"), full("CI"), full("C15"), full("CG")
+        nc[1] += 1
+        return r("ci", nc[1] - 1, nc[1])
+
+    def cut(x, a, b, st=1):
+        return r(x[0], a, b, st)
     PF = col(); tc(PF, PI)
     k_i, g_i = icol(), icol()
     ts(k_i, PI, 15, A.bitwise_and); ts(g_i, PI, 4, A.arith_shift_right)
     KF, GF = col(), col(); tc(KF, k_i); tc(GF, g_i)
     ts(CG, CI, 4, A.arith_shift_right); ts(C15, CI, 15, A.bitwise_and)
-    BDb, BDh, Ib, NIb, NIh = full("BDb"), full("BDh"), full("Ib"), full("NIb"), full("NIh")
-    ts(BDb, CG, GF, A.is_equal); tc(BDh, BDb)
-    ts(Ib, CI, PF, A.is_equal); ts(NIb, Ib, -1.0, A.mult)
-    ts(full("WI"), full("WC"), PF, A.is_equal); Ih = ("WI", 16, 144)
-    ts(NIh, Ih, -1.0, A.mult)
-    WF, LF = col(), col(); tc(WF, full("w0")); tc(LF, full("lim0"))
-    W2, S256 = full("W2"), full("S256")
-    ts(W2, BDb, WF, A.mult, 2.0, A.mult); ts(S256, BDb, 256.0, A.mult)
+    BDb, BDh, Ib, Ih, NIh, S256 = r("BDb"), r("BDh"), r("Ib"), r("Ih"), r("NIh"), r("S256")
+    ts(BDb, cut(CG, 0, 128), GF, A.is_equal); ts(Ib, cut(CI, 0, 128), PF, A.is_equal)
+    tc(Ih, Ib); ts(S256, BDb, 256.0, A.mult); ts(r("C2048"), Ib, 2048.0, A.mult); fill(r("ONES"), 1.0)
+    tc(r("wlb"), r("wl0", 0, 16, 8))
+    mm([(r("B6", 2 * s, 2 * s + 2, p0=64 * h, p1=64 * h + 64), cut(Ib, 64 * s, 64 * s + 64), r("wlb"), True, True) for s in range(2) for h in range(2)])
+    act(r("WL"), r("B6", 0, 4))
+    for s in range(2):
+        ts(r("W2%d" % s), BDb, r("WL", 2 * s, 2 * s + 1), A.mult, 2.0, A.mult)
+    LF = r("WL", 1, 4, 2); tc(r("TOP"), LF)
     KS = col(); ts(KS, KF, 256.0, A.mult, 1.0, A.add)
     NKC = []
     for m in range(3):
         c = col(); NKC.append(c); sc = float(1 << (5 + m))
-        ts(c, KF, 37.0 * sc, A.mult, (613 * m + 2048) * sc - 8388608.0, A.add)
-    TOP = full("TOP"); tc(TOP, LF)
-    ts(full("REP"), full("REPI"), PF, A.is_equal)
-    IND, IND128 = full("IND"), full("IND128")
-    ts(IND, ("CI", 0, 8), GF, A.is_equal); ts(IND128, IND, 128.0, A.mult)
-    OHK = full("OHK"); ts(OHK, ("CI", 0, 16), KF, A.is_equal)
+        ts(c, KF, 37.0 * sc, A.mult, 613 * m * sc - 8388608.0, A.add)
+    IND, IND128 = r("IND"), r("IND128")
+    ts(IND, cut(CI, 0, 8), GF, A.is_equal); ts(IND128, IND, 128.0, A.mult)
+    B2048, BJA, B1032, BMT, BEX = col(), col(), col(), col(), col()
+    for c, x in ((B2048, 2048.0), (BJA, 98288.0 - 8388608.0), (B1032, 1032.0), (BMT, 4095.5), (BEX, 60 * math.log(3.0))):
+        ts(c, KF, 0.0, A.mult, x, A.add)
 
-    def BL(l):
-        return ("BL", l * 128, l * 128 + 128)
+    def late_constants():
+        tc(BDh, BDb); ts(NIh, Ib, -1.0, A.mult); ts(r("NI16"), Ib, -0.0625, A.mult); ts(r("I32"), Ib, 32.0, A.mult); ts(r("I16"), Ib, 16.0, A.mult)
+        ts(r("RM"), cut(C15, 0, 128), KF, A.is_equal)
+        tc(r("CCh"), IND); ts(r("CCB"), IND, 8192.0, A.mult)
+        for h in range(2):
+            for p in range(2):
+                tc(r("DUP%d" % h, 64 * p, 64 * p + 64), cut(Ib, 64 * h, 64 * h + 64))
+            ts(r("ND%d" % h), r("DUP%d" % h), -1.0, A.mult)
+        ts(cut(CX, 0, 128), cut(C15, 0, 128), -1.0, A.mult, KF, A.add); ts(cut(CX, 128, 256), cut(CX, 0, 128), 15, A.bitwise_and)
+        ts(cut(CZ, 0, 128), cut(CX, 128, 256), 1.0, A.add); tt(r("CD"), cut(CZ, 0, 128), BDb, A.mult)
+        for d in range(1, 16):
+            ts(r("SH", 128 * (d - 1), 128 * d), r("CD"), d + 1.0, A.is_equal)
+        tt(CX, CG, C15, A.subtract); ts(CX, CX, 15, A.bitwise_and)
+        i64, i65 = col(), col()
+        ts(i64, PF, 64.0, A.is_equal, 16.0, A.mult); ts(i65, PF, 65.0, A.is_equal)
+        ts(CYf, CI, i64, A.mult); ts(CZ, CX, i65, A.mult); tt(CYf, CYf, CZ, A.add)
+        for a in range(2):
+            cs, cj = col(), col()
+            ts(cs, PF, -16.0 * a, A.add); ts(cj, PF, -16.0 * a - 32.0, A.add)
+            e = r("EE", 256 * a, 256 * a + 256)
+            ts(CZ, C15, cs, A.is_equal, -8192.0, A.mult); tt(e, CZ, CYf, A.add)
+            ts(CZ, CG, cj, A.is_equal, 8192.0, A.mult); tt(e, CZ, e, A.add)
+        for s in range(2):
+            fill(r("G%d" % s, p0=64), 1.0)
+        hi_, b_, b_f = icol(), icol(), col()
+        ts(hi_, PI, 6, A.arith_shift_right); ts(b_, PI, 4, A.arith_shift_right, 3, A.bitwise_and); tc(b_f, b_)
+        base = col(); ts(base, hi_, 64.0, A.mult, KF, A.add)
+        for a in range(4):
+            c = col(); ts(c, base, 16.0 * a, A.add)
+            ts(r("LA", 128 * a, 128 * a + 128), cut(CI, 0, 128), c, A.is_equal)
+        RLI = r("RLI")
+        ts(RLI, cut(CI, 0, 48), 3, A.bitwise_and); ts(r("CM"), RLI, b_f, A.is_equal)
+        for a in range(4):
+            ts(r("CM", 12 * a + 8, 12 * a + 12), r("CM", 12 * a + 8, 12 * a + 12), 64.0, A.mult)
+        fill(r("CADD", 0, 4), 0.0); fill(r("CADD", 4, 8), float(TMW)); ts(r("CADD", 8, 12), cut(CI, 0, 4), 16.0, A.mult, KF, A.add)
+        j, ja, jx = r("CN", 0, 3), r("RLI", 0, 3), r("RLI", 8, 11)
+        ts(j, cut(CI, 0, 3), 16.0, A.mult, KF, A.add)
+        ts(ja, j, -5.5, A.add, 1.0 / 12.0, A.mult)
+        ts(jx, ja, -12.0, A.mult); tt(jx, jx, j, A.add); ts(jx, jx, 7.5, A.is_gt, 4.0, A.mult); tt(jx, jx, ja, A.add); tc(r("RL", 0, 3), jx)
+        c15 = col(); ts(c15, KF, -1.0, A.mult, 15.0, A.add)
+        fill(r("TM"), 0.0)
+        tt(CX, CG, C15, A.subtract); ts(CYf, CX, c15, A.is_le); ts(CZ, C15, KF, A.is_lt); tt(r("TM", 0, 256), CYf, CZ, A.mult)
+        ts(r("TM", TMW, TMW + 256), CG, KF, A.is_le)
+        for t in range(V):
+            x = float(1 << (t + 2))
+            kx = col(); ts(kx, KF, x, A.mult)
+            ts(r("RO0", 9 * t, 9 * t + 8), cut(CI, 0, 8), 16.0 * x, A.mult, kx, A.add); ts(r("RO0", 9 * t + 8, 9 * t + 9), PI, x, A.mult)
+        ts(r("RO1"), r("RO0"), 127, A.bitwise_and); ts(r("RO2"), r("RO0"), 7, A.arith_shift_right); tt(r("RF"), r("RO1"), r("RO2"), A.add)
+        act(r("WT"), r("RF"), F.Exp, BEX, -math.log(3.0), extra=1.3)
+        ts(r("TH", 0, 5), r("WT", 8, 45, 9), 2.2, A.mult)
+        ts(r("T2"), r("RM"), -1e29, A.mult, 1e29, A.add)
+        for t in range(V):
+            ts(r("THR", 128 * t, 128 * t + 128), r("T2"), r("TH", t, t + 1), A.max)
+        ts(r("RLI", 16, 32), cut(CI, 0, 16), 7, A.bitwise_and); kt = col(); ts(kt, KF, 2048.0, A.add)
+        ts(r("TRC"), r("RLI", 16, 32), 16.0, A.mult, kt, A.add)
 
-    def PW(j):
-        return ("PW", j * 128, j * 128 + 128)
-    for l in range(16):
-        ts(BL(l), BDh, ("OHK", l, l + 1), A.mult)
-    for j in range(8):
-        ts(PW(j), Ib, float(1 << j), A.mult)
-    LT, LT0 = full("LT"), full("LT0")
-    ts(LT0, C15, KF, A.is_gt, 4.0, A.mult); tt(LT0, LT0, BDb, A.mult); tt(LT, LT0, Ib, A.subtract)
-    BD0 = full("BD0"); ts(BD0, BDb, ("OHK", 0, 1), A.mult)
-    KBD, BD64 = full("KBD"), full("BD64")
-    ts(KBD, BDb, KF, A.mult, 64.0, A.mult); ts(BD64, BDb, 64.0, A.mult)
-    HC = full("HC"); ts(HC, ("CI", 0, 64), 0.0625, A.mult)
-    P16, P15c = col(), col()
-    ts(P16, KF, 0.0, A.mult, 65536.0, A.add)
-    for b in range(4):
-        x, y = icol(), col()
-        ts(x, k_i, b, A.arith_shift_right, 1, A.bitwise_and)
-        ts(y, x, 2.0 ** -(1 << b) - 1.0, A.mult, 1.0, A.add)
-        tt(P16, P16, y, A.mult)
-    ts(P15c, P16, 0.5, A.mult)
-    M2C = col(); ts(M2C, KF, -64.0, A.mult, 64.0 * 31 + 63, A.add)
-    RB = full("RB"); ts(RB, ("C15", 0, 64), KF, A.is_equal)
-    SC0 = full("SC0"); ts(SC0, ("C15", 0, 64), 0.0, A.not_equal)
-    for c in range(8):
-        _add(gr, "V", vc(16), lambda c=c: vec.tensor_scalar(out=T.TRI[:, c, :], in0=sl("C15", 0, 16), scalar1=ap(KF), scalar2=None, op0=A.is_gt),
-             [("C15", 0, 16), KF], [("TRI", c, c + 1)])
-    ts(full("TRC"), full("TRI0"), KF, A.add)
-    _add(gr, "V", vc(128), lambda: vec.memset(sl("ONE"), 1.0), [], [full("ONE")])
-    for k in range(2):
-        _add(gr, "V", vc(2048), lambda k=k: vec.memset(sl("TAB%d" % k), 0.0), [], [full("TAB%d" % k)])
-
-    def RM(s):
-        return ("RM", s * 128, s * 128 + 128)
-
-    def CC(s):
-        return ("CC", s * 8, s * 8 + 8)
-
-    def PM(s):
-        return ("PM", (s - 1) * 128, s * 128)
-    rot_i = icol(); rot_h = icol(); lo_i = icol()
-    for s in (0, 1, 6, 2, 5, 3, 4):
-        rf, lf, hf = col(), col(), col()
-        if s == 0:
-            ts(rot_i, PI, 0.0, A.add)
-        else:
-            ts(rot_i, PI, float(1 << s), A.mult); ts(rot_i, rot_i, 127, A.bitwise_and)
-            ts(rot_h, PI, 7 - s, A.arith_shift_right); tt(rot_i, rot_i, rot_h, A.add)
-        tc(rf, rot_i); ts(lo_i, rot_i, 15, A.bitwise_and); tc(lf, lo_i)
-        ts(lo_i, rot_i, 4, A.arith_shift_right); tc(hf, lo_i)
-        ts(RM(s), C15, lf, A.is_equal); ts(CC(s), ("CI", 0, 8), hf, A.is_equal)
-        if 1 <= s <= 5:
-            ts(PM(s), CI, rf, A.is_equal)
-
-    for k in range(2):
+    for s in range(2):
         for p in range(2):
-            ts(("TB0%d" % k, 384 + 64 * p, 448 + 64 * p), ("front0", k * H + p, (k + 1) * H, 2), -2048.0, A.add)
-            act(("Z0%d" % k, 64 * p, 64 * p + 64), ("vein0", k * H + p, (k + 1) * H, 2))
+            ts(r("N0%d" % s, 64 * p, 64 * p + 64), r("front%d" % s, p, H, 2), -2048.0, A.add)
+            act(r("Z0%d" % s, 64 * p, 64 * p + 64), r("vein%d" % s, p, H, 2))
 
-    def view(h, t):
-        s = str(h)
-        return lambda n, a=None, b=None, st=None: ((n + s,) + ((0, BUF[n + s][1][1]) if a is None else ((a, b) if st is None else (a, b, st))))
+    def view(s):
+        gr["lead"] = LEAD * (1 - s)
+        return lambda n, *a, **k: r(n + str(s), *a, **k)
 
-    BU, BM, BS0, BS1 = "B6", "B7", "B4", "B5"
-    BK = ["B2", "B3"]
+    BK, BR, BM, BT = ["B0", "B1"], ["B2", "B3"], ["B4", "B5"], ["B6", "B7"]
 
-    def numbers(h, t):
-        v = view(h, t)
-        Z = full("Z%d%d" % (t, h)); tb = "TB%d%d" % (t, h); NCt = (tb, 384, 512)
-        mm([((BU, 256, 384), Ih, NCt, True, True)])
-        act((BU, 384, 512), (BU, 256, 384), bias=None, scale=None) if False else None
+    def numbers(s, t):
+        v = view(s); M = BM[s]
+        Z, N = r("Z%d%d" % (t, s)), r("N%d%d" % (t, s))
+        n, pq = r(M, 256, 384), r(M, 384, 512)
+        mm(group(n, (Ih, N), (r("C2048"), r("ONES"))))
         for m in range(3):
-            act(v("NK", m * H, m * H + H), (BU, 256, 384), F.Identity, NKC[m], float(1 << (5 + m)))
-        mm([((BU, 0, 128), W2, Z, True, True), ((BU, 128, 256), S256, Z, True, True)])
-        ts(v("VI"), (BU, 0, 256), 1.0, A.add); ts(v("VS"), v("VI"), 4095, A.bitwise_and)
-        ts((BU, 384, 512), (BU, 256, 384), 2048.0, A.add)
-        tt((BU, 0, 128), (BU, 384, 512), v("VS", 0, 128), A.mult)
+            act(v("NK", m * H, m * H + H), n, F.Identity, NKC[m], float(1 << (5 + m)))
+        mm(group(r(M, 0, 128), (v("W2"), Z)) + turned(r(M, 128, 256), (S256, Z, False)))
+        for k in range(16):
+            o = v("ZR", k, 16 * NV, 16); z = cut(Z, 0, NV)
+            if k < ZG:
+                _add(gr, "G", 0.17 + 2 * NV * CY, lambda o=o, z=z: g.affine_select(ap(o), ap(z), [[0, NV]], A.is_ge, 0.0, 0, 0), regs(z), [("ZR%d_%d" % (s, k), 0, 1)])
+            else:
+                _add(gr, "V", max(64, NV / 2) * CY, lambda o=o, z=z: vec.tensor_copy(out=ap(o), in_=ap(z)), regs(z), [("ZR%d_%d" % (s, k), 0, 1)])
+        ts(v("VI"), r(M, 0, 256), 1.0, A.add); ts(v("VS"), v("VI"), 4095, A.bitwise_and)
+        tt(pq, n, v("VS", 0, 128), A.mult)
         for m in range(3):
             o = (m * H, m * H + H)
-            tt(v("QI", *o), (BU, 0, 128), v("NK", *o), A.add)
-            ts(v("QS", *o), v("QI", *o), 5 + m, A.arith_shift_right, 4095, A.bitwise_and)
-            tc(v("OF", *o), v("QS", *o))
-        bk = "B%d" % (dbank[0] & 1); dbank[0] += 1
-        mm([((bk, 0, 128), Z, Ib, True, True)])
-        act(v("ZT"), (bk, 0, 128)); act(v("NZT"), (bk, 0, 128), scale=-1.0)
-        for a in range(0, 16 * max(VPART), 512):
-            bk = "B%d" % (dbank[0] & 1); dbank[0] += 1
-            mm([((bk, 0, 512), v("ZT"), ("REP", a, a + 512), True, True)])
-            act(v("ZR", a, a + 512), (bk, 0, 512))
-        ts((tb, 0, 384), v("OF"), -2048.0, A.add)
+            tt(v("QI", *o), pq, v("NK", *o), A.add)
+        for m in range(3):
+            o = (m * H, m * H + H)
+            _add(gr, "V", H * CY, lambda m=m, o=o: vec.tensor_scalar(out=ap(v("QS", m, 3 * H, 3)), in0=ap(v("QI", *o)), scalar1=5 + m, scalar2=4095,
+                 op0=A.arith_shift_right, op1=A.bitwise_and), regs(v("QI", *o)), [("QS%d" % s, m, m + 1)])
+        _add(gr, "V", 3 * H * CY, lambda: vec.tensor_scalar(out=ap(v("TB")), in0=ap(v("QS")), scalar1=-2048.0, scalar2=None, op0=A.add),
+             [("QS%d" % s, 0, 3)], regs(v("TB")))
+        ts(v("OS", last=slice(0, 3)), v("TB", NV, H), 2048.0, A.add)
+        for m in range(3):
+            ts(v("OV", m * NV, m * NV + NV), v("TB", 0, NV, last=m), 2048.0, A.add)
+        mm([x for m in range(3) for x in group(r(BR[s], m * H, m * H + H), (v("TB", last=m), Ih))] + group(r(BR[s], 384, 512), (N, Ih)))
         ts(v("MS"), v("VS", 128, 256), KS, A.is_equal)
-        ts(v("U32"), v("VS", 64, 128), 16.0, A.mult, -16.0 - 8388608.0, A.add)
+        ts(v("U16"), v("VS", 64, 128), -2048.0, A.add)
         ts(v("ZQ"), Z, 0.25, A.mult, 1031.625, A.add)
 
-    unit = [0]
-    dbank = [0]
-
-    def scores(h, t):
-        v = view(h, t); zr = "ZR%d" % h
+    def scores(s, t):
+        v = view(s); X = v("X", 0, W); Z = r("Z%d%d" % (t, s)); zr = [("ZR%d_%d" % (s, k), 0, 1) for k in range(16)]
+        for c in range(NS):
+            act(v("A", NV + c, NV + c + 1, 0), X, F.Abs, cut(Z, NV + c, NV + c + 1), -1.0, ix=v("OS", c, c + 1, 0, last=slice(0, 3)))
         for m in range(3):
-            u = unit[0] % 3; unit[0] += 1
-            D, G, L = "D%d" % u, "G%d" % u, "L%d" % u
-            nv = VPART[m]
-            of = "OF%d" % h
-            XW = ("X", 0, W)
-
-            def vg(a, b, m=m, D=D):
-                _add(gr, "V", 0.05 + 1.5 * CY * 16 * (b - a), lambda: vec.tensor_tensor(
-                    out=sl(D, 16 * a, 16 * b), in0=sl("X", 0, W).indirect(sl(of, m * H + a, m * H + b)), in1=sl(zr, 16 * a, 16 * b), op=A.subtract),
-                    [XW, (of, m * H + a, m * H + b), (zr, 16 * a, 16 * b)], [(D, 16 * a, 16 * b)])
-
-            def sg(a, b, m=m, G=G):
-                _add(gr, "S", 0.065 + 1.5 * CY * 16 * (b - a), lambda: sca.activation(
-                    out=sl(G, 16 * a, 16 * b), in_=sl("X", 0, W).indirect(sl(of, m * H + a, m * H + b)), func=F.Identity),
-                    [XW, (of, m * H + a, m * H + b)], [(G, 16 * a, 16 * b)])
-            for a in range(0, nv, 32):
-                vg(a, a + 32)
-            for a in range(nv, H, 32):
-                sg(a, a + 32)
-            for a in range(nv, H, 32):
-                bk = "B%d" % (dbank[0] & 1); dbank[0] += 1
-
-                r = (16 * a, 16 * a + 512)
-                mm([((bk, 0, 512), v("NZT"), ("REP",) + r, True, False), ((bk, 0, 512), Ib, (G,) + r, False, True)])
-                act((D, 16 * a, 16 * a + 512), (bk, 0, 512), F.Abs)
-            for a in range(0, nv, 32):
-                act((D, 16 * a, 16 * a + 512), (D, 16 * a, 16 * a + 512), F.Abs)
+            ms = slice(16 * m, 16 * m + 16)
+            for a in range(0, NV, 32):
+                b = min(NV, a + 32); d = v("D", 16 * (m * NV + a), 16 * (m * NV + b)); ix = v("OV", m * NV + a, m * NV + b)
+                _add(gr, "V", vcost(d, X, ix, 1), lambda a=a, b=b, d=d, ix=ix: vec.tensor_tensor(
+                    out=ap(d), in0=src(X, ix), in1=ap(v("ZR", 16 * a, 16 * b)), op=A.subtract), regs(X, ix) + zr, regs(d))
+                act(v("A", a, b, last=ms), d, F.Abs)
             for a in range(0, H, 64):
-                r = (16 * a, 16 * a + 1024)
-                ts((L,) + r, (D,) + r, TOP, A.is_le, 2.0 * m + 0.4375, A.add)
-            for k0 in range(0, 16, 8):
-                mm([x for k in range(k0, k0 + 8) for x in (
-                    ((BK[h], m * H + k, m * H + 128, 16), (D, k, 2048, 16), IND128, True, False),
-                    ((BK[h], m * H + k, m * H + 128, 16), (L, k, 2048, 16), IND, False, True))])
+                ts(v("L", a, a + 64, last=ms), v("A", a, a + 64, last=ms), r("TOP", s, s + 1), A.is_le, 2.0 * m + 0.4375, A.add)
+            for k0 in range(0, 16, 4):
+                mm([x for k in range(k0, k0 + 4) for x in group(r(BK[s], m * H + k, m * H + H, 16),
+                    (v("A", last=16 * m + k), IND128), (v("L", last=16 * m + k), IND))])
 
-    def choose(h, t):
-        v = view(h, t); B = BK[h]; tb = "TB%d%d" % (t, h)
-        act(v("K0"), (B, 0, 128))
-        tt(v("K1"), v("K0"), (B, 128, 256), A.min)
-        tt(v("KI"), v("K1"), (B, 256, 384), A.min)
-        ts(v("YI"), v("KI"), 4, A.arith_shift_right, 7, A.bitwise_and)
+    def choose(s, t):
+        v = view(s); B = BK[s]; N = r("N%d%d" % (t, s))
+        act(v("K0"), r(B, 0, 128))
+        tt(v("K1"), v("K0"), r(B, 128, 256), A.min)
+        tt(v("KI"), v("K1"), r(B, 256, 384), A.min)
+        ts(v("YI"), v("KI"), 112, A.bitwise_and)
         ts(v("OK"), v("KI"), 16, A.bitwise_and)
         for m in range(3):
-            ts(v("MK", m * H, m * H + H), v("YI"), 2.0 * m + 1.0, A.is_equal)
-        ts(v("MK", 384, 512), v("OK"), 0.0, A.is_equal)
-        mm([((BS0, s * H, s * H + H), v("MK", s * H, s * H + H), Ib, True, True) for s in range(4)])
-        tt(v("PR"), (BS0, 0, 512), full(tb), A.mult)
-        mm([((BM, 0, 128), Ih, v("PR", s * H, s * H + H), s == 0, s == 3) for s in range(4)])
+            ts(v("MK", m * H, m * H + H), v("YI"), 32.0 * m + 16.0, A.is_equal)
+        tt(v("PR", 384, 512), r(BR[s], 384, 512), v("OK"), A.mult)
+        tt(v("PR", 0, 384), r(BR[s], 0, 384), v("MK"), A.mult)
+        mm(group(r(BM[s], 0, 128), (Ih, N), (v("PR", 384, 512), r("NI16")), *[(v("PR", m * H, m * H + H), Ih) for m in range(3)]))
 
-    def meet(h, t):
-        v = view(h, t)
-        NPs, NPj, NPa = (BM, 0, 64), (BM, 64, 128), (BM, 0, 128)
-        ts(v("GS"), NPs, 0.125, A.mult, 1287.5625, A.add)
-        ts(v("JR", 0, 64), NPj, 0.125, A.mult, 1287.5625, A.add)
-        tc(v("FC"), NPa)
-        act(v("NF"), NPa, F.Identity, B2048)
-        act(v("J32"), NPj, F.Identity, B65536, 32.0)
-        tc(v("JR", 64, 128), v("JR", 0, 64)); tc(v("JR", 128, 256), v("JR", 0, 128))
+    def meet(s, t):
+        v = view(s); NP = r(BM[s], 0, 128); R = BR[s]; K = BK[s]
+        tc(v("FC"), NP)
+        act(v("NF"), NP, F.Identity, B2048)
+        mm([(r(R, 128 * x + 64 * h, 128 * x + 64 * h + 64, p0=32 * j, p1=32 * j + 32), cut(Ih, 64 * h + 32 * x, 64 * h + 32 * x + 32),
+             v("FC", 64 * j, 64 * j + 64), True, True) for x in range(2) for h in range(2) for j in range(2)])
+        ts(v("G", p1=64), r(R, 0, 256, p1=64), 0.125, A.mult, 1287.5625, A.add)
         for x in range(2):
-            bk = (BS0, BS1)[x]
-            mm([((bk, 64 * l, 64 * l + 64), BL(8 * x + l), v("GS"), True, True) for l in range(8)])
-            for y in range(2):
-                tt(v("EQ", 512 * x + 256 * y, 512 * x + 256 * y + 256), (bk, 256 * y, 256 * y + 256), v("JR"), A.is_equal)
-        for x in range(4):
-            lo, hi = max(2, 8 * x), min(31, 8 * x + 8)
-            bk = (BS0, BS1)[x & 1]
-            mm([((bk, 64 * (d - 8 * x), 64 * (d - 8 * x) + 64), ("WI", d, d + 128), v("FC", 64, 128), True, True) for d in range(lo, hi)])
-            act(v("TAB", 64 * lo, 64 * hi), (bk, 64 * (lo - 8 * x), 64 * (hi - 8 * x)))
-        for x in range(2):
-            mm([((BM, 128 + 64 * x, 192 + 64 * x), PW(7 - l), v("EQ", 512 * x + 64 * l, 512 * x + 64 * l + 64), l == 0, l == 7) for l in range(8)])
-        ts(v("M12"), (BM, 128, 256), 0.0, A.is_gt)
-        mm([((BM, 256, 320), LT, v("M12", 0, 64), True, False), ((BM, 256, 320), LT, v("M12", 64, 128), False, True)])
-        ts(v("OH"), (BM, 256, 320), 0.0, A.is_lt)
-        tt(v("P12", 0, 64), (BM, 128, 192), v("OH"), A.mult)
-        tt(v("P12", 64, 128), (BM, 192, 256), v("OH"), A.mult)
-        mm([((BM, 320, 384), S256, v("P12", 0, 64), True, False), ((BM, 320, 384), BDb, v("P12", 64, 128), False, True)])
-        ts(v("TP"), (BM, 320, 384), P15c, A.is_ge)
-        mm([((BM, 384, 448), KBD, v("OH"), True, False), ((BM, 384, 448), BDb, HC, False, False), ((BM, 384, 448), BD64, v("TP"), False, True)])
-        tt(v("DM"), (BM, 384, 448), RB, A.mult)
-        _add(gr, "V", vc(64), lambda: vec.tensor_tensor_scan(ap(v("DS")), ap(SC0), ap(v("DM")), 0.0, A.mult, A.add), [SC0, v("DM")], [v("DS")])
-        tc(v("DO"), v("DS", 15, 64, 16))
-        do = "DO%d" % h; tab = "TAB%d" % h; new = "NEW%d" % h
-        _add(gr, "S", 0.065 + 64 * 1.5 * CY, lambda: sca.activation(out=sl(new, 0, 64), in_=sl(tab).indirect(sl(do)), func=F.Identity),
-             [full(tab), full(do)], [(new, 0, 64)])
-        ts(v("MS1"), (BM, 320, 384), P16, A.is_ge)
-        ts(v("MS2"), (BM, 384, 448), M2C, A.is_le)
-        tt(v("MM", 0, 64), v("MS1"), v("MS2"), A.mult)
-        ts(v("MM", 64, 128), (BM, 256, 320), 0.0, A.not_equal)
-        tt((BM, 448, 512), v("NF", 64, 128), v("NF", 0, 64), A.mult)
-        tt((BM, 448, 512), (BM, 448, 512), v("U32"), A.add)
-        tt(v("JQ"), (BM, 448, 512), v("J32"), A.add)
-        ts(v("JT"), v("JQ"), 5, A.arith_shift_right, 4095, A.bitwise_and)
-        ts(v("NEW", 64, 128), v("JT"), -2048.0, A.add)
-        tt(v("PB"), v("MM"), v("FC"), A.mult)
-        tt(v("PA", 64, 128), v("NEW", 64, 128), v("MM", 64, 128), A.mult)
-        tt(v("PA", 0, 64), v("NEW", 0, 64), v("MM", 0, 64), A.mult)
-        F2 = (BK[h], 0, 128)
-        mm([(F2, Ih, v("FC"), True, False), (F2, NIh, v("PB"), False, False), (F2, Ih, v("PA"), False, True)])
+            mm([(r(BT[x], 256 * a, 256 * a + 256), v("G", 128 * x, 128 * x + 128, p1=66), r("EE", 256 * a, 256 * a + 256, p1=66), True, True) for a in range(2)])
+            for a in range(2):
+                o, i = v("R", 2 * x + a, 2 * x + a + 1), r(BT[x], 256 * a, 256 * a + 256)
+                _add(gr, "V", 256 * CY, lambda o=o, i=i: vec.tensor_reduce(out=ap(o), in_=ap(i), axis=AxisListType.X, op=A.min, apply_absolute_value=True), regs(i), regs(o))
+        ts(v("RI"), v("R"), 4096.0, A.min)
+        ts(v("W8", 0, 4), v("RI"), 4, A.arith_shift_right); ts(v("W8", 4, 8), v("RI"), 15, A.bitwise_and)
+        tt(v("RR"), v("W8"), r("CM"), A.mult, ix=r("RL", 0, 3))
+        mm(group(r(R, 256, 268), (Ib, r("CADD")), *[(r("LA", 128 * a, 128 * a + 128), v("RR", 12 * a, 12 * a + 12)) for a in range(4)]))
+        tc(v("LO"), r(R, 256, 268))
         if t < V - 1:
-            _add(gr, "V", vc(64), lambda: vec.tensor_reduce(out=ap(v("CNT")), in_=ap(v("OH")), axis=AxisListType.X, op=A.add), [v("OH")], [v("CNT")])
+            act(v("MT"), v("R"), F.Sign, BMT, -1.0)
+        J = v("FC", 64, 128)
+        for x in range(2):
+            mm([(r(BT[x], 64 * d, 64 * d + 64), r("SH", 128 * (8 * x + d - 1), 128 * (8 * x + d)) if x + d else Ih, J, True, True) for d in range(8)])
+            act(v("TAB", 512 * x, 512 * x + 512), r(BT[x]))
+        act(v("MM"), r("TM"), ix=v("LO", 0, 8))
+        mm(group(r(K, 0, 64), (r("I32"), J), (r("I16"), v("U16"))))
+        act(v("JA"), r(K, 0, 64), F.Identity, BJA)
+        tt(r(K, 64, 128), v("NF", 64, 128), v("NF", 0, 64), A.mult)
+        tt(v("JQ"), r(K, 64, 128), v("JA"), A.add)
+        ts(v("JT"), v("JQ"), 5, A.arith_shift_right, 4095, A.bitwise_and)
+        ts(r(K, 64, 128), v("JT"), -2048.0, A.add)
+        tt(v("PB"), NP, v("MM"), A.mult)
+        tt(v("PA", 64, 128), r(K, 64, 128), v("MM", 64, 128), A.mult)
+        tt(v("PA", 0, 64), v("TAB"), v("MM", 0, 64), A.mult, ix=v("LO", 8, 12))
+        mm(turned(r(K, 128, 256), (Ih, v("FC"), False), (NIh, v("PB"), False), (Ih, v("PA"), False)))
 
-    def send(name, h, t):
-        src = full("S%s%d%d" % (name, t, h))
-        dst = full("Z%d%d" % (t + 1, h)) if name == "Z" else ("TB%d%d" % (t + 1, h), 384, 512)
+    NE = []
+
+    def send(name, s, t):
+        x, y = r("S%s%d%d" % (name, t, s)), r("%s%d%d" % (name, t + 1, s))
         rid, pid, _ = topo.addr(nxt)
         en = topo.engines(core, nxt)
         en = en[:len(en) // 2] if name == "N" else en[len(en) // 2:]
         msk = sum(1 << e for e in en)
-        rs = "a%s%d%d" % (name.lower(), t + 1, h)
+        rs = "a%s%d%d" % (name.lower(), t + 1, s)
         NE.append(len(en))
-        x = ("link", 8 * len(NE), 8 * len(NE) + 1)
-        _add(gr, "G", 0.5, lambda: g.remote_dma(ap(dst), ap(src), T.sem[rs], T.sem.loc, pid, rid, msk), [src], [x], sem="loc")
-        _add(gr, "A", 2.5, None, [x], [dst], sem=(rs, len(en)))
+        ln = ("link", 8 * len(NE), 8 * len(NE) + 1)
+        _add(gr, "G", 0.5, lambda: g.remote_dma(ap(y), ap(x), T.sem[rs], T.sem.loc, pid, rid, msk), regs(x), [ln], sem="loc")
+        _add(gr, "A", 2.5, None, [ln], regs(y), sem=(rs, len(en)))
 
-    NE = []
-
-    def mine(h, t):
-        v = view(h, t); B = BK[h]; s = t + 1
-        F2, ET, EB, ELp, ELn, DW = (B, 0, 128), (B, 128, 256), (B, 256, 384), (B, 384, 392), (B, 392, 400), (B, 400, 408)
-        Z = full("Z%d%d" % (t, h))
+    def mine(s, t):
+        v = view(s); K, R, M = BK[s], BR[s], BM[s]
+        F2, ET, EB, EL = r(K, 128, 256), r(R, 0, 128), r(R, 128, 256), r(R, 256, 264)
+        Z = r("Z%d%d" % (t, s)); rows = slice(64 * s, 64 * s + 64)
         tt(v("FS"), F2, v("MS"), A.mult)
-        mm([(ET, v("FS"), BDh, True, True)])
-        tt(v("EMP"), ET, RM(0), A.mult)
-        mm([(ELp, v("EMP"), CC(0), True, True)])
+        mm(group(ET, (v("FS"), BDh)) + group(EB, (BDh, v("FS"))))
         if t < V - 1:
-            for p in range(2):
-                tc(("SN%d%d" % (t, h), 64 * p, 64 * p + 64), (B, p, 128, 2))
-            send("N", h, t)
+            tc(r("SN%d%d" % (t, s)), F2); send("N", s, t)
         else:
-            for q in range(4):
-                act(("YF", h * H + 32 * q, h * H + 32 * q + 32), (B, q, 128, 4), F.Identity, B2048)
-        ts(v("YO"), ELp, 2048.0, A.add)
-        yo = "YO%d" % h; yb = "YB%d" % h
-        _add(gr, "S", 0.065 + 128 * 1.5 * CY, lambda: sca.activation(out=sl(yb), in_=sl("X", 0, W).indirect(sl(yo)), func=F.Identity),
-             [("X", 0, W), full(yo)], [full(yb)])
-        tt(v("EMN"), ET, RM(s), A.mult); tc(v("ETF"), ET); ts(v("EPF"), ELp, 2048.0, A.add)
-        mm([(ELn, v("EMN"), CC(s), True, True), (EB, v("ETF"), PM(s), True, True)])
-        tc(v("ECL"), ELn); tc(v("EC"), EB)
-        mm([((B, 0, 128), Ib, v("YB"), True, False), ((B, 0, 128), Ib, Z, False, True),
-            ((B, 128, 256), Ib, v("YB"), True, False), ((B, 128, 256), NIh, v("ZQ"), False, True)])
-        ts(v("ZH"), (B, 0, 128), 0.5, A.mult, 1031.75, A.add)
+            for q in range(2):
+                act(v("YF", 64 * q, 64 * q + 64), r(K, 128 + q, 256, 2), F.Identity, B2048)
+            for h in range(2):
+                store("Y", T.yf[rows, H * h:H * h + H], v("YF", p0=64 * h, p1=64 * h + 64), 32768)
+        tt(v("EM"), ET, r("RM"), A.mult); tc(v("EC"), EB)
+        mm(group(EL, (v("EM"), r("CCh"))))
+        ts(v("YO"), EL, 2048.0, A.add); tc(v("EL"), EL)
+        act(v("YB"), v("X", 0, W), ix=v("YO"))
+        mm(turned(r(M, 0, 128), (Ib, Z, False), (Ib, v("YB"), True)))
+        ts(v("ZH"), r(M, 0, 128), 0.5, A.mult, 1031.75, A.add)
         if t < V - 1:
-            for p in range(2):
-                ts(("SZ%d%d" % (t, h), 64 * p, 64 * p + 64), v("ZH", p, 128, 2), -1032.0, A.add)
-            send("Z", h, t)
+            ts(r("SZ%d%d" % (t, s)), v("ZH"), -1032.0, A.add); send("Z", s, t)
         else:
-            for q in range(4):
-                ts(("YZ", h * H + 32 * q, h * H + 32 * q + 32), v("ZH", q, 128, 4), -1032.0, A.add)
-        act(v("NX"), (B, 128, 256), F.Relu, B1032)
-        ed = "ED%d" % h; ec = "EC%d" % h
+            for q in range(2):
+                ts(v("YZ", 64 * q, 64 * q + 64), v("ZH", q, 128, 2), -1032.0, A.add)
+            for h in range(2):
+                store("Y", T.yz[rows, H * h:H * h + H], v("YZ", p0=64 * h, p1=64 * h + 64), 16384)
+        mm([x for h in range(2) for x in turned(r(K, 256 + 128 * h, 384 + 128 * h), (r("ND%d" % h), v("ZQ"), False), (r("DUP%d" % h), v("YB"), True))])
+        act(v("NX"), r(K, 256, 512), F.Relu, B1032)
         for c in range(8):
-            _add(gr, "V", vc(64), lambda c=c: vec.tensor_scalar(out=T[ed][:, c, 0:H - 16 * c], in0=sl(ec, 16 * c, H),
-                 scalar1=ap(v("ECL", c, c + 1)), scalar2=None, op0=A.is_equal), [full(ec), v("ECL", c, c + 1)], [(ed, c, c + 1)])
-        if h == 1:
-            for c in range(8):
-                _add(gr, "V", vc(64), lambda c=c: vec.tensor_scalar(out=T.EX[:, c, :], in0=sl(ec),
-                     scalar1=ap(("ECL0", c, c + 1)), scalar2=None, op0=A.is_equal), [full(ec), ("ECL0", c, c + 1)], [("EX", c, c + 1)])
-        _add(gr, "V", vc(256), lambda: vec.tensor_tensor(out=T[ed][:, :, 0:16], in0=T[ed][:, :, 0:16], in1=T.TRI[:], op=A.mult),
-             [(ed, 0, 8), ("TRI", 0, 8)], [(ed, 0, 8)])
-
-        def dup():
-            for c in range(8):
-                x = ten.matmul(T[B][:, 256 + 16 * c:384], ap(BDb), T[ed][:, c, 0:H - 16 * c], c == 0, c == 7 and h == 0)
-            if h == 1:
-                for c in range(8):
-                    x = ten.matmul(T[B][:, 256:384], ap(BDb), T.EX[:, c, :], False, c == 7)
-            return x
-        _add(gr, "P", FIX["P"] + (700 + 1024 * h) * CY, dup, [reg(BDb), (ed, 0, 8)] + ([("EX", 0, 8)] if h else []), [EB])
-        ts(v("FLG"), EB, 0.0, A.is_gt)
-        mm([((B, 0, 128), v("FLG"), BD0, True, True)])
-        tt(v("DTM"), (B, 0, 128), RM(7 - s), A.mult)
-        mm([(DW, v("DTM"), CC(7 - s), True, True)])
-        tt(v("T1"), DW, ("TRC", 8 * h, 8 * h + 8), A.mult)
-        tt(v("T2"), v("T1"), v("EPF"), A.max)
-        tc(v("SO"), v("T2"))
-
-    def carve(h, t):
-        so = "SO%d" % h; nx = "NX%d" % h
-        _add(gr, "V", 0.05 + 128 * 3.5 * CY, lambda: vec.tensor_copy(out=sl("X").indirect(sl(so)), in_=sl(nx)),
-             [full(so), full(nx)], [("X", 0, W + C)])
+            ts(v("ED", H * c, H * c + H), v("EC"), v("EL", c, c + 1), A.is_equal, r("WT", 9 * t + c, 9 * t + c + 1), A.mult)
+        mm(group(ET, *[(v("ED", H * c, H * c + H), BDb) for c in range(8)]))
+        tt(v("DT"), ET, r("THR", 128 * t, 128 * t + 128), A.is_ge)
+        mm([x for h in range(2) for p in range(2) for x in group(r(R, 272 + 8 * h, 280 + 8 * h, p0=64 * p, p1=64 * p + 64),
+            (v("EM", 64 * h, 64 * h + 64), r("CCh")), (v("DT", 64 * h, 64 * h + 64), r("CCB")))])
+        tt(v("T1"), r(R, 272, 288), r("TRC"), A.min)
+        ts(v("SO"), v("T1"), 2048.0, A.add)
+        for h in (1, 0):
+            so, nx = v("SO", 8 * h, 8 * h + 8), v("NX", H * h, H * h + H)
+            _add(gr, "V", 0.05 + H * SCATTER * CY, lambda so=so, nx=nx: vec.tensor_copy(out=src(v("X"), so), in_=ap(nx)), regs(so, nx), regs(v("X")))
+        if t == V - 1:
+            for h in range(2):
+                store("YS"[h], T.yx[rows, 2048 * h:2048 * h + 2048], v("X", 2048 * h, 2048 * h + 2048, p0=64 * h, p1=64 * h + 64), 262144 * (1 + h))
 
     def limits():
-        B = BK[1]
-        mm([((B, 408, 409), full("ONE"), full("CNT0"), True, False), ((B, 408, 409), full("ONE"), full("CNT1"), False, True)])
-        tc(("EI", 0, 1), (B, 408, 409)); ts(("EI", 1, 2), ("EI", 0, 1), 3, A.bitwise_and)
-        tt(TOP, ("EI", 1, 2), LF, A.add)
-
-    B2048, B65536, B1032 = col(), col(), col()
-    for c, x in ((B2048, 2048.0), (B65536, 65536.0), (B1032, 1032.0)):
-        ts(c, KF, 0.0, A.mult, x, A.add)
+        B = BT[1]
+        mm(group(r(B, 0, 4), (r("ONES"), r("MT0")), (r("ONES"), r("MT1"))))
+        for k in range(2):
+            act(r("CN", 2, 6), r(B, 0, 4), acc=r("CN", k, k + 1))
+        ts(r("EI", 0, 2), r("CN", 0, 2), 0.5, A.mult, 512.0, A.add); ts(r("EI", 2, 4), r("EI", 0, 2), 3, A.bitwise_and)
+        tt(r("TOP"), r("EI", 2, 4), LF, A.add)
 
     numbers(0, 0); numbers(1, 0)
+    late_constants()
     for t in range(V):
-        scores(0, t); choose(0, t)
-        scores(1, t)
-        meet(0, t); mine(0, t)
-        choose(1, t); meet(1, t); mine(1, t)
-        if t < V - 1:
-            limits()
-        carve(0, t); carve(1, t)
-        if t < V - 1:
-            numbers(0, t + 1); numbers(1, t + 1)
-    store("Y", T.yf[:], full("YF")); store("S", T.yz[:], full("YZ"))
-    for k in range(4):
-        store("YS"[k & 1], T.yx[:, k * 1024:(k + 1) * 1024], ("X", k * 1024, (k + 1) * 1024))
+        for s in range(2):
+            gr["bulk"] = True
+            scores(s, t)
+            gr["bulk"] = False
+            choose(s, t)
+        for s in range(2):
+            meet(s, t)
+            if s == 1 and t < V - 1:
+                limits()
+            mine(s, t)
+            if t < V - 1:
+                numbers(s, t + 1)
 
     ops = gr["ops"]
     seq = _order(ops)
@@ -615,20 +580,14 @@ def rank_program(g, core, T, topo):
     for c in seq:
         o = ops[c]; q = o["q"]
         if q == "A":
-            o["key"] = o["sem"]
-            d = ops[o["deps"][0]] if o["deps"] else None
-            o["vc"] = {}
+            o["key"] = o["sem"]; o["vc"] = {}
             continue
         S = seen[q]
         want = {}
         for d in o["deps"]:
             k = ops[d].get("key")
-            if k is None:
-                continue
-            if S.get(k[0], 0) < k[1]:
-                want.setdefault(k[0], (0, None))
-                if want[k[0]][0] < k[1]:
-                    want[k[0]] = (k[1], d)
+            if k is not None and S.get(k[0], 0) < k[1] and want.get(k[0], (0, None))[0] < k[1]:
+                want[k[0]] = (k[1], d)
         for nm, (val, d) in sorted(want.items(), key=lambda kv: -ops[kv[1][1]].get("fin", 0)):
             if S.get(nm, 0) >= val:
                 continue
@@ -642,9 +601,7 @@ def rank_program(g, core, T, topo):
             count[q] += 1
             x.then_inc(T.sem[cs[q]], 1)
             o["key"] = (cs[q], count[q])
-        elif o["sem"] == "loc":
-            pass
-        else:
+        elif o["sem"] != "loc":
             x.then_inc(T.sem[o["sem"]], 16)
             o["key"] = (o["sem"], 16)
     for q in "VSPG":
@@ -654,4 +611,3 @@ def rank_program(g, core, T, topo):
         g.wait_ge(T.sem["d%d" % k], 16)
     if NE:
         g.wait_ge(T.sem.loc, sum(NE))
-    return ops

@@ -4,10 +4,13 @@ from concourse.mybir import AluOpType as A, AxisListType, ActivationFunctionType
 
 W, C, V = 4096, 256, 5
 H = 128
-NV = 80
-NS = H - NV
-ZG = 8
-TMW = 264
+NV = [64,64,64]
+VW = 32
+LW = 64
+KW = 4
+ZG = 16
+TMW = 1024
+HUGE = 2.0 ** 98
 
 SCRATCH = {}
 BUF = {}
@@ -30,17 +33,15 @@ def _sb(name, cols, dt):
 
 def _declare():
     b, h, f, i, u = "bfloat16", "float16", "float32", "int32", "uint16"
-    _sb("wl0", 16, i); _sb("wlb", 2, b); _sb("WL", 4, f)
-    _sb("PI", 1, i); _sb("CI", 256, i); _sb("C15", 256, i); _sb("CG", 256, i); _sb("CX", 256, i); _sb("CY", 256, f); _sb("CZ", 256, f)
-    _sb("ci", 32, i); _sb("cf", 64, f)
-    for n in ("BDb", "Ib", "S256", "C2048", "ONES", "DUP0", "DUP1", "T2", "CD"):
+    _sb("wl0", 16, i); _sb("wlb", 2, b); _sb("WL", 4, f); _sb("WW", 2, f)
+    _sb("ci", 16, i); _sb("cf", 16, f); _sb("ONES", 256, b); _sb("ZERO", 256, b)
+    for n in ("BD", "I", "S256", "C2048", "NHALF", "NI", "NI16", "I32", "I16", "DUP0", "DUP1", "ND0", "ND1", "RM", "NEG", "C15", "RW"):
         _sb(n, 128, b)
-    for n in ("BDh", "Ih", "NIh", "NI16", "I32", "I16", "ND0", "ND1", "RM"):
-        _sb(n, 128, h)
-    _sb("IND", 8, b); _sb("IND128", 8, b); _sb("CCh", 8, h); _sb("CCB", 8, b)
-    _sb("SH", 15 * 128, h); _sb("EE", 512, h); _sb("LA", 512, b); _sb("CM", 48, b); _sb("CADD", 12, b); _sb("RL", 4, u); _sb("RLI", 48, i)
-    _sb("TM", 2 * TMW, b); _sb("THR", V * 128, b); _sb("RO0", 45, i); _sb("RO1", 45, i); _sb("RO2", 45, i); _sb("RF", 45, f); _sb("WT", 45, f); _sb("TH", 8, f)
-    _sb("TRC", 16, f); _sb("EI", 4, i); _sb("CN", 8, f); _sb("TOP", 2, f)
+    _sb("IND128", 8, b); _sb("CCB", 8, b); _sb("REP", 512, b); _sb("REPI", 512, b); _sb("GA", 3 * 512, b)
+    _sb("SH", [8, 32], b); _sb("SHF", 2048, b); _sb("E0", 256, b); _sb("KL", 512, i); _sb("EE", 512, b); _sb("CI", 176, b); _sb("LA", 176, b)
+    _sb("CB", 96, b); _sb("CM", 32, b); _sb("CADD", 8, b); _sb("RL", 2, u); _sb("RLI", 4, i); _sb("T16", 512, b); _sb("TM", 2 * TMW, b)
+    _sb("RO", 24, i); _sb("RF", 5, f); _sb("WJ", 5, f); _sb("TH", 5, f); _sb("WT", 40, f)
+    _sb("TRI", 16, f); _sb("TRC", 16, f); _sb("EI", 4, i); _sb("CN", 8, f); _sb("TOP", 2, f)
     for k in range(2):
         s = str(k)
         _sb("X" + s, W + H, b); _sb("vein" + s, H, b); _sb("front" + s, H, i); _sb("W2" + s, 128, b)
@@ -49,16 +50,16 @@ def _declare():
         for t in range(V - 1):
             _sb("SN%d%d" % (t, k), H, h); _sb("SZ%d%d" % (t, k), H, b)
         _sb("VI" + s, 2 * H, i); _sb("VS" + s, 2 * H, i); _sb("MS" + s, H, b); _sb("NK" + s, 3 * H, f)
-        _sb("QI" + s, 3 * H, i); _sb("QS" + s, 3 * H, i); _sb("TB" + s, [H, 3], h); _sb("OV" + s, 3 * NV, u); _sb("OS" + s, [NS, 4], u)
-        _sb("ZR" + s, 16 * NV, b); _sb("U16" + s, 64, h); _sb("ZQ" + s, H, h)
-        _sb("D" + s, 48 * NV, b); _sb("A" + s, [H, 48], b); _sb("L" + s, [H, 48], b)
+        _sb("QI" + s, 3 * H, i); _sb("QS" + s, 3 * H, i); _sb("TB" + s, 3 * H, h); _sb("OF" + s, 3 * H, u)
+        _sb("ZR" + s, 16 * max(NV), b); _sb("U16" + s, 64, h); _sb("ZQ" + s, H, b); _sb("NZ" + s, H, b)
+        _sb("D" + s, 48 * H, b); _sb("L" + s, 48 * H, b)
         _sb("K0" + s, H, f); _sb("K1" + s, H, f); _sb("KI" + s, H, i); _sb("YI" + s, H, i); _sb("OK" + s, H, i)
         _sb("MK" + s, 3 * H, b); _sb("PR" + s, 4 * H, h)
-        _sb("FC" + s, H, h); _sb("NF" + s, H, f); _sb("G" + s, 256, h); _sb("R" + s, 4, f); _sb("RI" + s, 4, i); _sb("W8" + s, 8, i)
-        _sb("RR" + s, 48, b); _sb("LO" + s, 12, u); _sb("MT" + s, 4, b); _sb("TAB" + s, 1024, f); _sb("MM" + s, H, b)
+        _sb("FC" + s, H, h); _sb("NF" + s, H, f); _sb("G" + s, 256, h); _sb("R" + s, 4, i); _sb("W8" + s, 8, i)
+        _sb("RR" + s, 32, b); _sb("LO" + s, 8, u); _sb("MT" + s, 4, b); _sb("TAB" + s, 1024, f); _sb("MM" + s, H, b)
         _sb("JA" + s, 64, f); _sb("JQ" + s, 64, i); _sb("JT" + s, 64, i); _sb("PA" + s, H, h); _sb("PB" + s, H, h)
         _sb("FS" + s, H, h); _sb("EM" + s, H, h); _sb("EC" + s, H, h); _sb("EL" + s, 8, f); _sb("YO" + s, 8, u); _sb("YB" + s, H, b)
-        _sb("ZH" + s, H, h); _sb("NX" + s, 2 * H, b); _sb("ED" + s, 8 * H, b); _sb("DT" + s, H, b); _sb("T1" + s, 16, f); _sb("SO" + s, 16, u)
+        _sb("ZH" + s, H, f); _sb("NX" + s, 2 * H, b); _sb("ED" + s, 8 * H, b); _sb("DT" + s, H, b); _sb("T1" + s, 16, f); _sb("SO" + s, 16, u)
         _sb("YF" + s, H, f); _sb("YZ" + s, H, b)
     for k in range(8):
         SCRATCH["B%d" % k] = BUF["B%d" % k] = ("psum", [128, 512], "float32")
@@ -72,15 +73,20 @@ def _declare():
 _declare()
 
 CY = 0.00083
+PCY = 0.0005
 GATHER, SCATTER = 1.56, 3.8
 HOLD = {"G": 0.5, "Y": 0.1, "S": 0.1, "A": 0.1}
-LAT = 0.1
+LAT = 0.15
+FV = 0.045
+FS = 0.06
 SLACK = 0.04
 LEAD = 0.0
 
 
 def _add(gr, q, cost, fn, R, Wr, sem=None):
     ops = gr["ops"]; n = len(ops); deps = set()
+    if q == "G" and sem is None and ("alone", 0, 1) not in Wr:
+        R = R + [("alone", 0, 1)]
     for w, regs in ((False, R), (True, Wr)):
         for (name, a, b) in regs:
             if BUF.get(name, ("",))[0] == "psum":
@@ -105,7 +111,7 @@ def _add(gr, q, cost, fn, R, Wr, sem=None):
                 keep.append((n, a, b, w))
                 gr["acc"][name] = keep
     deps.discard(n)
-    ops.append({"q": q, "cost": cost, "fn": fn, "deps": sorted(deps), "sem": sem, "lead": gr["lead"], "bulk": gr["bulk"]})
+    ops.append({"q": q, "cost": cost, "fn": fn, "deps": sorted(deps), "sem": sem, "lead": gr["lead"], "bulk": gr["bulk"], "w": Wr})
     return n
 
 
@@ -164,25 +170,18 @@ def rank_program(g, core, T, topo):
     def r(n, a=0, b=None, st=1, p0=0, p1=128, last=None):
         return (n, a, BUF[n][1][1] if b is None else b, st, p0, p1, last)
 
-    def part(x, p0, p1):
-        return x[:4] + (p0, p1, x[6])
+    def cut(x, a, b, st=1, p0=0, p1=128):
+        return r(x[0], a, b, st, p0, p1)
 
     def ap(x):
         n, a, b, st, p0, p1, last = x
-        if len(BUF[n][1]) == 3:
-            if last is None:
-                last = slice(0, BUF[n][1][2])
-            return T[n][p0:p1, a, last] if st == 0 else T[n][p0:p1, a:b, last]
+        if last is not None:
+            return T[n][p0:p1, a:b, last]
         p, o = PLACE.get(n, (n, 0))
         return T[p][p0:p1, o + a:o + b:st] if st > 1 else T[p][p0:p1, o + a:o + b]
 
     def reg(x):
         n, a, b = x[:3]
-        if len(BUF[n][1]) == 3 and n[0] in "AL" and x[6] is not None:
-            m = (x[6].start if isinstance(x[6], slice) else x[6]) // 16
-            return [(n + "_%d" % m, a, b)]
-        if len(BUF[n][1]) == 3 and n[0] in "AL":
-            return [(n + "_%d" % m, a, b) for m in range(3)]
         if n[:-1] in ("X", "vein", "front", "G", "YF", "YZ"):
             return [(n + "_%d" % h, a, b) for h in range(2) if x[4] < 64 * h + 64 and 64 * h < x[5]]
         return [(n, a, b)]
@@ -191,10 +190,7 @@ def rank_program(g, core, T, topo):
         return sorted(set(y for x in xs if isinstance(x, tuple) for y in reg(x)))
 
     def cnt(x):
-        k = (x[2] - x[1] + max(x[3], 1) - 1) // max(x[3], 1)
-        if len(BUF[x[0]][1]) == 3:
-            k *= BUF[x[0]][1][2] if x[6] is None else (x[6].stop - x[6].start if isinstance(x[6], slice) else 1)
-        return k
+        return (x[2] - x[1] + x[3] - 1) // x[3] * (1 if x[6] is None else x[6].stop - x[6].start)
 
     def two(*xs):
         return all(BUF[x[0]][2] in ("bfloat16", "float16", "uint16") for x in xs)
@@ -206,7 +202,7 @@ def rank_program(g, core, T, topo):
         return ap(i).indirect(ap(ix)) if ix else ap(i)
 
     def vcost(o, i, ix, rate):
-        return 0.05 + cnt(o) * GATHER * CY if ix else max(64, cnt(o) * rate) * CY
+        return 0.05 + cnt(o) * GATHER * CY if ix else FV + max(64, cnt(o) * rate) * CY
 
     def tc(o, i):
         _add(gr, "V", vcost(o, i, None, 0.5 if two(o, i) else 1), lambda: vec.tensor_copy(out=ap(o), in_=ap(i)), regs(i), regs(o))
@@ -236,17 +232,17 @@ def rank_program(g, core, T, topo):
             if acc is not None:
                 kw["accum_out"] = ap(acc)
             return sca.activation(out=ap(o), in_=src(i, ix), func=func, **kw)
-        c = 0.065 + cnt(o) * GATHER * CY if ix else max(64, cnt(o)) * CY
+        c = 0.065 + cnt(o) * GATHER * CY if ix else FS + max(64, cnt(o)) * CY
         _add(gr, "S", c + extra, fn, regs(i, bias, scale, ix), regs(o, acc))
 
-    def mm(lst):
+    def mm(lst, span=None):
         def fn():
             x = None
             for o, l, q, s, e in lst:
                 x = ten.matmul(ap(o), ap(l), ap(q), s, e)
             return x
-        c = sum(max(min(64, cnt(l)), cnt(q)) * CY for o, l, q, s, e in lst)
-        lo = min(x[0][1] for x in lst); hi = max(x[0][2] for x in lst)
+        c = sum(max(min(64, cnt(l)), cnt(q)) * PCY for o, l, q, s, e in lst)
+        lo, hi = span or (min(x[0][1] for x in lst), max(x[0][2] for x in lst))
         _add(gr, "P", c, fn, regs(*[x[1] for x in lst], *[x[2] for x in lst]), [(lst[0][0][0], lo, hi)])
 
     def group(o, *pairs):
@@ -266,9 +262,9 @@ def rank_program(g, core, T, topo):
         eng = {"Y": syn, "S": sca}[q]
         _add(gr, q, 2.0 + byts / 150000.0, lambda: eng.dma_start(o(), i()), R, Wr, sem=s)
 
-    def load(q, o, x, byts, late=False):
-        dma(q, lambda: ap(o), lambda: x, [], regs(o), byts)
-        gr["ops"][-1]["first"] = not late
+    def load(q, o, x, byts, first=True, after=()):
+        dma(q, lambda: ap(o), lambda: x, regs(*after), regs(o), byts)
+        gr["ops"][-1]["first"] = first
 
     def store(q, x, i, byts):
         dma(q, lambda: x, lambda: ap(i), regs(i), [], byts)
@@ -281,105 +277,87 @@ def rank_program(g, core, T, topo):
             load("YS"[h], r("front%d" % s, p0=64 * h, p1=64 * h + 64), T.front[rows, H * h:H * h + H], 32768)
     for s in range(2):
         for h in range(2):
-            load("Y", r("X%d" % s, 0, W, p0=64 * h, p1=64 * h + 64), T.rock[64 * s:64 * s + 64, :], 524288 * (1 + h + 2 * s), late=True)
+            load("Y", r("X%d" % s, 0, W, p0=64 * h, p1=64 * h + 64), T.rock[64 * s:64 * s + 64, :], 524288 * (1 + h), False, [r("X0", 0, W)] * s)
 
     def iota(x, pattern, base, cm):
-        _add(gr, "G", 0.13 + 2 * cnt(x) * CY, lambda: g.iota(ap(x), pattern, base, cm), [], regs(x))
+        kw = {} if BUF[x[0]][2] == "int32" else {"allow_small_or_imprecise_dtypes": True}
+        _add(gr, "G", 0.13 + 2 * cnt(x) * CY, lambda: g.iota(ap(x), pattern, base, cm, **kw), [], regs(x) + [("alone", 0, 1)] * (x[4] > 0))
 
-    PI, CI, C15, CG, CX, CYf, CZ = r("PI"), r("CI"), r("C15"), r("CG"), r("CX"), r("CY"), r("CZ")
-    iota(PI, [[1, 1]], 0, 1); iota(CI, [[1, 256]], 0, 0)
-    nc = [0, 0]
+    def pick(o, i, pattern, op, x, base, cm):
+        _add(gr, "G", 0.17 + 2 * cnt(o) * CY, lambda: g.affine_select(ap(o), ap(i), pattern, op, x, base, cm), regs(i), regs(o))
 
-    def col():
-        nc[0] += 1
-        return r("cf", nc[0] - 1, nc[0])
-
-    def icol():
-        nc[1] += 1
-        return r("ci", nc[1] - 1, nc[1])
-
-    def cut(x, a, b, st=1):
-        return r(x[0], a, b, st)
-    PF = col(); tc(PF, PI)
-    k_i, g_i = icol(), icol()
-    ts(k_i, PI, 15, A.bitwise_and); ts(g_i, PI, 4, A.arith_shift_right)
-    KF, GF = col(), col(); tc(KF, k_i); tc(GF, g_i)
-    ts(CG, CI, 4, A.arith_shift_right); ts(C15, CI, 15, A.bitwise_and)
-    BDb, BDh, Ib, Ih, NIh, S256 = r("BDb"), r("BDh"), r("Ib"), r("Ih"), r("NIh"), r("S256")
-    ts(BDb, cut(CG, 0, 128), GF, A.is_equal); ts(Ib, cut(CI, 0, 128), PF, A.is_equal)
-    tc(Ih, Ib); ts(S256, BDb, 256.0, A.mult); ts(r("C2048"), Ib, 2048.0, A.mult); fill(r("ONES"), 1.0)
+    PI, k_i, g_i, p31 = [r("ci", k, k + 1) for k in range(4)]
+    KF, GF, P31, KS, NK0, NK1, NK2, LB, B4 = [r("cf", k, k + 1) for k in range(9)]
+    NKC = [NK0, NK1, NK2]
+    ONES, ZERO, BD_, I_, RM, S256 = r("ONES", 0, 128), r("ZERO", 0, 128), r("BD"), r("I"), r("RM"), r("S256")
+    IND = r("BD", 0, 128, 16)
+    fill(r("ZERO"), 0.0); fill(r("ONES"), 1.0)
+    iota(PI, [[1, 1]], 0, 1)
+    pick(I_, ZERO, [[-1, 128]], A.not_equal, 1.0, 0, 1)
+    pick(BD_, ONES, [[-16, 8], [0, 16]], A.is_ge, 0.0, 0, 1); pick(BD_, BD_, [[16, 8], [0, 16]], A.is_ge, 0.0, 15, -1)
+    iota(r("REPI"), [[1, 32], [0, 16]], 0, 0)
+    ts(k_i, PI, 15, A.bitwise_and); ts(g_i, PI, 4, A.arith_shift_right); ts(p31, PI, 31, A.bitwise_and)
+    tc(r("cf", 0, 3), r("ci", 1, 4))
+    ts(r("REP"), r("REPI"), P31, A.is_equal)
+    act(r("C2048"), I_, scale=2048.0); act(S256, BD_, scale=256.0); act(r("IND128"), IND, scale=128.0)
     tc(r("wlb"), r("wl0", 0, 16, 8))
-    mm([(r("B6", 2 * s, 2 * s + 2, p0=64 * h, p1=64 * h + 64), cut(Ib, 64 * s, 64 * s + 64), r("wlb"), True, True) for s in range(2) for h in range(2)])
-    act(r("WL"), r("B6", 0, 4))
+    mm([(r("B6", 2 * s, 2 * s + 2, p0=64 * h, p1=64 * h + 64), cut(I_, 64 * s, 64 * s + 64), r("wlb"), True, True) for s in range(2) for h in range(2)])
+    act(r("WL"), r("B6", 0, 4)); act(r("WW"), r("B6", 0, 4, 2), scale=2.0)
     for s in range(2):
-        ts(r("W2%d" % s), BDb, r("WL", 2 * s, 2 * s + 1), A.mult, 2.0, A.mult)
-    LF = r("WL", 1, 4, 2); tc(r("TOP"), LF)
-    KS = col(); ts(KS, KF, 256.0, A.mult, 1.0, A.add)
-    NKC = []
+        act(r("W2%d" % s), BD_, scale=r("WW", s, s + 1))
+    LF = r("WL", 1, 4, 2); act(r("TOP"), LF)
+    act(KS, KF, F.Identity, 1.0, 256.0)
     for m in range(3):
-        c = col(); NKC.append(c); sc = float(1 << (5 + m))
-        ts(c, KF, 37.0 * sc, A.mult, 613 * m * sc - 8388608.0, A.add)
-    IND, IND128 = r("IND"), r("IND128")
-    ts(IND, cut(CI, 0, 8), GF, A.is_equal); ts(IND128, IND, 128.0, A.mult)
-    B2048, BJA, B1032, BMT, BEX = col(), col(), col(), col(), col()
-    for c, x in ((B2048, 2048.0), (BJA, 98288.0 - 8388608.0), (B1032, 1032.0), (BMT, 4095.5), (BEX, 60 * math.log(3.0))):
-        ts(c, KF, 0.0, A.mult, x, A.add)
+        sc = float(1 << (5 + m))
+        act(NKC[m], KF, F.Identity, 613 * m * sc - 8388608.0, 37.0 * sc)
 
     def late_constants():
-        tc(BDh, BDb); ts(NIh, Ib, -1.0, A.mult); ts(r("NI16"), Ib, -0.0625, A.mult); ts(r("I32"), Ib, 32.0, A.mult); ts(r("I16"), Ib, 16.0, A.mult)
-        ts(r("RM"), cut(C15, 0, 128), KF, A.is_equal)
-        tc(r("CCh"), IND); ts(r("CCB"), IND, 8192.0, A.mult)
-        for h in range(2):
-            for p in range(2):
-                tc(r("DUP%d" % h, 64 * p, 64 * p + 64), cut(Ib, 64 * h, 64 * h + 64))
-            ts(r("ND%d" % h), r("DUP%d" % h), -1.0, A.mult)
-        ts(cut(CX, 0, 128), cut(C15, 0, 128), -1.0, A.mult, KF, A.add); ts(cut(CX, 128, 256), cut(CX, 0, 128), 15, A.bitwise_and)
-        ts(cut(CZ, 0, 128), cut(CX, 128, 256), 1.0, A.add); tt(r("CD"), cut(CZ, 0, 128), BDb, A.mult)
-        for d in range(1, 16):
-            ts(r("SH", 128 * (d - 1), 128 * d), r("CD"), d + 1.0, A.is_equal)
-        tt(CX, CG, C15, A.subtract); ts(CX, CX, 15, A.bitwise_and)
-        i64, i65 = col(), col()
-        ts(i64, PF, 64.0, A.is_equal, 16.0, A.mult); ts(i65, PF, 65.0, A.is_equal)
-        ts(CYf, CI, i64, A.mult); ts(CZ, CX, i65, A.mult); tt(CYf, CYf, CZ, A.add)
+        for n, x in (("NI16", -0.0625), ("I32", 32.0), ("I16", 16.0), ("NI", -1.0), ("NHALF", -0.5)):
+            act(r(n), I_, scale=x)
+        iota(r("C15"), [[0, 8], [1, 16]], 0, 0); ts(RM, r("C15"), KF, A.is_equal)
+        act(r("CCB"), IND, scale=8192.0); act(r("NEG"), RM, F.Identity, -HUGE, HUGE)
+        fill(r("E0"), 0.0)
+        iota(r("E0", p0=64, p1=65), [[16, 256]], 0, 0); iota(r("KL", 0, 256, p0=96, p1=97), [[1, 16], [-1, 16]], 0, 0)
+        ts(r("KL", 256, 512, p0=96, p1=97), r("KL", 0, 256, p0=96, p1=97), 15, A.bitwise_and); tc(r("E0", p0=96, p1=97), r("KL", 256, 512, p0=96, p1=97))
         for a in range(2):
-            cs, cj = col(), col()
-            ts(cs, PF, -16.0 * a, A.add); ts(cj, PF, -16.0 * a - 32.0, A.add)
             e = r("EE", 256 * a, 256 * a + 256)
-            ts(CZ, C15, cs, A.is_equal, -8192.0, A.mult); tt(e, CZ, CYf, A.add)
-            ts(CZ, CG, cj, A.is_equal, 8192.0, A.mult); tt(e, CZ, e, A.add)
+            pick(e, r("E0"), [[0, 16], [-1, 16]], A.not_equal, -8192.0, -16 * a, 1)
+            pick(e, e, [[-1, 16], [0, 16]], A.not_equal, 8192.0, -16 * a - 32, 1)
         for s in range(2):
             fill(r("G%d" % s, p0=64), 1.0)
-        hi_, b_, b_f = icol(), icol(), col()
-        ts(hi_, PI, 6, A.arith_shift_right); ts(b_, PI, 4, A.arith_shift_right, 3, A.bitwise_and); tc(b_f, b_)
-        base = col(); ts(base, hi_, 64.0, A.mult, KF, A.add)
-        for a in range(4):
-            c = col(); ts(c, base, 16.0 * a, A.add)
-            ts(r("LA", 128 * a, 128 * a + 128), cut(CI, 0, 128), c, A.is_equal)
-        RLI = r("RLI")
-        ts(RLI, cut(CI, 0, 48), 3, A.bitwise_and); ts(r("CM"), RLI, b_f, A.is_equal)
-        for a in range(4):
-            ts(r("CM", 12 * a + 8, 12 * a + 12), r("CM", 12 * a + 8, 12 * a + 12), 64.0, A.mult)
-        fill(r("CADD", 0, 4), 0.0); fill(r("CADD", 4, 8), float(TMW)); ts(r("CADD", 8, 12), cut(CI, 0, 4), 16.0, A.mult, KF, A.add)
-        j, ja, jx = r("CN", 0, 3), r("RLI", 0, 3), r("RLI", 8, 11)
-        ts(j, cut(CI, 0, 3), 16.0, A.mult, KF, A.add)
-        ts(ja, j, -5.5, A.add, 1.0 / 12.0, A.mult)
-        ts(jx, ja, -12.0, A.mult); tt(jx, jx, j, A.add); ts(jx, jx, 7.5, A.is_gt, 4.0, A.mult); tt(jx, jx, ja, A.add); tc(r("RL", 0, 3), jx)
-        c15 = col(); ts(c15, KF, -1.0, A.mult, 15.0, A.add)
+        _add(gr, "G", 0.17 + 512 * CY, lambda: g.affine_select(T.SH[:], ap(r("ZERO")), [[-16, 8], [0, 2], [-1, 16]], A.not_equal, 1.0, 0, 1), regs(r("ZERO")), regs(r("SH")))
+        for d in range(1, 16):
+            act(r("SHF", 128 * d, 128 * d + 128), r("SH", last=slice(d, d + 16)))
+        iota(r("CI"), [[1, 176]], 0, 0)
+        for h in range(2):
+            act(cut(LB, 7, 8, p0=64 * h, p1=64 * h + 64), cut(KF, 0, 1, p0=64 * h, p1=64 * h + 64), F.Identity, 48.0 + 64 * h)
+            act(cut(B4, 8, 9, p0=64 * h, p1=64 * h + 64), cut(GF, 1, 2, p0=64 * h, p1=64 * h + 64), F.Identity, -4.0 * h)
+        ts(r("LA"), r("CI"), LB, A.is_equal)
+        iota(r("CB", 0, 32), [[0, 8], [1, 4]], 0, 0); iota(r("CB", 32, 64), [[0, 4], [63, 2], [0, 4]], 1, 0)
+        ts(r("CB", 64, 96), r("CB", 0, 32), B4, A.is_equal); tt(r("CM"), r("CB", 64, 96), r("CB", 32, 64), A.mult)
+        act(r("CADD", 0, 4), cut(ZERO, 0, 4)); act(r("CADD", 4, 8), r("CI", 0, 4), F.Identity, KF, 16.0)
+        ts(r("RLI", 0, 2), r("CI", 0, 2), 16.0, A.mult, KF, A.add); ts(r("RLI", 2, 4), r("RLI", 0, 2), 2, A.arith_shift_right); tc(r("RL"), r("RLI", 2, 4))
         fill(r("TM"), 0.0)
-        tt(CX, CG, C15, A.subtract); ts(CYf, CX, c15, A.is_le); ts(CZ, C15, KF, A.is_lt); tt(r("TM", 0, 256), CYf, CZ, A.mult)
-        ts(r("TM", TMW, TMW + 256), CG, KF, A.is_le)
+        x, y, one = r("T16", 0, 256, p1=32), r("T16", 256, 512, p1=32), r("ONES", p1=32)
+        pick(x, one, [[0, 16], [-1, 16]], A.is_gt, 0.0, 0, 1); pick(x, x, [[-1, 16], [1, 16]], A.is_ge, 0.0, 15, -1)
+        pick(y, one, [[-1, 16], [0, 16]], A.is_ge, 0.0, 0, 1)
+        mm(group(r("B7"), (r("RM", p1=16), r("T16", p1=16))))
+        for j in range(2):
+            act(r("TM", TMW * j, TMW * j + 256), r("B7", 256 * j, 256 * j + 256))
+        for h in range(2):
+            pick(r("DUP%d" % h), ZERO, [[0, 2], [-1, 64]], A.not_equal, 1.0, -64 * h, 1)
+            act(r("ND%d" % h), r("DUP%d" % h), scale=-1.0)
         for t in range(V):
-            x = float(1 << (t + 2))
-            kx = col(); ts(kx, KF, x, A.mult)
-            ts(r("RO0", 9 * t, 9 * t + 8), cut(CI, 0, 8), 16.0 * x, A.mult, kx, A.add); ts(r("RO0", 9 * t + 8, 9 * t + 9), PI, x, A.mult)
-        ts(r("RO1"), r("RO0"), 127, A.bitwise_and); ts(r("RO2"), r("RO0"), 7, A.arith_shift_right); tt(r("RF"), r("RO1"), r("RO2"), A.add)
-        act(r("WT"), r("RF"), F.Exp, BEX, -math.log(3.0), extra=1.3)
-        ts(r("TH", 0, 5), r("WT", 8, 45, 9), 2.2, A.mult)
-        ts(r("T2"), r("RM"), -1e29, A.mult, 1e29, A.add)
+            iota(r("RO", t, t + 1), [[1, 1]], 0, 1 << (t + 2))
+        ts(r("RO", 8, 13), r("RO", 0, 5), 127, A.bitwise_and); ts(r("RO", 16, 21), r("RO", 0, 5), 7, A.arith_shift_right)
+        tt(r("RF"), r("RO", 8, 13), r("RO", 16, 21), A.add)
+        act(r("RF"), r("RF"), F.Identity, -60.0)
+        act(r("WJ"), r("RF"), F.Exp, None, -math.log(3.0), extra=1.3); act(r("TH"), r("WJ"), scale=2.2)
         for t in range(V):
-            ts(r("THR", 128 * t, 128 * t + 128), r("T2"), r("TH", t, t + 1), A.max)
-        ts(r("RLI", 16, 32), cut(CI, 0, 16), 7, A.bitwise_and); kt = col(); ts(kt, KF, 2048.0, A.add)
-        ts(r("TRC"), r("RLI", 16, 32), 16.0, A.mult, kt, A.add)
+            act(r("RW"), RM, scale=r("WJ", t, t + 1))
+            mm(group(r("B7", 8 * t, 8 * t + 8), (r("RW"), IND)))
+        act(r("WT"), r("B7", 0, 40))
+        iota(r("TRI"), [[0, 2], [16, 8]], 2048, 0); act(r("TRC"), r("TRI"), F.Identity, KF)
 
     for s in range(2):
         for p in range(2):
@@ -390,22 +368,26 @@ def rank_program(g, core, T, topo):
         gr["lead"] = LEAD * (1 - s)
         return lambda n, *a, **k: r(n + str(s), *a, **k)
 
-    BK, BR, BM, BT = ["B0", "B1"], ["B2", "B3"], ["B4", "B5"], ["B6", "B7"]
+    BK, BM, BD, BT = ["B0", "B1"], ["B2", "B3"], ["B4", "B5"], ["B6", "B7"]
 
     def numbers(s, t):
-        v = view(s); M = BM[s]
+        v = view(s); M = BM[s]; K = BK[s]
         Z, N = r("Z%d%d" % (t, s)), r("N%d%d" % (t, s))
         n, pq = r(M, 256, 384), r(M, 384, 512)
-        mm(group(n, (Ih, N), (r("C2048"), r("ONES"))))
+        mm(group(n, (I_, N), (r("C2048"), ONES)))
         for m in range(3):
             act(v("NK", m * H, m * H + H), n, F.Identity, NKC[m], float(1 << (5 + m)))
         mm(group(r(M, 0, 128), (v("W2"), Z)) + turned(r(M, 128, 256), (S256, Z, False)))
+        mm(group(r(K, 0, 128), (Z, I_))); act(v("NZ"), r(K, 0, 128), scale=-1.0)
+        nz = max(NV)
         for k in range(16):
-            o = v("ZR", k, 16 * NV, 16); z = cut(Z, 0, NV)
-            if k < ZG:
-                _add(gr, "G", 0.17 + 2 * NV * CY, lambda o=o, z=z: g.affine_select(ap(o), ap(z), [[0, NV]], A.is_ge, 0.0, 0, 0), regs(z), [("ZR%d_%d" % (s, k), 0, 1)])
+            o = v("ZR", k, 16 * nz, 16); z = cut(Z, 0, nz); wr = [("ZR%d_%d" % (s, k), 0, 1)]
+            if t == 0:
+                _add(gr, "S", FS + max(64, nz) * CY, lambda o=o, z=z: sca.activation(out=ap(o), in_=ap(z), func=F.Identity), regs(z), wr)
+            elif k < ZG:
+                _add(gr, "G", 0.17 + 2 * nz * CY, lambda o=o, z=z: g.affine_select(ap(o), ap(z), [[0, nz]], A.is_ge, 0.0, 0, 0), regs(z), wr)
             else:
-                _add(gr, "V", max(64, NV / 2) * CY, lambda o=o, z=z: vec.tensor_copy(out=ap(o), in_=ap(z)), regs(z), [("ZR%d_%d" % (s, k), 0, 1)])
+                _add(gr, "V", FV + max(64, nz / 2) * CY, lambda o=o, z=z: vec.tensor_copy(out=ap(o), in_=ap(z)), regs(z), wr)
         ts(v("VI"), r(M, 0, 256), 1.0, A.add); ts(v("VS"), v("VI"), 4095, A.bitwise_and)
         tt(pq, n, v("VS", 0, 128), A.mult)
         for m in range(3):
@@ -413,34 +395,36 @@ def rank_program(g, core, T, topo):
             tt(v("QI", *o), pq, v("NK", *o), A.add)
         for m in range(3):
             o = (m * H, m * H + H)
-            _add(gr, "V", H * CY, lambda m=m, o=o: vec.tensor_scalar(out=ap(v("QS", m, 3 * H, 3)), in0=ap(v("QI", *o)), scalar1=5 + m, scalar2=4095,
-                 op0=A.arith_shift_right, op1=A.bitwise_and), regs(v("QI", *o)), [("QS%d" % s, m, m + 1)])
-        _add(gr, "V", 3 * H * CY, lambda: vec.tensor_scalar(out=ap(v("TB")), in0=ap(v("QS")), scalar1=-2048.0, scalar2=None, op0=A.add),
-             [("QS%d" % s, 0, 3)], regs(v("TB")))
-        ts(v("OS", last=slice(0, 3)), v("TB", NV, H), 2048.0, A.add)
-        for m in range(3):
-            ts(v("OV", m * NV, m * NV + NV), v("TB", 0, NV, last=m), 2048.0, A.add)
-        mm([x for m in range(3) for x in group(r(BR[s], m * H, m * H + H), (v("TB", last=m), Ih))] + group(r(BR[s], 384, 512), (N, Ih)))
+            ts(v("QS", *o), v("QI", *o), 5 + m, A.arith_shift_right, 4095, A.bitwise_and)
+        tc(v("OF"), v("QS")); ts(v("TB"), v("OF"), -2048.0, A.add)
+        mm([x for m in range(3) for x in group(r(M, m * H, m * H + H), (v("TB", m * H, m * H + H), I_))] + group(r(M, 384, 512), (N, I_)))
         ts(v("MS"), v("VS", 128, 256), KS, A.is_equal)
         ts(v("U16"), v("VS", 64, 128), -2048.0, A.add)
-        ts(v("ZQ"), Z, 0.25, A.mult, 1031.625, A.add)
+        act(v("ZQ"), Z, F.Identity, 159.625, 0.25)
+
+    turn = [0]
 
     def scores(s, t):
-        v = view(s); X = v("X", 0, W); Z = r("Z%d%d" % (t, s)); zr = [("ZR%d_%d" % (s, k), 0, 1) for k in range(16)]
-        for c in range(NS):
-            act(v("A", NV + c, NV + c + 1, 0), X, F.Abs, cut(Z, NV + c, NV + c + 1), -1.0, ix=v("OS", c, c + 1, 0, last=slice(0, 3)))
+        v = view(s); X = v("X", 0, W); zr = [("ZR%d_%d" % (s, k), 0, 1) for k in range(16)]
         for m in range(3):
-            ms = slice(16 * m, 16 * m + 16)
-            for a in range(0, NV, 32):
-                b = min(NV, a + 32); d = v("D", 16 * (m * NV + a), 16 * (m * NV + b)); ix = v("OV", m * NV + a, m * NV + b)
+            o = 16 * H * m
+            for a in range(NV[m], H, 32):
+                turn[0] += 1
+                ga = r("GA", 512 * (turn[0] % 3), 512 * (turn[0] % 3) + 512); bk = BD[turn[0] & 1]
+                act(ga, X, ix=v("OF", m * H + a, m * H + a + 32))
+                mm(group(r(bk), (v("NZ", p0=a, p1=a + 32), r("REP", p0=a, p1=a + 32)), (I_, ga)))
+                act(v("D", o + 16 * a, o + 16 * a + 512), r(bk), F.Abs)
+            for a in range(0, NV[m], VW):
+                b = min(NV[m], a + VW); d = v("D", o + 16 * a, o + 16 * b); ix = v("OF", m * H + a, m * H + b)
                 _add(gr, "V", vcost(d, X, ix, 1), lambda a=a, b=b, d=d, ix=ix: vec.tensor_tensor(
                     out=ap(d), in0=src(X, ix), in1=ap(v("ZR", 16 * a, 16 * b)), op=A.subtract), regs(X, ix) + zr, regs(d))
-                act(v("A", a, b, last=ms), d, F.Abs)
-            for a in range(0, H, 64):
-                ts(v("L", a, a + 64, last=ms), v("A", a, a + 64, last=ms), r("TOP", s, s + 1), A.is_le, 2.0 * m + 0.4375, A.add)
-            for k0 in range(0, 16, 4):
-                mm([x for k in range(k0, k0 + 4) for x in group(r(BK[s], m * H + k, m * H + H, 16),
-                    (v("A", last=16 * m + k), IND128), (v("L", last=16 * m + k), IND))])
+                act(d, d, F.Abs)
+            for a in range(0, H, LW):
+                x = (o + 16 * a, o + 16 * (a + LW))
+                ts(v("L", *x), v("D", *x), r("TOP", s, s + 1), A.is_le, 2.0 * m + 0.4375, A.add)
+            for k0 in range(0, 16, KW):
+                mm([x for k in range(k0, k0 + KW) for x in group(r(BK[s], m * H + k, m * H + H, 16),
+                    (v("D", o + k, o + 16 * H, 16), r("IND128")), (v("L", o + k, o + 16 * H, 16), IND))], (m * H + 8 * k0, m * H + 8 * (k0 + KW)))
 
     def choose(s, t):
         v = view(s); B = BK[s]; N = r("N%d%d" % (t, s))
@@ -451,44 +435,44 @@ def rank_program(g, core, T, topo):
         ts(v("OK"), v("KI"), 16, A.bitwise_and)
         for m in range(3):
             ts(v("MK", m * H, m * H + H), v("YI"), 32.0 * m + 16.0, A.is_equal)
-        tt(v("PR", 384, 512), r(BR[s], 384, 512), v("OK"), A.mult)
-        tt(v("PR", 0, 384), r(BR[s], 0, 384), v("MK"), A.mult)
-        mm(group(r(BM[s], 0, 128), (Ih, N), (v("PR", 384, 512), r("NI16")), *[(v("PR", m * H, m * H + H), Ih) for m in range(3)]))
+        tt(v("PR", 384, 512), r(BM[s], 384, 512), v("OK"), A.mult)
+        tt(v("PR", 0, 384), r(BM[s], 0, 384), v("MK"), A.mult)
+        mm(group(r(B, 384, 512), (I_, N), (v("PR", 384, 512), r("NI16")), *[(v("PR", m * H, m * H + H), I_) for m in range(3)]))
 
     def meet(s, t):
-        v = view(s); NP = r(BM[s], 0, 128); R = BR[s]; K = BK[s]
+        v = view(s); NP = r(BK[s], 384, 512); R = BM[s]; K = BK[s]
         tc(v("FC"), NP)
-        act(v("NF"), NP, F.Identity, B2048)
-        mm([(r(R, 128 * x + 64 * h, 128 * x + 64 * h + 64, p0=32 * j, p1=32 * j + 32), cut(Ih, 64 * h + 32 * x, 64 * h + 32 * x + 32),
+        act(v("NF"), NP, F.Identity, 2048.0)
+        mm([(r(R, 128 * x + 64 * h, 128 * x + 64 * h + 64, p0=32 * j, p1=32 * j + 32), cut(I_, 64 * h + 32 * x, 64 * h + 32 * x + 32),
              v("FC", 64 * j, 64 * j + 64), True, True) for x in range(2) for h in range(2) for j in range(2)])
         ts(v("G", p1=64), r(R, 0, 256, p1=64), 0.125, A.mult, 1287.5625, A.add)
         for x in range(2):
-            mm([(r(BT[x], 256 * a, 256 * a + 256), v("G", 128 * x, 128 * x + 128, p1=66), r("EE", 256 * a, 256 * a + 256, p1=66), True, True) for a in range(2)])
+            mm([(r(BT[x], 256 * a, 256 * a + 256), v("G", 128 * x, 128 * x + 128, p1=97), r("EE", 256 * a, 256 * a + 256, p1=97), True, True) for a in range(2)])
             for a in range(2):
                 o, i = v("R", 2 * x + a, 2 * x + a + 1), r(BT[x], 256 * a, 256 * a + 256)
-                _add(gr, "V", 256 * CY, lambda o=o, i=i: vec.tensor_reduce(out=ap(o), in_=ap(i), axis=AxisListType.X, op=A.min, apply_absolute_value=True), regs(i), regs(o))
-        ts(v("RI"), v("R"), 4096.0, A.min)
-        ts(v("W8", 0, 4), v("RI"), 4, A.arith_shift_right); ts(v("W8", 4, 8), v("RI"), 15, A.bitwise_and)
-        tt(v("RR"), v("W8"), r("CM"), A.mult, ix=r("RL", 0, 3))
-        mm(group(r(R, 256, 268), (Ib, r("CADD")), *[(r("LA", 128 * a, 128 * a + 128), v("RR", 12 * a, 12 * a + 12)) for a in range(4)]))
-        tc(v("LO"), r(R, 256, 268))
+                _add(gr, "V", FV + 256 * CY, lambda o=o, i=i: vec.tensor_reduce(out=ap(o), in_=ap(i), axis=AxisListType.X, op=A.min, apply_absolute_value=True), regs(i), regs(o))
+        ts(v("W8", 0, 8, 2), v("R"), 4, A.arith_shift_right); ts(v("W8", 1, 8, 2), v("R"), 15, A.bitwise_and)
+        tt(v("RR"), v("W8"), r("CM"), A.mult, ix=r("RL"))
+        mm(group(r(R, 256, 264), (I_, r("CADD")), *[(r("LA", 48 - 16 * a, 176 - 16 * a), v("RR", 8 * a, 8 * a + 8)) for a in range(4)]))
+        ts(v("LO"), r(R, 256, 264), TMW - 1.0, A.min)
         if t < V - 1:
-            act(v("MT"), v("R"), F.Sign, BMT, -1.0)
+            act(v("MT"), r(R, 256, 260), F.Sign, 255.5, -1.0)
         J = v("FC", 64, 128)
         for x in range(2):
-            mm([(r(BT[x], 64 * d, 64 * d + 64), r("SH", 128 * (8 * x + d - 1), 128 * (8 * x + d)) if x + d else Ih, J, True, True) for d in range(8)])
+            mm([(r(BT[x], 64 * d, 64 * d + 64), r("SHF", 128 * (8 * x + d), 128 * (8 * x + d + 1)) if x + d else I_, J, True, True) for d in range(8)])
             act(v("TAB", 512 * x, 512 * x + 512), r(BT[x]))
-        act(v("MM"), r("TM"), ix=v("LO", 0, 8))
+        for j in range(2):
+            act(v("MM", 64 * j, 64 * j + 64), r("TM", TMW * j, TMW * j + TMW), ix=v("LO", 0, 4))
         mm(group(r(K, 0, 64), (r("I32"), J), (r("I16"), v("U16"))))
-        act(v("JA"), r(K, 0, 64), F.Identity, BJA)
+        act(v("JA"), r(K, 0, 64), F.Identity, 98288.0 - 8388608.0)
         tt(r(K, 64, 128), v("NF", 64, 128), v("NF", 0, 64), A.mult)
         tt(v("JQ"), r(K, 64, 128), v("JA"), A.add)
         ts(v("JT"), v("JQ"), 5, A.arith_shift_right, 4095, A.bitwise_and)
         ts(r(K, 64, 128), v("JT"), -2048.0, A.add)
         tt(v("PB"), NP, v("MM"), A.mult)
         tt(v("PA", 64, 128), r(K, 64, 128), v("MM", 64, 128), A.mult)
-        tt(v("PA", 0, 64), v("TAB"), v("MM", 0, 64), A.mult, ix=v("LO", 8, 12))
-        mm(turned(r(K, 128, 256), (Ih, v("FC"), False), (NIh, v("PB"), False), (Ih, v("PA"), False)))
+        tt(v("PA", 0, 64), v("TAB"), v("MM", 0, 64), A.mult, ix=v("LO", 4, 8))
+        mm(turned(r(K, 128, 256), (I_, v("FC"), False), (r("NI"), v("PB"), False), (I_, v("PA"), False)))
 
     NE = []
 
@@ -505,39 +489,39 @@ def rank_program(g, core, T, topo):
         _add(gr, "A", 2.5, None, [ln], regs(y), sem=(rs, len(en)))
 
     def mine(s, t):
-        v = view(s); K, R, M = BK[s], BR[s], BM[s]
+        v = view(s); K, R = BK[s], BM[s]
         F2, ET, EB, EL = r(K, 128, 256), r(R, 0, 128), r(R, 128, 256), r(R, 256, 264)
         Z = r("Z%d%d" % (t, s)); rows = slice(64 * s, 64 * s + 64)
         tt(v("FS"), F2, v("MS"), A.mult)
-        mm(group(ET, (v("FS"), BDh)) + group(EB, (BDh, v("FS"))))
+        mm(group(ET, (v("FS"), BD_)) + group(EB, (BD_, v("FS"))))
         if t < V - 1:
             tc(r("SN%d%d" % (t, s)), F2); send("N", s, t)
         else:
             for q in range(2):
-                act(v("YF", 64 * q, 64 * q + 64), r(K, 128 + q, 256, 2), F.Identity, B2048)
+                act(v("YF", 64 * q, 64 * q + 64), r(K, 128 + q, 256, 2), F.Identity, 2048.0)
             for h in range(2):
                 store("Y", T.yf[rows, H * h:H * h + H], v("YF", p0=64 * h, p1=64 * h + 64), 32768)
-        tt(v("EM"), ET, r("RM"), A.mult); tc(v("EC"), EB)
-        mm(group(EL, (v("EM"), r("CCh"))))
-        ts(v("YO"), EL, 2048.0, A.add); tc(v("EL"), EL)
+        tt(v("EM"), ET, RM, A.mult); tc(v("EC"), EB)
+        mm(group(EL, (v("EM"), IND)))
+        ts(v("YO"), EL, 2048.0, A.add); act(v("EL"), EL)
         act(v("YB"), v("X", 0, W), ix=v("YO"))
-        mm(turned(r(M, 0, 128), (Ib, Z, False), (Ib, v("YB"), True)))
-        ts(v("ZH"), r(M, 0, 128), 0.5, A.mult, 1031.75, A.add)
+        mm(turned(r(K, 0, 128), (I_, Z, False), (r("NHALF"), ONES, True), (I_, v("YB"), True)))
+        act(v("ZH"), r(K, 0, 128), F.Identity, 12582912.0, 0.5)
         if t < V - 1:
-            ts(r("SZ%d%d" % (t, s)), v("ZH"), -1032.0, A.add); send("Z", s, t)
+            act(r("SZ%d%d" % (t, s)), v("ZH"), F.Identity, -12582912.0); send("Z", s, t)
         else:
             for q in range(2):
-                ts(v("YZ", 64 * q, 64 * q + 64), v("ZH", q, 128, 2), -1032.0, A.add)
+                act(v("YZ", 64 * q, 64 * q + 64), v("ZH", q, 128, 2), F.Identity, -12582912.0)
             for h in range(2):
                 store("Y", T.yz[rows, H * h:H * h + H], v("YZ", p0=64 * h, p1=64 * h + 64), 16384)
         mm([x for h in range(2) for x in turned(r(K, 256 + 128 * h, 384 + 128 * h), (r("ND%d" % h), v("ZQ"), False), (r("DUP%d" % h), v("YB"), True))])
-        act(v("NX"), r(K, 256, 512), F.Relu, B1032)
+        act(v("NX"), r(K, 256, 512), F.Relu, 160.0)
         for c in range(8):
-            ts(v("ED", H * c, H * c + H), v("EC"), v("EL", c, c + 1), A.is_equal, r("WT", 9 * t + c, 9 * t + c + 1), A.mult)
-        mm(group(ET, *[(v("ED", H * c, H * c + H), BDb) for c in range(8)]))
-        tt(v("DT"), ET, r("THR", 128 * t, 128 * t + 128), A.is_ge)
+            ts(v("ED", H * c, H * c + H), v("EC"), v("EL", c, c + 1), A.is_equal, r("WT", 8 * t + c, 8 * t + c + 1), A.mult)
+        mm(group(ET, (I_, r("NEG")), *[(v("ED", H * c, H * c + H), BD_) for c in range(8)]))
+        ts(v("DT"), ET, r("TH", t, t + 1), A.is_ge)
         mm([x for h in range(2) for p in range(2) for x in group(r(R, 272 + 8 * h, 280 + 8 * h, p0=64 * p, p1=64 * p + 64),
-            (v("EM", 64 * h, 64 * h + 64), r("CCh")), (v("DT", 64 * h, 64 * h + 64), r("CCB")))])
+            (v("EM", 64 * h, 64 * h + 64), IND), (v("DT", 64 * h, 64 * h + 64), r("CCB")))])
         tt(v("T1"), r(R, 272, 288), r("TRC"), A.min)
         ts(v("SO"), v("T1"), 2048.0, A.add)
         for h in (1, 0):
@@ -549,7 +533,7 @@ def rank_program(g, core, T, topo):
 
     def limits():
         B = BT[1]
-        mm(group(r(B, 0, 4), (r("ONES"), r("MT0")), (r("ONES"), r("MT1"))))
+        mm(group(r(B, 0, 4), (ONES, r("MT0")), (ONES, r("MT1"))))
         for k in range(2):
             act(r("CN", 2, 6), r(B, 0, 4), acc=r("CN", k, k + 1))
         ts(r("EI", 0, 2), r("CN", 0, 2), 0.5, A.mult, 512.0, A.add); ts(r("EI", 2, 4), r("EI", 0, 2), 3, A.bitwise_and)

@@ -7,6 +7,9 @@ H = 128
 NV = [64,64,64]
 VW = 32
 LW = 64
+OFP = [[0,128],[128,384]]
+ZS = 4
+CV = 3
 KW = 4
 ZG = 16
 TMW = 1024
@@ -33,11 +36,12 @@ def _sb(name, cols, dt):
 
 def _declare():
     b, h, f, i, u = "bfloat16", "float16", "float32", "int32", "uint16"
-    _sb("wl0", 16, i); _sb("wlb", 2, b); _sb("WL", 4, f); _sb("WW", 2, f)
+    _sb("wl0", 16, i); _sb("wlb", 2, b); _sb("WL", 4, f); _sb("WW", 6, f)
     _sb("ci", 16, i); _sb("cf", 16, f); _sb("ONES", 256, b); _sb("ZERO", 256, b)
-    for n in ("BD", "I", "S256", "C2048", "NHALF", "NI", "NI16", "I32", "I16", "DUP0", "DUP1", "ND0", "ND1", "RM", "NEG", "C15", "RW"):
+    for n in ("BD", "I", "BD16", "NK16", "C160", "C160K", "N4096", "N23", "N65536", "I16", "I32", "I64", "I128", "HALF", "NQ", "NI", "NI16",
+              "DUP0", "DUP1", "ND0", "ND1", "RM", "NEG", "C15", "RW"):
         _sb(n, 128, b)
-    _sb("IND128", 8, b); _sb("CCB", 8, b); _sb("REP", 512, b); _sb("REPI", 512, b); _sb("GA", 3 * 512, b)
+    _sb("IND128", 8, b); _sb("CCB", 8, b); _sb("OFF8", 8, b); _sb("REP", 512, b); _sb("REPI", 512, b); _sb("GA", 3 * 512, b)
     _sb("SH", [8, 32], b); _sb("SHF", 2048, b); _sb("E0", 256, b); _sb("KL", 512, i); _sb("EE", 512, b); _sb("CI", 176, b); _sb("LA", 176, b)
     _sb("CB", 96, b); _sb("CM", 32, b); _sb("CADD", 8, b); _sb("RL", 2, u); _sb("RLI", 4, i); _sb("T16", 512, b); _sb("TM", 2 * TMW, b)
     _sb("RO", 24, i); _sb("RF", 5, f); _sb("WJ", 5, f); _sb("TH", 5, f); _sb("WT", 40, f)
@@ -49,9 +53,9 @@ def _declare():
             _sb("Z%d%d" % (t, k), H, b); _sb("N%d%d" % (t, k), H, h)
         for t in range(V - 1):
             _sb("SN%d%d" % (t, k), H, h); _sb("SZ%d%d" % (t, k), H, b)
-        _sb("VI" + s, 2 * H, i); _sb("VS" + s, 2 * H, i); _sb("MS" + s, H, b); _sb("NK" + s, 3 * H, f)
+        _sb("HB" + s, H, b); _sb("XR" + s, H, f); _sb("XS" + s, H, b); _sb("W16" + s, 128, b); _sb("W2K" + s, 128, b); _sb("MS" + s, H, b); _sb("NK" + s, 3 * H, f)
         _sb("QI" + s, 3 * H, i); _sb("QS" + s, 3 * H, i); _sb("TB" + s, 3 * H, h); _sb("OF" + s, 3 * H, u)
-        _sb("ZR" + s, 16 * max(NV), b); _sb("U16" + s, 64, h); _sb("ZQ" + s, H, b); _sb("NZ" + s, H, b)
+        _sb("ZR" + s, 16 * max(NV), b); _sb("ZQ" + s, H, b); _sb("NZ" + s, H, b)
         _sb("D" + s, 48 * H, b); _sb("L" + s, 48 * H, b)
         _sb("K0" + s, H, f); _sb("K1" + s, H, f); _sb("KI" + s, H, i); _sb("YI" + s, H, i); _sb("OK" + s, H, i)
         _sb("MK" + s, 3 * H, b); _sb("PR" + s, 4 * H, h)
@@ -73,14 +77,20 @@ def _declare():
 _declare()
 
 CY = 0.00083
-PCY = 0.0005
+PCY = 0.00045
 GATHER, SCATTER = 1.56, 3.8
 HOLD = {"G": 0.5, "Y": 0.1, "S": 0.1, "A": 0.1}
-LAT = 0.15
-FV = 0.045
+LAT = 0.2
+DFIX = 1.7
+DRATE = 250000.0
+FV = 0.05
 FS = 0.06
 SLACK = 0.04
 LEAD = 0.0
+ROUNDS = 4
+PERIODS = []
+SPANS = [10,13,16]
+ORDER = []
 
 
 def _add(gr, q, cost, fn, R, Wr, sem=None):
@@ -156,7 +166,54 @@ def _order(ops):
             est[s] = max(est[s], fin[c] + LAT)
             if need[s] == 0:
                 ready.setdefault(ops[s]["q"], []).append(s)
-    return out
+    pred = [o["deps"] for o in ops]
+    best = (max(fin), out, fin)
+    starts = [fin]
+    part = {}
+    for i in range(n):
+        if ops[i]["bulk"]:
+            part.setdefault((ops[i]["bulk"], ops[i]["q"]), []).append(i)
+    for period in PERIODS:
+        for span in SPANS:
+            due = [1e9] * n
+            for (k, q), lst in part.items():
+                tot = sum(ops[i]["cost"] for i in lst); acc = 0.0
+                for i in lst:
+                    due[i] = period * k / 2 + span * acc / tot; acc += ops[i]["cost"]
+            for i in range(n - 1, -1, -1):
+                due[i] = min([due[i], period * (V + 1)] + [due[s] - LAT - ops[i]["cost"] for s in succ[i]]) - 1e3 * ops[i].get("first", 0)
+            starts.append(_place(ops, sorted(range(n), key=lambda i: (due[i], i)), pred, False))
+    for fin in starts:
+        for _ in range(ROUNDS):
+            if max(fin) < best[0]:
+                best = (max(fin), sorted(range(n), key=lambda i: (fin[i] - ops[i]["cost"], i)), fin)
+            back = _place(ops, sorted(range(n), key=lambda i: -fin[i]), succ, True)
+            fin = _place(ops, sorted(range(n), key=lambda i: -back[i]), pred, False)
+    return best[1], best[2]
+
+
+def _place(ops, order, before, backward):
+    fin = [0.0] * len(ops); busy = {}
+    for i in order:
+        o = ops[i]; q = o["q"]; dur = o["cost"]
+        st = max([fin[d] + LAT for d in before[i]] or [0.0])
+        if q != "A":
+            hold = HOLD[q] if o["sem"] is not None else dur
+            off = dur - hold if backward else 0.0
+            lst = busy.setdefault(q, [])
+            a = st + off; lo = 0; hi = len(lst)
+            while lo < hi:
+                mid = (lo + hi) // 2
+                if lst[mid][1] <= a:
+                    lo = mid + 1
+                else:
+                    hi = mid
+            while lo < len(lst) and lst[lo][0] < a + hold - 1e-9:
+                a = max(a, lst[lo][1]); lo += 1
+            lst.insert(lo, (a, a + hold))
+            st = a - off
+        fin[i] = st + dur
+    return fin
 
 
 def rank_program(g, core, T, topo):
@@ -260,7 +317,7 @@ def rank_program(g, core, T, topo):
     def dma(q, o, i, R, Wr, byts):
         s = "d%d" % dn[0]; dn[0] += 1
         eng = {"Y": syn, "S": sca}[q]
-        _add(gr, q, 2.0 + byts / 150000.0, lambda: eng.dma_start(o(), i()), R, Wr, sem=s)
+        _add(gr, q, DFIX + byts / DRATE, lambda: eng.dma_start(o(), i()), R, Wr, sem=s)
 
     def load(q, o, x, byts, first=True, after=()):
         dma(q, lambda: ap(o), lambda: x, regs(*after), regs(o), byts)
@@ -286,10 +343,19 @@ def rank_program(g, core, T, topo):
     def pick(o, i, pattern, op, x, base, cm):
         _add(gr, "G", 0.17 + 2 * cnt(o) * CY, lambda: g.affine_select(ap(o), ap(i), pattern, op, x, base, cm), regs(i), regs(o))
 
+    alt = [0]
+
+    def times(o, i, x):
+        alt[0] += 1
+        if alt[0] % CV:
+            ts(o, i, x, A.mult)
+        else:
+            act(o, i, scale=x)
+
     PI, k_i, g_i, p31 = [r("ci", k, k + 1) for k in range(4)]
     KF, GF, P31, KS, NK0, NK1, NK2, LB, B4 = [r("cf", k, k + 1) for k in range(9)]
     NKC = [NK0, NK1, NK2]
-    ONES, ZERO, BD_, I_, RM, S256 = r("ONES", 0, 128), r("ZERO", 0, 128), r("BD"), r("I"), r("RM"), r("S256")
+    ONES, ZERO, BD_, I_, RM = r("ONES", 0, 128), r("ZERO", 0, 128), r("BD"), r("I"), r("RM")
     IND = r("BD", 0, 128, 16)
     fill(r("ZERO"), 0.0); fill(r("ONES"), 1.0)
     iota(PI, [[1, 1]], 0, 1)
@@ -299,23 +365,28 @@ def rank_program(g, core, T, topo):
     ts(k_i, PI, 15, A.bitwise_and); ts(g_i, PI, 4, A.arith_shift_right); ts(p31, PI, 31, A.bitwise_and)
     tc(r("cf", 0, 3), r("ci", 1, 4))
     ts(r("REP"), r("REPI"), P31, A.is_equal)
-    act(r("C2048"), I_, scale=2048.0); act(S256, BD_, scale=256.0); act(r("IND128"), IND, scale=128.0)
+    for n, x in (("I16", 16.0), ("C160", 160.0 * 4096), ("N4096", -4096.0), ("C160K", 160.0 * 2 ** 23), ("N23", -2.0 ** 23), ("I32", 32.0), ("I64", 64.0), ("I128", 128.0)):
+        times(r(n), I_, x)
+    act(r("BD16"), BD_, scale=0.0625); act(r("IND128"), IND, scale=128.0)
     tc(r("wlb"), r("wl0", 0, 16, 8))
     mm([(r("B6", 2 * s, 2 * s + 2, p0=64 * h, p1=64 * h + 64), cut(I_, 64 * s, 64 * s + 64), r("wlb"), True, True) for s in range(2) for h in range(2)])
-    act(r("WL"), r("B6", 0, 4)); act(r("WW"), r("B6", 0, 4, 2), scale=2.0)
+    act(r("WL"), r("B6", 0, 4))
+    for j, x in enumerate((32.0, 2.0, 4096.0)):
+        act(r("WW", 2 * j, 2 * j + 2), r("B6", 0, 4, 2), scale=x)
     for s in range(2):
-        act(r("W2%d" % s), BD_, scale=r("WW", s, s + 1))
+        for j, n in enumerate(("W16", "W2", "W2K")):
+            times(r(n + str(s)), BD_, r("WW", 2 * j + s, 2 * j + s + 1))
     LF = r("WL", 1, 4, 2); act(r("TOP"), LF)
-    act(KS, KF, F.Identity, 1.0, 256.0)
+    act(KS, KF, scale=-0.0625); act(r("NK16"), I_, scale=KS)
     for m in range(3):
         sc = float(1 << (5 + m))
-        act(NKC[m], KF, F.Identity, 613 * m * sc - 8388608.0, 37.0 * sc)
+        act(NKC[m], KF, F.Identity, (613 * m + 2048) * sc + 2048.0 - 8388608.0, 37.0 * sc)
 
     def late_constants():
-        for n, x in (("NI16", -0.0625), ("I32", 32.0), ("I16", 16.0), ("NI", -1.0), ("NHALF", -0.5)):
-            act(r(n), I_, scale=x)
+        for n, x in (("NI16", -0.0625), ("N65536", -65536.0), ("NI", -1.0), ("HALF", 0.5), ("NQ", -0.25)):
+            times(r(n), I_, x)
         iota(r("C15"), [[0, 8], [1, 16]], 0, 0); ts(RM, r("C15"), KF, A.is_equal)
-        act(r("CCB"), IND, scale=8192.0); act(r("NEG"), RM, F.Identity, -HUGE, HUGE)
+        act(r("CCB"), IND, scale=4096.0); act(r("NEG"), RM, F.Identity, -HUGE, HUGE); act(r("OFF8"), cut(ONES, 0, 8), scale=512.0)
         fill(r("E0"), 0.0)
         iota(r("E0", p0=64, p1=65), [[16, 256]], 0, 0); iota(r("KL", 0, 256, p0=96, p1=97), [[1, 16], [-1, 16]], 0, 0)
         ts(r("KL", 256, 512, p0=96, p1=97), r("KL", 0, 256, p0=96, p1=97), 15, A.bitwise_and); tc(r("E0", p0=96, p1=97), r("KL", 256, 512, p0=96, p1=97))
@@ -327,7 +398,7 @@ def rank_program(g, core, T, topo):
             fill(r("G%d" % s, p0=64), 1.0)
         _add(gr, "G", 0.17 + 512 * CY, lambda: g.affine_select(T.SH[:], ap(r("ZERO")), [[-16, 8], [0, 2], [-1, 16]], A.not_equal, 1.0, 0, 1), regs(r("ZERO")), regs(r("SH")))
         for d in range(1, 16):
-            act(r("SHF", 128 * d, 128 * d + 128), r("SH", last=slice(d, d + 16)))
+            times(r("SHF", 128 * d, 128 * d + 128), r("SH", last=slice(d, d + 16)), 1.0)
         iota(r("CI"), [[1, 176]], 0, 0)
         for h in range(2):
             act(cut(LB, 7, 8, p0=64 * h, p1=64 * h + 64), cut(KF, 0, 1, p0=64 * h, p1=64 * h + 64), F.Identity, 48.0 + 64 * h)
@@ -346,15 +417,15 @@ def rank_program(g, core, T, topo):
             act(r("TM", TMW * j, TMW * j + 256), r("B7", 256 * j, 256 * j + 256))
         for h in range(2):
             pick(r("DUP%d" % h), ZERO, [[0, 2], [-1, 64]], A.not_equal, 1.0, -64 * h, 1)
-            act(r("ND%d" % h), r("DUP%d" % h), scale=-1.0)
+            times(r("ND%d" % h), r("DUP%d" % h), -1.0)
         for t in range(V):
             iota(r("RO", t, t + 1), [[1, 1]], 0, 1 << (t + 2))
         ts(r("RO", 8, 13), r("RO", 0, 5), 127, A.bitwise_and); ts(r("RO", 16, 21), r("RO", 0, 5), 7, A.arith_shift_right)
         tt(r("RF"), r("RO", 8, 13), r("RO", 16, 21), A.add)
         act(r("RF"), r("RF"), F.Identity, -60.0)
-        act(r("WJ"), r("RF"), F.Exp, None, -math.log(3.0), extra=1.3); act(r("TH"), r("WJ"), scale=2.2)
+        act(r("WJ"), r("RF"), F.Exp, None, -math.log(3.0), extra=1.3); act(r("TH"), r("WJ"), scale=-2.2)
         for t in range(V):
-            act(r("RW"), RM, scale=r("WJ", t, t + 1))
+            times(r("RW"), RM, r("WJ", t, t + 1))
             mm(group(r("B7", 8 * t, 8 * t + 8), (r("RW"), IND)))
         act(r("WT"), r("B7", 0, 40))
         iota(r("TRI"), [[0, 2], [16, 8]], 2048, 0); act(r("TRC"), r("TRI"), F.Identity, KF)
@@ -373,33 +444,37 @@ def rank_program(g, core, T, topo):
     def numbers(s, t):
         v = view(s); M = BM[s]; K = BK[s]
         Z, N = r("Z%d%d" % (t, s)), r("N%d%d" % (t, s))
-        n, pq = r(M, 256, 384), r(M, 384, 512)
-        mm(group(n, (I_, N), (r("C2048"), ONES)))
+        U, v1, x = r(M, 0, 128), r(M, 128, 256), r(M, 256, 384)
+        mm(group(U, (r("I16"), ONES), (v("W16"), Z)))
+        act(v("HB"), U, F.Identity, 159.5, 2.0 ** -16)
+        mm(group(v1, (r("C160"), ONES), (I_, ONES), (v("W2"), Z), (r("N4096"), v("HB"))))
+        mm(group(r(K, 0, 128), (Z, I_)))
         for m in range(3):
-            act(v("NK", m * H, m * H + H), n, F.Identity, NKC[m], float(1 << (5 + m)))
-        mm(group(r(M, 0, 128), (v("W2"), Z)) + turned(r(M, 128, 256), (S256, Z, False)))
-        mm(group(r(K, 0, 128), (Z, I_))); act(v("NZ"), r(K, 0, 128), scale=-1.0)
+            mm(group(r(K, m * H + H, m * H + 2 * H), (r("C160K"), ONES), (v("W2K"), Z), (r("N23"), v("HB")), (r("I%d" % (32 << m)), N)))
+        for m in range(3):
+            act(v("NK", m * H, m * H + H), r(K, m * H + H, m * H + 2 * H), F.Identity, NKC[m])
+        act(v("NZ"), r(K, 0, 128), scale=-1.0)
         nz = max(NV)
         for k in range(16):
             o = v("ZR", k, 16 * nz, 16); z = cut(Z, 0, nz); wr = [("ZR%d_%d" % (s, k), 0, 1)]
-            if t == 0:
+            if t == 0 and k < ZS:
                 _add(gr, "S", FS + max(64, nz) * CY, lambda o=o, z=z: sca.activation(out=ap(o), in_=ap(z), func=F.Identity), regs(z), wr)
-            elif k < ZG:
+            elif k < ZG and t > 0:
                 _add(gr, "G", 0.17 + 2 * nz * CY, lambda o=o, z=z: g.affine_select(ap(o), ap(z), [[0, nz]], A.is_ge, 0.0, 0, 0), regs(z), wr)
             else:
                 _add(gr, "V", FV + max(64, nz / 2) * CY, lambda o=o, z=z: vec.tensor_copy(out=ap(o), in_=ap(z)), regs(z), wr)
-        ts(v("VI"), r(M, 0, 256), 1.0, A.add); ts(v("VS"), v("VI"), 4095, A.bitwise_and)
-        tt(pq, n, v("VS", 0, 128), A.mult)
+        tt(U, v1, N, A.mult)
         for m in range(3):
             o = (m * H, m * H + H)
-            tt(v("QI", *o), pq, v("NK", *o), A.add)
-        for m in range(3):
-            o = (m * H, m * H + H)
+            tt(v("QI", *o), U, v("NK", *o), A.add)
             ts(v("QS", *o), v("QI", *o), 5 + m, A.arith_shift_right, 4095, A.bitwise_and)
-        tc(v("OF"), v("QS")); ts(v("TB"), v("OF"), -2048.0, A.add)
-        mm([x for m in range(3) for x in group(r(M, m * H, m * H + H), (v("TB", m * H, m * H + H), I_))] + group(r(M, 384, 512), (N, I_)))
-        ts(v("MS"), v("VS", 128, 256), KS, A.is_equal)
-        ts(v("U16"), v("VS", 64, 128), -2048.0, A.add)
+        for o in OFP:
+            tc(v("OF", *o), v("QS", *o))
+        ts(v("TB"), v("OF"), -2048.0, A.add)
+        mm(turned(x, (r("BD16"), Z, False), (r("NK16"), ONES, True)))
+        act(v("XR"), x, F.Identity, 12582912.0); act(v("XS"), v("XR"), F.Identity, -12582912.0)
+        tt(v("MS"), x, v("XS"), A.is_equal)
+        mm([y for m in range(3) for y in group(r(M, m * H, m * H + H), (v("TB", m * H, m * H + H), I_))] + group(r(M, 384, 512), (N, I_)))
         act(v("ZQ"), Z, F.Identity, 159.625, 0.25)
 
     turn = [0]
@@ -425,11 +500,15 @@ def rank_program(g, core, T, topo):
             for k0 in range(0, 16, KW):
                 mm([x for k in range(k0, k0 + KW) for x in group(r(BK[s], m * H + k, m * H + H, 16),
                     (v("D", o + k, o + 16 * H, 16), r("IND128")), (v("L", o + k, o + 16 * H, 16), IND))], (m * H + 8 * k0, m * H + 8 * (k0 + KW)))
+            blk = gr["bulk"]; gr["bulk"] = False
+            if m == 0:
+                act(v("K0"), r(BK[s], 0, 128))
+            if m == 1:
+                tt(v("K1"), v("K0"), r(BK[s], 128, 256), A.min)
+            gr["bulk"] = blk
 
     def choose(s, t):
         v = view(s); B = BK[s]; N = r("N%d%d" % (t, s))
-        act(v("K0"), r(B, 0, 128))
-        tt(v("K1"), v("K0"), r(B, 128, 256), A.min)
         tt(v("KI"), v("K1"), r(B, 256, 384), A.min)
         ts(v("YI"), v("KI"), 112, A.bitwise_and)
         ts(v("OK"), v("KI"), 16, A.bitwise_and)
@@ -463,8 +542,8 @@ def rank_program(g, core, T, topo):
             act(v("TAB", 512 * x, 512 * x + 512), r(BT[x]))
         for j in range(2):
             act(v("MM", 64 * j, 64 * j + 64), r("TM", TMW * j, TMW * j + TMW), ix=v("LO", 0, 4))
-        mm(group(r(K, 0, 64), (r("I32"), J), (r("I16"), v("U16"))))
-        act(v("JA"), r(K, 0, 64), F.Identity, 98288.0 - 8388608.0)
+        mm(group(r(K, 0, 64), (r("I32"), J), (v("W16"), r("Z%d%d" % (t, s), 64, 128)), (r("N65536"), v("HB", 64, 128))))
+        act(v("JA"), r(K, 0, 64), F.Identity, 65536.0 * 161 - 8388608.0)
         tt(r(K, 64, 128), v("NF", 64, 128), v("NF", 0, 64), A.mult)
         tt(v("JQ"), r(K, 64, 128), v("JA"), A.add)
         ts(v("JT"), v("JQ"), 5, A.arith_shift_right, 4095, A.bitwise_and)
@@ -480,7 +559,6 @@ def rank_program(g, core, T, topo):
         x, y = r("S%s%d%d" % (name, t, s)), r("%s%d%d" % (name, t + 1, s))
         rid, pid, _ = topo.addr(nxt)
         en = topo.engines(core, nxt)
-        en = en[:len(en) // 2] if name == "N" else en[len(en) // 2:]
         msk = sum(1 << e for e in en)
         rs = "a%s%d%d" % (name.lower(), t + 1, s)
         NE.append(len(en))
@@ -505,11 +583,11 @@ def rank_program(g, core, T, topo):
         mm(group(EL, (v("EM"), IND)))
         ts(v("YO"), EL, 2048.0, A.add); act(v("EL"), EL)
         act(v("YB"), v("X", 0, W), ix=v("YO"))
-        mm(turned(r(K, 0, 128), (I_, Z, False), (r("NHALF"), ONES, True), (I_, v("YB"), True)))
-        act(v("ZH"), r(K, 0, 128), F.Identity, 12582912.0, 0.5)
+        mm(turned(r(K, 0, 128), (r("HALF"), Z, False), (r("NQ"), ONES, True), (r("HALF"), v("YB"), True)))
         if t < V - 1:
-            act(r("SZ%d%d" % (t, s)), v("ZH"), F.Identity, -12582912.0); send("Z", s, t)
+            ts(r("SZ%d%d" % (t, s)), r(K, 0, 128), 12582912.0, A.add, -12582912.0, A.add); send("Z", s, t)
         else:
+            act(v("ZH"), r(K, 0, 128), F.Identity, 12582912.0)
             for q in range(2):
                 act(v("YZ", 64 * q, 64 * q + 64), v("ZH", q, 128, 2), F.Identity, -12582912.0)
             for h in range(2):
@@ -519,9 +597,9 @@ def rank_program(g, core, T, topo):
         for c in range(8):
             ts(v("ED", H * c, H * c + H), v("EC"), v("EL", c, c + 1), A.is_equal, r("WT", 8 * t + c, 8 * t + c + 1), A.mult)
         mm(group(ET, (I_, r("NEG")), *[(v("ED", H * c, H * c + H), BD_) for c in range(8)]))
-        ts(v("DT"), ET, r("TH", t, t + 1), A.is_ge)
+        act(v("DT"), ET, F.Sign, r("TH", t, t + 1))
         mm([x for h in range(2) for p in range(2) for x in group(r(R, 272 + 8 * h, 280 + 8 * h, p0=64 * p, p1=64 * p + 64),
-            (v("EM", 64 * h, 64 * h + 64), IND), (v("DT", 64 * h, 64 * h + 64), r("CCB")))])
+            (cut(ONES, 0, 64), r("OFF8")), (v("EM", 64 * h, 64 * h + 64), IND), (v("DT", 64 * h, 64 * h + 64), r("CCB")))])
         tt(v("T1"), r(R, 272, 288), r("TRC"), A.min)
         ts(v("SO"), v("T1"), 2048.0, A.add)
         for h in (1, 0):
@@ -543,7 +621,7 @@ def rank_program(g, core, T, topo):
     late_constants()
     for t in range(V):
         for s in range(2):
-            gr["bulk"] = True
+            gr["bulk"] = 2 * t + s + 1
             scores(s, t)
             gr["bulk"] = False
             choose(s, t)
@@ -556,7 +634,9 @@ def rank_program(g, core, T, topo):
                 numbers(s, t + 1)
 
     ops = gr["ops"]
-    seq = _order(ops)
+    if not ORDER:
+        ORDER.extend(_order(ops))
+    seq, fin = ORDER
     eng = {"V": vec, "S": sca, "P": ten, "G": g, "Y": syn}
     cs = {"V": "cV", "S": "cS", "P": "cP", "G": "cG"}
     count = {q: 0 for q in eng}
@@ -572,7 +652,7 @@ def rank_program(g, core, T, topo):
             k = ops[d].get("key")
             if k is not None and S.get(k[0], 0) < k[1] and want.get(k[0], (0, None))[0] < k[1]:
                 want[k[0]] = (k[1], d)
-        for nm, (val, d) in sorted(want.items(), key=lambda kv: -ops[kv[1][1]].get("fin", 0)):
+        for nm, (val, d) in sorted(want.items(), key=lambda kv: -fin[kv[1][1]]):
             if S.get(nm, 0) >= val:
                 continue
             eng[q].wait_ge(T.sem[nm], val)

@@ -4,12 +4,21 @@ from concourse.mybir import AluOpType as A, AxisListType, ActivationFunctionType
 
 W, C, V = 4096, 256, 5
 H = 128
-NV = [64,64,64]
+NV = [96,64,64]
+NV1 = [64,64,64]
+NVA = [64,64,64]
+NVB = [64,64,64]
+NVY = [64,64,64]
+NVZ = [64,64,64]
+SW = 32
+CH = [64,0,96,32]
 VW = 32
-LW = 64
+LW = 32
 OFP = [[0,128],[128,384]]
-ZS = 4
-CV = 3
+ZN = 64
+ZM = 0
+ON_S = "EC0,EL0,EL1,FC1,G0,HB0,HB1,JA1,JC1,K00,K01,NF0,NF1,NK0,NK1,NZ0,NZ1,OF0,OG0,SN0,SN1,SO1,XS0,YO0,YO1,ZQ0,ZQ1"
+CV = 1000
 KW = 4
 ZG = 16
 TMW = 1024
@@ -38,12 +47,12 @@ def _declare():
     b, h, f, i, u = "bfloat16", "float16", "float32", "int32", "uint16"
     _sb("wl0", 16, i); _sb("wlb", 2, b); _sb("WL", 4, f); _sb("WW", 6, f)
     _sb("ci", 16, i); _sb("cf", 16, f); _sb("ONES", 256, b); _sb("ZERO", 256, b)
-    for n in ("BD", "I", "BD16", "NK16", "C160", "C160K", "N4096", "N23", "N65536", "I16", "I32", "I64", "I128", "HALF", "NQ", "NI", "NI16",
+    for n in ("BD", "I", "BD16", "NK16", "C160", "N4096", "N65536", "C1040", "I2080", "I2048", "HALF", "NQ", "NI", "NI16",
               "DUP0", "DUP1", "ND0", "ND1", "RM", "NEG", "C15", "RW"):
         _sb(n, 128, b)
-    _sb("IND128", 8, b); _sb("CCB", 8, b); _sb("OFF8", 8, b); _sb("REP", 512, b); _sb("REPI", 512, b); _sb("GA", 3 * 512, b)
+    _sb("IND128", 8, b); _sb("CCB", 8, b); _sb("OFF8", 8, b); _sb("REP", 512, b); _sb("REPI", 512, b);
     _sb("SH", [8, 32], b); _sb("SHF", 2048, b); _sb("E0", 256, b); _sb("KL", 512, i); _sb("EE", 512, b); _sb("CI", 176, b); _sb("LA", 176, b)
-    _sb("CB", 96, b); _sb("CM", 32, b); _sb("CADD", 8, b); _sb("RL", 2, u); _sb("RLI", 4, i); _sb("T16", 512, b); _sb("TM", 2 * TMW, b)
+    _sb("CB", 96, b); _sb("CM", 32, b); _sb("CADD", 4, b); _sb("RL", 2, u); _sb("RLI", 4, i); _sb("T16", 512, b); _sb("TM", 2 * TMW, b)
     _sb("RO", 24, i); _sb("RF", 5, f); _sb("WJ", 5, f); _sb("TH", 5, f); _sb("WT", 40, f)
     _sb("TRI", 16, f); _sb("TRC", 16, f); _sb("EI", 4, i); _sb("CN", 8, f); _sb("TOP", 2, f)
     for k in range(2):
@@ -53,13 +62,13 @@ def _declare():
             _sb("Z%d%d" % (t, k), H, b); _sb("N%d%d" % (t, k), H, h)
         for t in range(V - 1):
             _sb("SN%d%d" % (t, k), H, h); _sb("SZ%d%d" % (t, k), H, b)
-        _sb("HB" + s, H, b); _sb("XR" + s, H, f); _sb("XS" + s, H, b); _sb("W16" + s, 128, b); _sb("W2K" + s, 128, b); _sb("MS" + s, H, b); _sb("NK" + s, 3 * H, f)
+        _sb("HB" + s, H, b); _sb("XS" + s, H, h); _sb("W16" + s, 128, b); _sb("NF" + s, H, f); _sb("MS" + s, H, b); _sb("NK" + s, 3 * H, f)
         _sb("QI" + s, 3 * H, i); _sb("QS" + s, 3 * H, i); _sb("TB" + s, 3 * H, h); _sb("OF" + s, 3 * H, u)
-        _sb("ZR" + s, 16 * max(NV), b); _sb("ZQ" + s, H, b); _sb("NZ" + s, H, b)
+        _sb("ZQ" + s, H, b); _sb("NZ" + s, H, b); _sb("ZR" + s, 16 * ZN, b)
         _sb("D" + s, 48 * H, b); _sb("L" + s, 48 * H, b)
         _sb("K0" + s, H, f); _sb("K1" + s, H, f); _sb("KI" + s, H, i); _sb("YI" + s, H, i); _sb("OK" + s, H, i)
         _sb("MK" + s, 3 * H, b); _sb("PR" + s, 4 * H, h)
-        _sb("FC" + s, H, h); _sb("NF" + s, H, f); _sb("G" + s, 256, h); _sb("R" + s, 4, i); _sb("W8" + s, 8, i)
+        _sb("FC" + s, H, h); _sb("G" + s, 256, h); _sb("R" + s, 4, i); _sb("W8" + s, 8, i)
         _sb("RR" + s, 32, b); _sb("LO" + s, 8, u); _sb("MT" + s, 4, b); _sb("TAB" + s, 1024, f); _sb("MM" + s, H, b)
         _sb("JA" + s, 64, f); _sb("JQ" + s, 64, i); _sb("JT" + s, 64, i); _sb("PA" + s, H, h); _sb("PB" + s, H, h)
         _sb("FS" + s, H, h); _sb("EM" + s, H, h); _sb("EC" + s, H, h); _sb("EL" + s, 8, f); _sb("YO" + s, 8, u); _sb("YB" + s, H, b)
@@ -87,7 +96,7 @@ FV = 0.05
 FS = 0.06
 SLACK = 0.04
 LEAD = 0.0
-ROUNDS = 4
+ROUNDS = 3
 PERIODS = []
 SPANS = [10,13,16]
 ORDER = []
@@ -292,6 +301,14 @@ def rank_program(g, core, T, topo):
         c = 0.065 + cnt(o) * GATHER * CY if ix else FS + max(64, cnt(o)) * CY
         _add(gr, "S", c + extra, fn, regs(i, bias, scale, ix), regs(o, acc))
 
+    def aff(name, o, i, mul=1.0, add=0.0):
+        if name in ON_S.split(","):
+            act(o, i, F.Identity, add if add else None, mul if mul != 1.0 else None)
+        elif mul == 1.0 and add == 0.0:
+            tc(o, i)
+        else:
+            ts(o, i, mul, A.mult, add, A.add)
+
     def mm(lst, span=None):
         def fn():
             x = None
@@ -365,26 +382,26 @@ def rank_program(g, core, T, topo):
     ts(k_i, PI, 15, A.bitwise_and); ts(g_i, PI, 4, A.arith_shift_right); ts(p31, PI, 31, A.bitwise_and)
     tc(r("cf", 0, 3), r("ci", 1, 4))
     ts(r("REP"), r("REPI"), P31, A.is_equal)
-    for n, x in (("I16", 16.0), ("C160", 160.0 * 4096), ("N4096", -4096.0), ("C160K", 160.0 * 2 ** 23), ("N23", -2.0 ** 23), ("I32", 32.0), ("I64", 64.0), ("I128", 128.0)):
+    for n, x in (("C160", 160.0 * 4096), ("N4096", -4096.0), ("C1040", 1040.0)):
         times(r(n), I_, x)
     act(r("BD16"), BD_, scale=0.0625); act(r("IND128"), IND, scale=128.0)
     tc(r("wlb"), r("wl0", 0, 16, 8))
     mm([(r("B6", 2 * s, 2 * s + 2, p0=64 * h, p1=64 * h + 64), cut(I_, 64 * s, 64 * s + 64), r("wlb"), True, True) for s in range(2) for h in range(2)])
     act(r("WL"), r("B6", 0, 4))
-    for j, x in enumerate((32.0, 2.0, 4096.0)):
+    for j, x in enumerate((32.0, 2.0)):
         act(r("WW", 2 * j, 2 * j + 2), r("B6", 0, 4, 2), scale=x)
     for s in range(2):
-        for j, n in enumerate(("W16", "W2", "W2K")):
+        for j, n in enumerate(("W16", "W2")):
             times(r(n + str(s)), BD_, r("WW", 2 * j + s, 2 * j + s + 1))
     LF = r("WL", 1, 4, 2); act(r("TOP"), LF)
     act(KS, KF, scale=-0.0625); act(r("NK16"), I_, scale=KS)
     for m in range(3):
         sc = float(1 << (5 + m))
-        act(NKC[m], KF, F.Identity, (613 * m + 2048) * sc + 2048.0 - 8388608.0, 37.0 * sc)
+        act(NKC[m], KF, F.Identity, (613 * m + 2048) * sc - 8388608.0, 37.0 * sc)
 
     def late_constants():
-        for n, x in (("NI16", -0.0625), ("N65536", -65536.0), ("NI", -1.0), ("HALF", 0.5), ("NQ", -0.25)):
-            times(r(n), I_, x)
+        for n, x in (("NI16", -0.0625), ("N65536", -65536.0), ("I2080", 2080.0), ("I2048", 2048.0), ("NI", -1.0), ("HALF", 0.5), ("NQ", -0.25)):
+            pick(r(n), ZERO, [[-1, 128]], A.not_equal, x, 0, 1)
         iota(r("C15"), [[0, 8], [1, 16]], 0, 0); ts(RM, r("C15"), KF, A.is_equal)
         act(r("CCB"), IND, scale=4096.0); act(r("NEG"), RM, F.Identity, -HUGE, HUGE); act(r("OFF8"), cut(ONES, 0, 8), scale=512.0)
         fill(r("E0"), 0.0)
@@ -398,15 +415,15 @@ def rank_program(g, core, T, topo):
             fill(r("G%d" % s, p0=64), 1.0)
         _add(gr, "G", 0.17 + 512 * CY, lambda: g.affine_select(T.SH[:], ap(r("ZERO")), [[-16, 8], [0, 2], [-1, 16]], A.not_equal, 1.0, 0, 1), regs(r("ZERO")), regs(r("SH")))
         for d in range(1, 16):
-            times(r("SHF", 128 * d, 128 * d + 128), r("SH", last=slice(d, d + 16)), 1.0)
+            pick(r("SHF", 128 * d, 128 * d + 128), r("SH", last=slice(d, d + 16)), [[0, 8], [0, 16]], A.is_ge, 0.0, 0, 0)
         iota(r("CI"), [[1, 176]], 0, 0)
         for h in range(2):
             act(cut(LB, 7, 8, p0=64 * h, p1=64 * h + 64), cut(KF, 0, 1, p0=64 * h, p1=64 * h + 64), F.Identity, 48.0 + 64 * h)
             act(cut(B4, 8, 9, p0=64 * h, p1=64 * h + 64), cut(GF, 1, 2, p0=64 * h, p1=64 * h + 64), F.Identity, -4.0 * h)
         ts(r("LA"), r("CI"), LB, A.is_equal)
-        iota(r("CB", 0, 32), [[0, 8], [1, 4]], 0, 0); iota(r("CB", 32, 64), [[0, 4], [63, 2], [0, 4]], 1, 0)
+        iota(r("CB", 0, 32), [[0, 8], [1, 4]], 0, 0); iota(r("CB", 32, 64), [[63, 2], [0, 16]], 1, 0)
         ts(r("CB", 64, 96), r("CB", 0, 32), B4, A.is_equal); tt(r("CM"), r("CB", 64, 96), r("CB", 32, 64), A.mult)
-        act(r("CADD", 0, 4), cut(ZERO, 0, 4)); act(r("CADD", 4, 8), r("CI", 0, 4), F.Identity, KF, 16.0)
+        act(r("CADD"), r("CI", 0, 4), F.Identity, KF, 16.0)
         ts(r("RLI", 0, 2), r("CI", 0, 2), 16.0, A.mult, KF, A.add); ts(r("RLI", 2, 4), r("RLI", 0, 2), 2, A.arith_shift_right); tc(r("RL"), r("RLI", 2, 4))
         fill(r("TM"), 0.0)
         x, y, one = r("T16", 0, 256, p1=32), r("T16", 256, 512, p1=32), r("ONES", p1=32)
@@ -417,7 +434,7 @@ def rank_program(g, core, T, topo):
             act(r("TM", TMW * j, TMW * j + 256), r("B7", 256 * j, 256 * j + 256))
         for h in range(2):
             pick(r("DUP%d" % h), ZERO, [[0, 2], [-1, 64]], A.not_equal, 1.0, -64 * h, 1)
-            times(r("ND%d" % h), r("DUP%d" % h), -1.0)
+            pick(r("ND%d" % h), ZERO, [[0, 2], [-1, 64]], A.not_equal, -1.0, -64 * h, 1)
         for t in range(V):
             iota(r("RO", t, t + 1), [[1, 1]], 0, 1 << (t + 2))
         ts(r("RO", 8, 13), r("RO", 0, 5), 127, A.bitwise_and); ts(r("RO", 16, 21), r("RO", 0, 5), 7, A.arith_shift_right)
@@ -441,59 +458,65 @@ def rank_program(g, core, T, topo):
 
     BK, BM, BD, BT = ["B0", "B1"], ["B2", "B3"], ["B4", "B5"], ["B6", "B7"]
 
+    def share(s, t):
+        return [NVA, NVB][s] if t == 0 else [NVY, NVZ][s] if t == V - 1 else [NV, NV1][s]
+
     def numbers(s, t):
         v = view(s); M = BM[s]; K = BK[s]
         Z, N = r("Z%d%d" % (t, s)), r("N%d%d" % (t, s))
         U, v1, x = r(M, 0, 128), r(M, 128, 256), r(M, 256, 384)
-        mm(group(U, (r("I16"), ONES), (v("W16"), Z)))
-        act(v("HB"), U, F.Identity, 159.5, 2.0 ** -16)
+        mm(group(U, (v("W16"), Z)))
+        aff("HB%d" % s, v("HB"), U, 2.0 ** -16, 159.5 + 2.0 ** -12)
         mm(group(v1, (r("C160"), ONES), (I_, ONES), (v("W2"), Z), (r("N4096"), v("HB"))))
         mm(group(r(K, 0, 128), (Z, I_)))
+        aff("NF%d" % s, v("NF"), N, add=2048.0)
         for m in range(3):
-            mm(group(r(K, m * H + H, m * H + 2 * H), (r("C160K"), ONES), (v("W2K"), Z), (r("N23"), v("HB")), (r("I%d" % (32 << m)), N)))
-        for m in range(3):
-            act(v("NK", m * H, m * H + H), r(K, m * H + H, m * H + 2 * H), F.Identity, NKC[m])
-        act(v("NZ"), r(K, 0, 128), scale=-1.0)
-        nz = max(NV)
-        for k in range(16):
-            o = v("ZR", k, 16 * nz, 16); z = cut(Z, 0, nz); wr = [("ZR%d_%d" % (s, k), 0, 1)]
-            if t == 0 and k < ZS:
-                _add(gr, "S", FS + max(64, nz) * CY, lambda o=o, z=z: sca.activation(out=ap(o), in_=ap(z), func=F.Identity), regs(z), wr)
-            elif k < ZG and t > 0:
-                _add(gr, "G", 0.17 + 2 * nz * CY, lambda o=o, z=z: g.affine_select(ap(o), ap(z), [[0, nz]], A.is_ge, 0.0, 0, 0), regs(z), wr)
+            aff("NK%d" % s, v("NK", m * H, m * H + H), N, float(32 << m), NKC[m])
+        aff("NZ%d" % s, v("NZ"), r(K, 0, 128), -1.0)
+        for k in range(16 if t > 0 else 0):
+            o = v("ZR", k, 16 * ZN, 16); z = cut(Z, 0, ZN); wr = [("ZR%d_%d" % (s, k), 0, 1)]
+            if k >= ZG:
+                _add(gr, "S", FS + max(64, ZN) * CY, lambda o=o, z=z: sca.activation(out=ap(o), in_=ap(z), func=F.Identity), regs(z), wr)
             else:
-                _add(gr, "V", FV + max(64, nz / 2) * CY, lambda o=o, z=z: vec.tensor_copy(out=ap(o), in_=ap(z)), regs(z), wr)
-        tt(U, v1, N, A.mult)
+                _add(gr, "G", 0.17 + 2 * ZN * CY, lambda o=o, z=z: g.affine_select(ap(o), ap(z), [[0, ZN]], A.is_ge, 0.0, 0, 0), regs(z), wr)
+        tt(U, v1, v("NF"), A.mult)
         for m in range(3):
             o = (m * H, m * H + H)
             tt(v("QI", *o), U, v("NK", *o), A.add)
             ts(v("QS", *o), v("QI", *o), 5 + m, A.arith_shift_right, 4095, A.bitwise_and)
         for o in OFP:
-            tc(v("OF", *o), v("QS", *o))
-        ts(v("TB"), v("OF"), -2048.0, A.add)
-        mm(turned(x, (r("BD16"), Z, False), (r("NK16"), ONES, True)))
-        act(v("XR"), x, F.Identity, 12582912.0); act(v("XS"), v("XR"), F.Identity, -12582912.0)
+            aff("O%s%d" % ("FG"[o[0] > 0], s), v("OF", *o), v("QS", *o))
+        aff("TB%d" % s, v("TB"), v("QS") if "TB%d" % s in ON_S else v("OF"), add=-2048.0)
+        mm(turned(x, (r("BD16"), Z, False), (r("NK16"), ONES, True), (r("C1040"), ONES, True)))
+        aff("XS%d" % s, v("XS"), x)
         tt(v("MS"), x, v("XS"), A.is_equal)
-        mm([y for m in range(3) for y in group(r(M, m * H, m * H + H), (v("TB", m * H, m * H + H), I_))] + group(r(M, 384, 512), (N, I_)))
-        act(v("ZQ"), Z, F.Identity, 159.625, 0.25)
+        aff("ZQ%d" % s, v("ZQ"), Z, 0.25, 159.625)
 
-    turn = [0]
+    turn = [0, 0]
 
     def scores(s, t):
-        v = view(s); X = v("X", 0, W); zr = [("ZR%d_%d" % (s, k), 0, 1) for k in range(16)]
+        v = view(s); X = v("X", 0, W)
         for m in range(3):
             o = 16 * H * m
-            for a in range(NV[m], H, 32):
+            nv = share(s, t)[m]; zn = min(ZN, nv) if m >= ZM and t > 0 else 0; zr = [("ZR%d_%d" % (s, k), 0, 1) for k in range(16)]
+            calls = [("S", a, min(H, a + SW)) for a in range(nv, H, SW)] + [("V", a, min(nv, a + VW)) for a in range(0, nv, VW)]
+            for q, a, b in calls:
+                d = v("D", o + 16 * a, o + 16 * b); ix = v("OF", m * H + a, m * H + b)
+                if q == "S":
+                    act(d, X, ix=ix)
+                elif b <= zn:
+                    _add(gr, "V", vcost(d, X, ix, 1), lambda a=a, b=b, d=d, ix=ix: vec.tensor_tensor(
+                        out=ap(d), in0=src(X, ix), in1=ap(v("ZR", 16 * a, 16 * b)), op=A.subtract), regs(X, ix) + zr, regs(d))
+                else:
+                    _add(gr, "V", vcost(d, X, ix, 1), lambda d=d, ix=ix: vec.tensor_copy(out=ap(d), in_=src(X, ix)), regs(X, ix), regs(d))
+            for a in CH:
+                if a + 32 <= zn:
+                    d = v("D", o + 16 * a, o + 16 * a + 512); act(d, d, F.Abs)
+                    continue
                 turn[0] += 1
-                ga = r("GA", 512 * (turn[0] % 3), 512 * (turn[0] % 3) + 512); bk = BD[turn[0] & 1]
-                act(ga, X, ix=v("OF", m * H + a, m * H + a + 32))
-                mm(group(r(bk), (v("NZ", p0=a, p1=a + 32), r("REP", p0=a, p1=a + 32)), (I_, ga)))
-                act(v("D", o + 16 * a, o + 16 * a + 512), r(bk), F.Abs)
-            for a in range(0, NV[m], VW):
-                b = min(NV[m], a + VW); d = v("D", o + 16 * a, o + 16 * b); ix = v("OF", m * H + a, m * H + b)
-                _add(gr, "V", vcost(d, X, ix, 1), lambda a=a, b=b, d=d, ix=ix: vec.tensor_tensor(
-                    out=ap(d), in0=src(X, ix), in1=ap(v("ZR", 16 * a, 16 * b)), op=A.subtract), regs(X, ix) + zr, regs(d))
-                act(d, d, F.Abs)
+                d = v("D", o + 16 * a, o + 16 * a + 512); bk = (BD + [BM[s]])[turn[0] % 3]
+                mm(group(r(bk), (v("NZ", p0=a, p1=a + 32), r("REP", p0=a, p1=a + 32)), (I_, d)))
+                act(d, r(bk), F.Abs)
             for a in range(0, H, LW):
                 x = (o + 16 * a, o + 16 * (a + LW))
                 ts(v("L", *x), v("D", *x), r("TOP", s, s + 1), A.is_le, 2.0 * m + 0.4375, A.add)
@@ -502,13 +525,14 @@ def rank_program(g, core, T, topo):
                     (v("D", o + k, o + 16 * H, 16), r("IND128")), (v("L", o + k, o + 16 * H, 16), IND))], (m * H + 8 * k0, m * H + 8 * (k0 + KW)))
             blk = gr["bulk"]; gr["bulk"] = False
             if m == 0:
-                act(v("K0"), r(BK[s], 0, 128))
+                aff("K0%d" % s, v("K0"), r(BK[s], 0, 128))
             if m == 1:
                 tt(v("K1"), v("K0"), r(BK[s], 128, 256), A.min)
             gr["bulk"] = blk
 
     def choose(s, t):
-        v = view(s); B = BK[s]; N = r("N%d%d" % (t, s))
+        v = view(s); B = BK[s]; M = BM[s]; N = r("N%d%d" % (t, s))
+        mm([y for m in range(3) for y in group(r(M, m * H, m * H + H), (v("TB", m * H, m * H + H), I_))] + group(r(M, 384, 512), (N, I_)))
         tt(v("KI"), v("K1"), r(B, 256, 384), A.min)
         ts(v("YI"), v("KI"), 112, A.bitwise_and)
         ts(v("OK"), v("KI"), 16, A.bitwise_and)
@@ -520,19 +544,19 @@ def rank_program(g, core, T, topo):
 
     def meet(s, t):
         v = view(s); NP = r(BK[s], 384, 512); R = BM[s]; K = BK[s]
-        tc(v("FC"), NP)
-        act(v("NF"), NP, F.Identity, 2048.0)
+        aff("FC%d" % s, v("FC"), NP)
         mm([(r(R, 128 * x + 64 * h, 128 * x + 64 * h + 64, p0=32 * j, p1=32 * j + 32), cut(I_, 64 * h + 32 * x, 64 * h + 32 * x + 32),
              v("FC", 64 * j, 64 * j + 64), True, True) for x in range(2) for h in range(2) for j in range(2)])
-        ts(v("G", p1=64), r(R, 0, 256, p1=64), 0.125, A.mult, 1287.5625, A.add)
+        aff("G%d" % s, v("G", p1=64), r(R, 0, 256, p1=64), 0.125, 1287.5625)
         for x in range(2):
             mm([(r(BT[x], 256 * a, 256 * a + 256), v("G", 128 * x, 128 * x + 128, p1=97), r("EE", 256 * a, 256 * a + 256, p1=97), True, True) for a in range(2)])
             for a in range(2):
                 o, i = v("R", 2 * x + a, 2 * x + a + 1), r(BT[x], 256 * a, 256 * a + 256)
                 _add(gr, "V", FV + 256 * CY, lambda o=o, i=i: vec.tensor_reduce(out=ap(o), in_=ap(i), axis=AxisListType.X, op=A.min, apply_absolute_value=True), regs(i), regs(o))
-        ts(v("W8", 0, 8, 2), v("R"), 4, A.arith_shift_right); ts(v("W8", 1, 8, 2), v("R"), 15, A.bitwise_and)
+        ts(v("W8", 0, 4), v("R"), 4, A.arith_shift_right); ts(v("W8", 4, 8), v("R"), 15, A.bitwise_and)
         tt(v("RR"), v("W8"), r("CM"), A.mult, ix=r("RL"))
-        mm(group(r(R, 256, 264), (I_, r("CADD")), *[(r("LA", 48 - 16 * a, 176 - 16 * a), v("RR", 8 * a, 8 * a + 8)) for a in range(4)]))
+        mm([y for x in range(2) for y in group(r(R, 256 + 4 * x, 260 + 4 * x), *([(I_, r("CADD"))] * x + [
+            (r("LA", 48 - 16 * a, 176 - 16 * a), v("RR", 16 * x + 4 * a, 16 * x + 4 * a + 4)) for a in range(4)]))])
         ts(v("LO"), r(R, 256, 264), TMW - 1.0, A.min)
         if t < V - 1:
             act(v("MT"), r(R, 256, 260), F.Sign, 255.5, -1.0)
@@ -542,12 +566,12 @@ def rank_program(g, core, T, topo):
             act(v("TAB", 512 * x, 512 * x + 512), r(BT[x]))
         for j in range(2):
             act(v("MM", 64 * j, 64 * j + 64), r("TM", TMW * j, TMW * j + TMW), ix=v("LO", 0, 4))
-        mm(group(r(K, 0, 64), (r("I32"), J), (v("W16"), r("Z%d%d" % (t, s), 64, 128)), (r("N65536"), v("HB", 64, 128))))
-        act(v("JA"), r(K, 0, 64), F.Identity, 65536.0 * 161 - 8388608.0)
-        tt(r(K, 64, 128), v("NF", 64, 128), v("NF", 0, 64), A.mult)
+        mm(group(r(K, 0, 64), (r("I2080"), J), (r("I2048"), v("FC", 0, 64)), (v("W16"), r("Z%d%d" % (t, s), 64, 128)), (r("N65536"), v("HB", 64, 128))))
+        aff("JA%d" % s, v("JA"), r(K, 0, 64), add=65536.0 * 161 - 4194304.0)
+        tt(r(K, 64, 128), r(K, 448, 512), v("FC", 0, 64), A.mult)
         tt(v("JQ"), r(K, 64, 128), v("JA"), A.add)
         ts(v("JT"), v("JQ"), 5, A.arith_shift_right, 4095, A.bitwise_and)
-        ts(r(K, 64, 128), v("JT"), -2048.0, A.add)
+        aff("JC%d" % s, r(K, 64, 128), v("JT"), add=-2048.0)
         tt(v("PB"), NP, v("MM"), A.mult)
         tt(v("PA", 64, 128), r(K, 64, 128), v("MM", 64, 128), A.mult)
         tt(v("PA", 0, 64), v("TAB"), v("MM", 0, 64), A.mult, ix=v("LO", 4, 8))
@@ -573,15 +597,15 @@ def rank_program(g, core, T, topo):
         tt(v("FS"), F2, v("MS"), A.mult)
         mm(group(ET, (v("FS"), BD_)) + group(EB, (BD_, v("FS"))))
         if t < V - 1:
-            tc(r("SN%d%d" % (t, s)), F2); send("N", s, t)
+            aff("SN%d" % s, r("SN%d%d" % (t, s)), F2); send("N", s, t)
         else:
             for q in range(2):
                 act(v("YF", 64 * q, 64 * q + 64), r(K, 128 + q, 256, 2), F.Identity, 2048.0)
             for h in range(2):
                 store("Y", T.yf[rows, H * h:H * h + H], v("YF", p0=64 * h, p1=64 * h + 64), 32768)
-        tt(v("EM"), ET, RM, A.mult); tc(v("EC"), EB)
+        tt(v("EM"), ET, RM, A.mult); aff("EC%d" % s, v("EC"), EB)
         mm(group(EL, (v("EM"), IND)))
-        ts(v("YO"), EL, 2048.0, A.add); act(v("EL"), EL)
+        aff("YO%d" % s, v("YO"), EL, add=2048.0); aff("EL%d" % s, v("EL"), EL)
         act(v("YB"), v("X", 0, W), ix=v("YO"))
         mm(turned(r(K, 0, 128), (r("HALF"), Z, False), (r("NQ"), ONES, True), (r("HALF"), v("YB"), True)))
         if t < V - 1:
@@ -601,7 +625,7 @@ def rank_program(g, core, T, topo):
         mm([x for h in range(2) for p in range(2) for x in group(r(R, 272 + 8 * h, 280 + 8 * h, p0=64 * p, p1=64 * p + 64),
             (cut(ONES, 0, 64), r("OFF8")), (v("EM", 64 * h, 64 * h + 64), IND), (v("DT", 64 * h, 64 * h + 64), r("CCB")))])
         tt(v("T1"), r(R, 272, 288), r("TRC"), A.min)
-        ts(v("SO"), v("T1"), 2048.0, A.add)
+        aff("SO%d" % s, v("SO"), v("T1"), add=2048.0)
         for h in (1, 0):
             so, nx = v("SO", 8 * h, 8 * h + 8), v("NX", H * h, H * h + H)
             _add(gr, "V", 0.05 + H * SCATTER * CY, lambda so=so, nx=nx: vec.tensor_copy(out=src(v("X"), so), in_=ap(nx)), regs(so, nx), regs(v("X")))
@@ -617,7 +641,10 @@ def rank_program(g, core, T, topo):
         ts(r("EI", 0, 2), r("CN", 0, 2), 0.5, A.mult, 512.0, A.add); ts(r("EI", 2, 4), r("EI", 0, 2), 3, A.bitwise_and)
         tt(r("TOP"), r("EI", 2, 4), LF, A.add)
 
-    numbers(0, 0); numbers(1, 0)
+    numbers(0, 0)
+    for o in gr["ops"]:
+        o["lead"] = 1e3
+    numbers(1, 0)
     late_constants()
     for t in range(V):
         for s in range(2):

import math
import comms_topo
from concourse.mybir import AluOpType as A, AxisListType, ActivationFunctionType as F

W, C, V = 4096, 256, 5
H = 128
NV = [96,64,64]
NV1 = [64,64,64]
NVA = [64,64,64]
NVB = [64,64,64]
NVY = [64,64,64]
NVZ = [64,64,64]
SW = 32
CH = [64,0,96,32]
VW = 32
LW = 32
OFP = [[0,128],[128,384]]
ZN = 64
ZM = 0
ON_S = "EC0,EL0,EL1,FC1,G0,HB0,HB1,JA1,JC1,K00,K01,NF0,NF1,NK0,NK1,NZ0,NZ1,OF0,OG0,SN0,SN1,SO1,XS0,YO0,YO1,ZQ0,ZQ1"
CV = 1000
KW = 4
ZG = 16
TMW = 1024
HUGE = 2.0 ** 98

SCRATCH = {}
BUF = {}
PLACE = {}
POOL = {"bfloat16": ["PoolB", 0], "float16": ["PoolH", 0], "float32": ["PoolF", 0], "int32": ["PoolI", 0], "uint16": ["PoolU", 0]}
SEMAPHORES = ["cV", "cS", "cP", "cG", "loc"]


def _sb(name, cols, dt):
    BUF[name] = ("sbuf", [128] + (cols if isinstance(cols, list) else [cols]), dt)
    if isinstance(cols, list):
        SCRATCH[name] = BUF[name]
        return
    step = 8 if dt in ("float32", "int32") else 16
    p = POOL[dt]
    PLACE[name] = (p[0], p[1])
    p[1] += (cols + step - 1) // step * step
    SCRATCH[p[0]] = ("sbuf", [128, p[1]], dt)


def _declare():
    b, h, f, i, u = "bfloat16", "float16", "float32", "int32", "uint16"
    _sb("wl0", 16, i); _sb("wlb", 2, b); _sb("WL", 4, f); _sb("WW", 6, f)
    _sb("ci", 16, i); _sb("cf", 16, f); _sb("ONES", 256, b); _sb("ZERO", 256, b)
    for n in ("BD", "I", "BD16", "NK16", "C160", "N4096", "N65536", "C1040", "I2080", "I2048", "HALF", "NQ", "NI", "NI16",
              "DUP0", "DUP1", "ND0", "ND1", "RM", "NEG", "C15", "RW"):
        _sb(n, 128, b)
    _sb("IND128", 8, b); _sb("CCB", 8, b); _sb("OFF8", 8, b); _sb("REP", 512, b); _sb("REPI", 512, b);
    _sb("SH", [8, 32], b); _sb("SHF", 2048, b); _sb("E0", 256, b); _sb("KL", 512, i); _sb("EE", 512, b); _sb("CI", 176, b); _sb("LA", 176, b)
    _sb("CB", 96, b); _sb("CM", 32, b); _sb("CADD", 4, b); _sb("RL", 2, u); _sb("RLI", 4, i); _sb("T16", 512, b); _sb("TM", 2 * TMW, b)
    _sb("RO", 24, i); _sb("RF", 5, f); _sb("WJ", 5, f); _sb("TH", 5, f); _sb("WT", 40, f)
    _sb("TRI", 16, f); _sb("TRC", 16, f); _sb("EI", 4, i); _sb("CN", 8, f); _sb("TOP", 2, f)
    for k in range(2):
        s = str(k)
        _sb("X" + s, W + H, b); _sb("vein" + s, H, b); _sb("front" + s, H, i); _sb("W2" + s, 128, b)
        for t in range(V):
            _sb("Z%d%d" % (t, k), H, b); _sb("N%d%d" % (t, k), H, h)
        for t in range(V - 1):
            _sb("SN%d%d" % (t, k), H, h); _sb("SZ%d%d" % (t, k), H, b)
        _sb("HB" + s, H, b); _sb("XS" + s, H, h); _sb("W16" + s, 128, b); _sb("NF" + s, H, f); _sb("MS" + s, H, b); _sb("NK" + s, 3 * H, f)
        _sb("QI" + s, 3 * H, i); _sb("QS" + s, 3 * H, i); _sb("TB" + s, 3 * H, h); _sb("OF" + s, 3 * H, u)
        _sb("ZQ" + s, H, b); _sb("NZ" + s, H, b); _sb("ZR" + s, 16 * ZN, b)
        _sb("D" + s, 48 * H, b); _sb("L" + s, 48 * H, b)
        _sb("K0" + s, H, f); _sb("K1" + s, H, f); _sb("KI" + s, H, i); _sb("YI" + s, H, i); _sb("OK" + s, H, i)
        _sb("MK" + s, 3 * H, b); _sb("PR" + s, 4 * H, h)
        _sb("FC" + s, H, h); _sb("G" + s, 256, h); _sb("R" + s, 4, i); _sb("W8" + s, 8, i)
        _sb("RR" + s, 32, b); _sb("LO" + s, 8, u); _sb("MT" + s, 4, b); _sb("TAB" + s, 1024, f); _sb("MM" + s, H, b)
        _sb("JA" + s, 64, f); _sb("JQ" + s, 64, i); _sb("JT" + s, 64, i); _sb("PA" + s, H, h); _sb("PB" + s, H, h)
        _sb("FS" + s, H, h); _sb("EM" + s, H, h); _sb("EC" + s, H, h); _sb("EL" + s, 8, f); _sb("YO" + s, 8, u); _sb("YB" + s, H, b)
        _sb("ZH" + s, H, f); _sb("NX" + s, 2 * H, b); _sb("ED" + s, 8 * H, b); _sb("DT" + s, H, b); _sb("T1" + s, 16, f); _sb("SO" + s, 16, u)
        _sb("YF" + s, H, f); _sb("YZ" + s, H, b)
    for k in range(8):
        SCRATCH["B%d" % k] = BUF["B%d" % k] = ("psum", [128, 512], "float32")
    for t in range(1, V):
        for k in range(2):
            SEMAPHORES.append("an%d%d" % (t, k)); SEMAPHORES.append("az%d%d" % (t, k))
    for k in range(40):
        SEMAPHORES.append("d%d" % k)


_declare()

CY = 0.00083
PCY = 0.00045
GATHER, SCATTER = 1.56, 3.8
HOLD = {"G": 0.5, "Y": 0.1, "S": 0.1, "A": 0.1}
LAT = 0.2
DFIX = 1.7
DRATE = 250000.0
FV = 0.05
FS = 0.06
SLACK = 0.04
LEAD = 0.0
ROUNDS = 3
PERIODS = []
SPANS = [10,13,16]
ORDER = []


def _add(gr, q, cost, fn, R, Wr, sem=None):
    ops = gr["ops"]; n = len(ops); deps = set()
    if q == "G" and sem is None and ("alone", 0, 1) not in Wr:
        R = R + [("alone", 0, 1)]
    for w, regs in ((False, R), (True, Wr)):
        for (name, a, b) in regs:
            if BUF.get(name, ("",))[0] == "psum":
                ep = gr["bank"].setdefault(name, [None, [], []])
                if ep[0] != q:
                    ep[2] = ep[1]; ep[1] = []; ep[0] = q
                for o in ep[2]:
                    deps.add(o[0])
                for o in ep[1]:
                    if o[1] < b and a < o[2] and (w or o[3]):
                        deps.add(o[0])
                ep[1].append((n, a, b, w))
            else:
                lst = gr["acc"].setdefault(name, [])
                keep = []
                for o in lst:
                    if o[1] < b and a < o[2] and (w or o[3]):
                        deps.add(o[0])
                        if w and a <= o[1] and o[2] <= b and o[0] != n:
                            continue
                    keep.append(o)
                keep.append((n, a, b, w))
                gr["acc"][name] = keep
    deps.discard(n)
    ops.append({"q": q, "cost": cost, "fn": fn, "deps": sorted(deps), "sem": sem, "lead": gr["lead"], "bulk": gr["bulk"], "w": Wr})
    return n


def _order(ops):
    n = len(ops); succ = [[] for _ in ops]; need = [0] * n
    for i, o in enumerate(ops):
        need[i] = len(o["deps"])
        for d in o["deps"]:
            succ[d].append(i)
    pr = [0.0] * n
    for i in range(n - 1, -1, -1):
        pr[i] = ops[i]["cost"] + max([pr[s] + LAT for s in succ[i]] + [ops[i]["lead"]]) + 1e3 * ops[i].get("first", 0)
    for i in range(n):
        if ops[i]["bulk"]:
            pr[i] = -float(i)
    free = {}; fin = [0.0] * n; est = [0.0] * n; out = []
    ready = {}
    for i in range(n):
        if need[i] == 0:
            ready.setdefault(ops[i]["q"], []).append(i)
    while any(ready.values()):
        best = None
        for q, lst in ready.items():
            if not lst:
                continue
            f = free.get(q, 0.0)
            t0 = min(max(f, est[i]) for i in lst)
            c = max((i for i in lst if max(f, est[i]) <= t0 + SLACK), key=lambda i: pr[i])
            st = max(f, est[c])
            if best is None or st < best[0]:
                best = (st, c, q)
        st, c, q = best
        ready[q].remove(c)
        dur = ops[c]["cost"]
        hold = HOLD[q] if ops[c]["sem"] is not None else dur
        free[q] = st + hold if q != "A" else 0.0
        fin[c] = st + dur
        ops[c]["fin"] = fin[c]
        out.append(c)
        for s in succ[c]:
            need[s] -= 1
            est[s] = max(est[s], fin[c] + LAT)
            if need[s] == 0:
                ready.setdefault(ops[s]["q"], []).append(s)
    pred = [o["deps"] for o in ops]
    best = (max(fin), out, fin)
    starts = [fin]
    part = {}
    for i in range(n):
        if ops[i]["bulk"]:
            part.setdefault((ops[i]["bulk"], ops[i]["q"]), []).append(i)
    for period in PERIODS:
        for span in SPANS:
            due = [1e9] * n
            for (k, q), lst in part.items():
                tot = sum(ops[i]["cost"] for i in lst); acc = 0.0
                for i in lst:
                    due[i] = period * k / 2 + span * acc / tot; acc += ops[i]["cost"]
            for i in range(n - 1, -1, -1):
                due[i] = min([due[i], period * (V + 1)] + [due[s] - LAT - ops[i]["cost"] for s in succ[i]]) - 1e3 * ops[i].get("first", 0)
            starts.append(_place(ops, sorted(range(n), key=lambda i: (due[i], i)), pred, False))
    for fin in starts:
        for _ in range(ROUNDS):
            if max(fin) < best[0]:
                best = (max(fin), sorted(range(n), key=lambda i: (fin[i] - ops[i]["cost"], i)), fin)
            back = _place(ops, sorted(range(n), key=lambda i: -fin[i]), succ, True)
            fin = _place(ops, sorted(range(n), key=lambda i: -back[i]), pred, False)
    return best[1], best[2]


def _place(ops, order, before, backward):
    fin = [0.0] * len(ops); busy = {}
    for i in order:
        o = ops[i]; q = o["q"]; dur = o["cost"]
        st = max([fin[d] + LAT for d in before[i]] or [0.0])
        if q != "A":
            hold = HOLD[q] if o["sem"] is not None else dur
            off = dur - hold if backward else 0.0
            lst = busy.setdefault(q, [])
            a = st + off; lo = 0; hi = len(lst)
            while lo < hi:
                mid = (lo + hi) // 2
                if lst[mid][1] <= a:
                    lo = mid + 1
                else:
                    hi = mid
            while lo < len(lst) and lst[lo][0] < a + hold - 1e-9:
                a = max(a, lst[lo][1]); lo += 1
            lst.insert(lo, (a, a + hold))
            st = a - off
        fin[i] = st + dur
    return fin


def rank_program(g, core, T, topo):
    rank = T.rank_of(core)
    if rank is None:
        return
    nxt = T.cores[(rank + 1) % len(T.cores)]
    gr = {"ops": [], "acc": {}, "bank": {}, "lead": 0.0, "bulk": False}
    vec, sca, ten, syn = g.vector, g.scalar, g.tensor, g.sync

    def r(n, a=0, b=None, st=1, p0=0, p1=128, last=None):
        return (n, a, BUF[n][1][1] if b is None else b, st, p0, p1, last)

    def cut(x, a, b, st=1, p0=0, p1=128):
        return r(x[0], a, b, st, p0, p1)

    def ap(x):
        n, a, b, st, p0, p1, last = x
        if last is not None:
            return T[n][p0:p1, a:b, last]
        p, o = PLACE.get(n, (n, 0))
        return T[p][p0:p1, o + a:o + b:st] if st > 1 else T[p][p0:p1, o + a:o + b]

    def reg(x):
        n, a, b = x[:3]
        if n[:-1] in ("X", "vein", "front", "G", "YF", "YZ"):
            return [(n + "_%d" % h, a, b) for h in range(2) if x[4] < 64 * h + 64 and 64 * h < x[5]]
        return [(n, a, b)]

    def regs(*xs):
        return sorted(set(y for x in xs if isinstance(x, tuple) for y in reg(x)))

    def cnt(x):
        return (x[2] - x[1] + x[3] - 1) // x[3] * (1 if x[6] is None else x[6].stop - x[6].start)

    def two(*xs):
        return all(BUF[x[0]][2] in ("bfloat16", "float16", "uint16") for x in xs)

    def sv(s):
        return ap(s) if isinstance(s, tuple) else s

    def src(i, ix):
        return ap(i).indirect(ap(ix)) if ix else ap(i)

    def vcost(o, i, ix, rate):
        return 0.05 + cnt(o) * GATHER * CY if ix else FV + max(64, cnt(o) * rate) * CY

    def tc(o, i):
        _add(gr, "V", vcost(o, i, None, 0.5 if two(o, i) else 1), lambda: vec.tensor_copy(out=ap(o), in_=ap(i)), regs(i), regs(o))

    def ts(o, i, s1, op0, s2=None, op1=None):
        def fn():
            if op1 is None:
                return vec.tensor_scalar(out=ap(o), in0=ap(i), scalar1=sv(s1), scalar2=None, op0=op0)
            return vec.tensor_scalar(out=ap(o), in0=ap(i), scalar1=sv(s1), scalar2=sv(s2), op0=op0, op1=op1)
        _add(gr, "V", vcost(o, i, None, 0.5 if two(o, i) else 1), fn, regs(i, s1, s2), regs(o))

    def tt(o, i, j, op, ix=None):
        ps = "psum" in (BUF[i[0]][0], BUF[j[0]][0])
        _add(gr, "V", vcost(o, i, ix, 1 if ps else 2), lambda: vec.tensor_tensor(out=ap(o), in0=src(i, ix), in1=ap(j), op=op),
             regs(i, j, ix), regs(o))

    def fill(o, x):
        _add(gr, "V", vcost(o, o, None, 0.5 if two(o) else 1), lambda: vec.memset(ap(o), x), [], regs(o))

    def act(o, i, func=F.Identity, bias=None, scale=None, ix=None, acc=None, extra=0.0):
        def fn():
            kw = {}
            if bias is not None:
                kw["bias"] = sv(bias)
            if scale is not None:
                kw["scale"] = sv(scale)
            if acc is not None:
                kw["accum_out"] = ap(acc)
            return sca.activation(out=ap(o), in_=src(i, ix), func=func, **kw)
        c = 0.065 + cnt(o) * GATHER * CY if ix else FS + max(64, cnt(o)) * CY
        _add(gr, "S", c + extra, fn, regs(i, bias, scale, ix), regs(o, acc))

    def aff(name, o, i, mul=1.0, add=0.0):
        if name in ON_S.split(","):
            act(o, i, F.Identity, add if add else None, mul if mul != 1.0 else None)
        elif mul == 1.0 and add == 0.0:
            tc(o, i)
        else:
            ts(o, i, mul, A.mult, add, A.add)

    def mm(lst, span=None):
        def fn():
            x = None
            for o, l, q, s, e in lst:
                x = ten.matmul(ap(o), ap(l), ap(q), s, e)
            return x
        c = sum(max(min(64, cnt(l)), cnt(q)) * PCY for o, l, q, s, e in lst)
        lo, hi = span or (min(x[0][1] for x in lst), max(x[0][2] for x in lst))
        _add(gr, "P", c, fn, regs(*[x[1] for x in lst], *[x[2] for x in lst]), [(lst[0][0][0], lo, hi)])

    def group(o, *pairs):
        return [(o, l, q, k == 0, k == len(pairs) - 1) for k, (l, q) in enumerate(pairs)]

    def turned(o, *pairs):
        out = []
        for p in range(2):
            oo = r(o[0], o[1] + 64 * p, o[1] + 64 * p + 64)
            out += group(oo, *[(l, r(q[0], q[1] + 64 * p, q[1] + 64 * p + 64) if done else r(q[0], q[1] + p, q[2], 2)) for l, q, done in pairs])
        return out

    dn = [0]

    def dma(q, o, i, R, Wr, byts):
        s = "d%d" % dn[0]; dn[0] += 1
        eng = {"Y": syn, "S": sca}[q]
        _add(gr, q, DFIX + byts / DRATE, lambda: eng.dma_start(o(), i()), R, Wr, sem=s)

    def load(q, o, x, byts, first=True, after=()):
        dma(q, lambda: ap(o), lambda: x, regs(*after), regs(o), byts)
        gr["ops"][-1]["first"] = first

    def store(q, x, i, byts):
        dma(q, lambda: x, lambda: ap(i), regs(i), [], byts)

    load("S", r("wl0", 0, 1), T.w[:], 512); load("Y", r("wl0", 8, 9), T.lim[:], 512)
    for s in range(2):
        rows = slice(64 * s, 64 * s + 64)
        for h in range(2):
            load("YS"[h], r("vein%d" % s, p0=64 * h, p1=64 * h + 64), T.vein[rows, H * h:H * h + H], 16384)
            load("YS"[h], r("front%d" % s, p0=64 * h, p1=64 * h + 64), T.front[rows, H * h:H * h + H], 32768)
    for s in range(2):
        for h in range(2):
            load("Y", r("X%d" % s, 0, W, p0=64 * h, p1=64 * h + 64), T.rock[64 * s:64 * s + 64, :], 524288 * (1 + h), False, [r("X0", 0, W)] * s)

    def iota(x, pattern, base, cm):
        kw = {} if BUF[x[0]][2] == "int32" else {"allow_small_or_imprecise_dtypes": True}
        _add(gr, "G", 0.13 + 2 * cnt(x) * CY, lambda: g.iota(ap(x), pattern, base, cm, **kw), [], regs(x) + [("alone", 0, 1)] * (x[4] > 0))

    def pick(o, i, pattern, op, x, base, cm):
        _add(gr, "G", 0.17 + 2 * cnt(o) * CY, lambda: g.affine_select(ap(o), ap(i), pattern, op, x, base, cm), regs(i), regs(o))

    alt = [0]

    def times(o, i, x):
        alt[0] += 1
        if alt[0] % CV:
            ts(o, i, x, A.mult)
        else:
            act(o, i, scale=x)

    PI, k_i, g_i, p31 = [r("ci", k, k + 1) for k in range(4)]
    KF, GF, P31, KS, NK0, NK1, NK2, LB, B4 = [r("cf", k, k + 1) for k in range(9)]
    NKC = [NK0, NK1, NK2]
    ONES, ZERO, BD_, I_, RM = r("ONES", 0, 128), r("ZERO", 0, 128), r("BD"), r("I"), r("RM")
    IND = r("BD", 0, 128, 16)
    fill(r("ZERO"), 0.0); fill(r("ONES"), 1.0)
    iota(PI, [[1, 1]], 0, 1)
    pick(I_, ZERO, [[-1, 128]], A.not_equal, 1.0, 0, 1)
    pick(BD_, ONES, [[-16, 8], [0, 16]], A.is_ge, 0.0, 0, 1); pick(BD_, BD_, [[16, 8], [0, 16]], A.is_ge, 0.0, 15, -1)
    iota(r("REPI"), [[1, 32], [0, 16]], 0, 0)
    ts(k_i, PI, 15, A.bitwise_and); ts(g_i, PI, 4, A.arith_shift_right); ts(p31, PI, 31, A.bitwise_and)
    tc(r("cf", 0, 3), r("ci", 1, 4))
    ts(r("REP"), r("REPI"), P31, A.is_equal)
    for n, x in (("C160", 160.0 * 4096), ("N4096", -4096.0), ("C1040", 1040.0)):
        times(r(n), I_, x)
    act(r("BD16"), BD_, scale=0.0625); act(r("IND128"), IND, scale=128.0)
    tc(r("wlb"), r("wl0", 0, 16, 8))
    mm([(r("B6", 2 * s, 2 * s + 2, p0=64 * h, p1=64 * h + 64), cut(I_, 64 * s, 64 * s + 64), r("wlb"), True, True) for s in range(2) for h in range(2)])
    act(r("WL"), r("B6", 0, 4))
    for j, x in enumerate((32.0, 2.0)):
        act(r("WW", 2 * j, 2 * j + 2), r("B6", 0, 4, 2), scale=x)
    for s in range(2):
        for j, n in enumerate(("W16", "W2")):
            times(r(n + str(s)), BD_, r("WW", 2 * j + s, 2 * j + s + 1))
    LF = r("WL", 1, 4, 2); act(r("TOP"), LF)
    act(KS, KF, scale=-0.0625); act(r("NK16"), I_, scale=KS)
    for m in range(3):
        sc = float(1 << (5 + m))
        act(NKC[m], KF, F.Identity, (613 * m + 2048) * sc - 8388608.0, 37.0 * sc)

    def late_constants():
        for n, x in (("NI16", -0.0625), ("N65536", -65536.0), ("I2080", 2080.0), ("I2048", 2048.0), ("NI", -1.0), ("HALF", 0.5), ("NQ", -0.25)):
            pick(r(n), ZERO, [[-1, 128]], A.not_equal, x, 0, 1)
        iota(r("C15"), [[0, 8], [1, 16]], 0, 0); ts(RM, r("C15"), KF, A.is_equal)
        act(r("CCB"), IND, scale=4096.0); act(r("NEG"), RM, F.Identity, -HUGE, HUGE); act(r("OFF8"), cut(ONES, 0, 8), scale=512.0)
        fill(r("E0"), 0.0)
        iota(r("E0", p0=64, p1=65), [[16, 256]], 0, 0); iota(r("KL", 0, 256, p0=96, p1=97), [[1, 16], [-1, 16]], 0, 0)
        ts(r("KL", 256, 512, p0=96, p1=97), r("KL", 0, 256, p0=96, p1=97), 15, A.bitwise_and); tc(r("E0", p0=96, p1=97), r("KL", 256, 512, p0=96, p1=97))
        for a in range(2):
            e = r("EE", 256 * a, 256 * a + 256)
            pick(e, r("E0"), [[0, 16], [-1, 16]], A.not_equal, -8192.0, -16 * a, 1)
            pick(e, e, [[-1, 16], [0, 16]], A.not_equal, 8192.0, -16 * a - 32, 1)
        for s in range(2):
            fill(r("G%d" % s, p0=64), 1.0)
        _add(gr, "G", 0.17 + 512 * CY, lambda: g.affine_select(T.SH[:], ap(r("ZERO")), [[-16, 8], [0, 2], [-1, 16]], A.not_equal, 1.0, 0, 1), regs(r("ZERO")), regs(r("SH")))
        for d in range(1, 16):
            pick(r("SHF", 128 * d, 128 * d + 128), r("SH", last=slice(d, d + 16)), [[0, 8], [0, 16]], A.is_ge, 0.0, 0, 0)
        iota(r("CI"), [[1, 176]], 0, 0)
        for h in range(2):
            act(cut(LB, 7, 8, p0=64 * h, p1=64 * h + 64), cut(KF, 0, 1, p0=64 * h, p1=64 * h + 64), F.Identity, 48.0 + 64 * h)
            act(cut(B4, 8, 9, p0=64 * h, p1=64 * h + 64), cut(GF, 1, 2, p0=64 * h, p1=64 * h + 64), F.Identity, -4.0 * h)
        ts(r("LA"), r("CI"), LB, A.is_equal)
        iota(r("CB", 0, 32), [[0, 8], [1, 4]], 0, 0); iota(r("CB", 32, 64), [[63, 2], [0, 16]], 1, 0)
        ts(r("CB", 64, 96), r("CB", 0, 32), B4, A.is_equal); tt(r("CM"), r("CB", 64, 96), r("CB", 32, 64), A.mult)
        act(r("CADD"), r("CI", 0, 4), F.Identity, KF, 16.0)
        ts(r("RLI", 0, 2), r("CI", 0, 2), 16.0, A.mult, KF, A.add); ts(r("RLI", 2, 4), r("RLI", 0, 2), 2, A.arith_shift_right); tc(r("RL"), r("RLI", 2, 4))
        fill(r("TM"), 0.0)
        x, y, one = r("T16", 0, 256, p1=32), r("T16", 256, 512, p1=32), r("ONES", p1=32)
        pick(x, one, [[0, 16], [-1, 16]], A.is_gt, 0.0, 0, 1); pick(x, x, [[-1, 16], [1, 16]], A.is_ge, 0.0, 15, -1)
        pick(y, one, [[-1, 16], [0, 16]], A.is_ge, 0.0, 0, 1)
        mm(group(r("B7"), (r("RM", p1=16), r("T16", p1=16))))
        for j in range(2):
            act(r("TM", TMW * j, TMW * j + 256), r("B7", 256 * j, 256 * j + 256))
        for h in range(2):
            pick(r("DUP%d" % h), ZERO, [[0, 2], [-1, 64]], A.not_equal, 1.0, -64 * h, 1)
            pick(r("ND%d" % h), ZERO, [[0, 2], [-1, 64]], A.not_equal, -1.0, -64 * h, 1)
        for t in range(V):
            iota(r("RO", t, t + 1), [[1, 1]], 0, 1 << (t + 2))
        ts(r("RO", 8, 13), r("RO", 0, 5), 127, A.bitwise_and); ts(r("RO", 16, 21), r("RO", 0, 5), 7, A.arith_shift_right)
        tt(r("RF"), r("RO", 8, 13), r("RO", 16, 21), A.add)
        act(r("RF"), r("RF"), F.Identity, -60.0)
        act(r("WJ"), r("RF"), F.Exp, None, -math.log(3.0), extra=1.3); act(r("TH"), r("WJ"), scale=-2.2)
        for t in range(V):
            times(r("RW"), RM, r("WJ", t, t + 1))
            mm(group(r("B7", 8 * t, 8 * t + 8), (r("RW"), IND)))
        act(r("WT"), r("B7", 0, 40))
        iota(r("TRI"), [[0, 2], [16, 8]], 2048, 0); act(r("TRC"), r("TRI"), F.Identity, KF)

    for s in range(2):
        for p in range(2):
            ts(r("N0%d" % s, 64 * p, 64 * p + 64), r("front%d" % s, p, H, 2), -2048.0, A.add)
            act(r("Z0%d" % s, 64 * p, 64 * p + 64), r("vein%d" % s, p, H, 2))

    def view(s):
        gr["lead"] = LEAD * (1 - s)
        return lambda n, *a, **k: r(n + str(s), *a, **k)

    BK, BM, BD, BT = ["B0", "B1"], ["B2", "B3"], ["B4", "B5"], ["B6", "B7"]

    def share(s, t):
        return [NVA, NVB][s] if t == 0 else [NVY, NVZ][s] if t == V - 1 else [NV, NV1][s]

    def numbers(s, t):
        v = view(s); M = BM[s]; K = BK[s]
        Z, N = r("Z%d%d" % (t, s)), r("N%d%d" % (t, s))
        U, v1, x = r(M, 0, 128), r(M, 128, 256), r(M, 256, 384)
        mm(group(U, (v("W16"), Z)))
        aff("HB%d" % s, v("HB"), U, 2.0 ** -16, 159.5 + 2.0 ** -12)
        mm(group(v1, (r("C160"), ONES), (I_, ONES), (v("W2"), Z), (r("N4096"), v("HB"))))
        mm(group(r(K, 0, 128), (Z, I_)))
        aff("NF%d" % s, v("NF"), N, add=2048.0)
        for m in range(3):
            aff("NK%d" % s, v("NK", m * H, m * H + H), N, float(32 << m), NKC[m])
        aff("NZ%d" % s, v("NZ"), r(K, 0, 128), -1.0)
        for k in range(16 if t > 0 else 0):
            o = v("ZR", k, 16 * ZN, 16); z = cut(Z, 0, ZN); wr = [("ZR%d_%d" % (s, k), 0, 1)]
            if k >= ZG:
                _add(gr, "S", FS + max(64, ZN) * CY, lambda o=o, z=z: sca.activation(out=ap(o), in_=ap(z), func=F.Identity), regs(z), wr)
            else:
                _add(gr, "G", 0.17 + 2 * ZN * CY, lambda o=o, z=z: g.affine_select(ap(o), ap(z), [[0, ZN]], A.is_ge, 0.0, 0, 0), regs(z), wr)
        tt(U, v1, v("NF"), A.mult)
        for m in range(3):
            o = (m * H, m * H + H)
            tt(v("QI", *o), U, v("NK", *o), A.add)
            ts(v("QS", *o), v("QI", *o), 5 + m, A.arith_shift_right, 4095, A.bitwise_and)
        for o in OFP:
            aff("O%s%d" % ("FG"[o[0] > 0], s), v("OF", *o), v("QS", *o))
        aff("TB%d" % s, v("TB"), v("QS") if "TB%d" % s in ON_S else v("OF"), add=-2048.0)
        mm(turned(x, (r("BD16"), Z, False), (r("NK16"), ONES, True), (r("C1040"), ONES, True)))
        aff("XS%d" % s, v("XS"), x)
        tt(v("MS"), x, v("XS"), A.is_equal)
        aff("ZQ%d" % s, v("ZQ"), Z, 0.25, 159.625)

    turn = [0, 0]

    def scores(s, t):
        v = view(s); X = v("X", 0, W)
        for m in range(3):
            o = 16 * H * m
            nv = share(s, t)[m]; zn = min(ZN, nv) if m >= ZM and t > 0 else 0; zr = [("ZR%d_%d" % (s, k), 0, 1) for k in range(16)]
            calls = [("S", a, min(H, a + SW)) for a in range(nv, H, SW)] + [("V", a, min(nv, a + VW)) for a in range(0, nv, VW)]
            for q, a, b in calls:
                d = v("D", o + 16 * a, o + 16 * b); ix = v("OF", m * H + a, m * H + b)
                if q == "S":
                    act(d, X, ix=ix)
                elif b <= zn:
                    _add(gr, "V", vcost(d, X, ix, 1), lambda a=a, b=b, d=d, ix=ix: vec.tensor_tensor(
                        out=ap(d), in0=src(X, ix), in1=ap(v("ZR", 16 * a, 16 * b)), op=A.subtract), regs(X, ix) + zr, regs(d))
                else:
                    _add(gr, "V", vcost(d, X, ix, 1), lambda d=d, ix=ix: vec.tensor_copy(out=ap(d), in_=src(X, ix)), regs(X, ix), regs(d))
            for a in CH:
                if a + 32 <= zn:
                    d = v("D", o + 16 * a, o + 16 * a + 512); act(d, d, F.Abs)
                    continue
                turn[0] += 1
                d = v("D", o + 16 * a, o + 16 * a + 512); bk = (BD + [BM[s]])[turn[0] % 3]
                mm(group(r(bk), (v("NZ", p0=a, p1=a + 32), r("REP", p0=a, p1=a + 32)), (I_, d)))
                act(d, r(bk), F.Abs)
            for a in range(0, H, LW):
                x = (o + 16 * a, o + 16 * (a + LW))
                ts(v("L", *x), v("D", *x), r("TOP", s, s + 1), A.is_le, 2.0 * m + 0.4375, A.add)
            for k0 in range(0, 16, KW):
                mm([x for k in range(k0, k0 + KW) for x in group(r(BK[s], m * H + k, m * H + H, 16),
                    (v("D", o + k, o + 16 * H, 16), r("IND128")), (v("L", o + k, o + 16 * H, 16), IND))], (m * H + 8 * k0, m * H + 8 * (k0 + KW)))
            blk = gr["bulk"]; gr["bulk"] = False
            if m == 0:
                aff("K0%d" % s, v("K0"), r(BK[s], 0, 128))
            if m == 1:
                tt(v("K1"), v("K0"), r(BK[s], 128, 256), A.min)
            gr["bulk"] = blk

    def choose(s, t):
        v = view(s); B = BK[s]; M = BM[s]; N = r("N%d%d" % (t, s))
        mm([y for m in range(3) for y in group(r(M, m * H, m * H + H), (v("TB", m * H, m * H + H), I_))] + group(r(M, 384, 512), (N, I_)))
        tt(v("KI"), v("K1"), r(B, 256, 384), A.min)
        ts(v("YI"), v("KI"), 112, A.bitwise_and)
        ts(v("OK"), v("KI"), 16, A.bitwise_and)
        for m in range(3):
            ts(v("MK", m * H, m * H + H), v("YI"), 32.0 * m + 16.0, A.is_equal)
        tt(v("PR", 384, 512), r(BM[s], 384, 512), v("OK"), A.mult)
        tt(v("PR", 0, 384), r(BM[s], 0, 384), v("MK"), A.mult)
        mm(group(r(B, 384, 512), (I_, N), (v("PR", 384, 512), r("NI16")), *[(v("PR", m * H, m * H + H), I_) for m in range(3)]))

    def meet(s, t):
        v = view(s); NP = r(BK[s], 384, 512); R = BM[s]; K = BK[s]
        aff("FC%d" % s, v("FC"), NP)
        mm([(r(R, 128 * x + 64 * h, 128 * x + 64 * h + 64, p0=32 * j, p1=32 * j + 32), cut(I_, 64 * h + 32 * x, 64 * h + 32 * x + 32),
             v("FC", 64 * j, 64 * j + 64), True, True) for x in range(2) for h in range(2) for j in range(2)])
        aff("G%d" % s, v("G", p1=64), r(R, 0, 256, p1=64), 0.125, 1287.5625)
        for x in range(2):
            mm([(r(BT[x], 256 * a, 256 * a + 256), v("G", 128 * x, 128 * x + 128, p1=97), r("EE", 256 * a, 256 * a + 256, p1=97), True, True) for a in range(2)])
            for a in range(2):
                o, i = v("R", 2 * x + a, 2 * x + a + 1), r(BT[x], 256 * a, 256 * a + 256)
                _add(gr, "V", FV + 256 * CY, lambda o=o, i=i: vec.tensor_reduce(out=ap(o), in_=ap(i), axis=AxisListType.X, op=A.min, apply_absolute_value=True), regs(i), regs(o))
        ts(v("W8", 0, 4), v("R"), 4, A.arith_shift_right); ts(v("W8", 4, 8), v("R"), 15, A.bitwise_and)
        tt(v("RR"), v("W8"), r("CM"), A.mult, ix=r("RL"))
        mm([y for x in range(2) for y in group(r(R, 256 + 4 * x, 260 + 4 * x), *([(I_, r("CADD"))] * x + [
            (r("LA", 48 - 16 * a, 176 - 16 * a), v("RR", 16 * x + 4 * a, 16 * x + 4 * a + 4)) for a in range(4)]))])
        ts(v("LO"), r(R, 256, 264), TMW - 1.0, A.min)
        if t < V - 1:
            act(v("MT"), r(R, 256, 260), F.Sign, 255.5, -1.0)
        J = v("FC", 64, 128)
        for x in range(2):
            mm([(r(BT[x], 64 * d, 64 * d + 64), r("SHF", 128 * (8 * x + d), 128 * (8 * x + d + 1)) if x + d else I_, J, True, True) for d in range(8)])
            act(v("TAB", 512 * x, 512 * x + 512), r(BT[x]))
        for j in range(2):
            act(v("MM", 64 * j, 64 * j + 64), r("TM", TMW * j, TMW * j + TMW), ix=v("LO", 0, 4))
        mm(group(r(K, 0, 64), (r("I2080"), J), (r("I2048"), v("FC", 0, 64)), (v("W16"), r("Z%d%d" % (t, s), 64, 128)), (r("N65536"), v("HB", 64, 128))))
        aff("JA%d" % s, v("JA"), r(K, 0, 64), add=65536.0 * 161 - 4194304.0)
        tt(r(K, 64, 128), r(K, 448, 512), v("FC", 0, 64), A.mult)
        tt(v("JQ"), r(K, 64, 128), v("JA"), A.add)
        ts(v("JT"), v("JQ"), 5, A.arith_shift_right, 4095, A.bitwise_and)
        aff("JC%d" % s, r(K, 64, 128), v("JT"), add=-2048.0)
        tt(v("PB"), NP, v("MM"), A.mult)
        tt(v("PA", 64, 128), r(K, 64, 128), v("MM", 64, 128), A.mult)
        tt(v("PA", 0, 64), v("TAB"), v("MM", 0, 64), A.mult, ix=v("LO", 4, 8))
        mm(turned(r(K, 128, 256), (I_, v("FC"), False), (r("NI"), v("PB"), False), (I_, v("PA"), False)))

    NE = []

    def send(name, s, t):
        x, y = r("S%s%d%d" % (name, t, s)), r("%s%d%d" % (name, t + 1, s))
        rid, pid, _ = topo.addr(nxt)
        en = topo.engines(core, nxt)
        msk = sum(1 << e for e in en)
        rs = "a%s%d%d" % (name.lower(), t + 1, s)
        NE.append(len(en))
        ln = ("link", 8 * len(NE), 8 * len(NE) + 1)
        _add(gr, "G", 0.5, lambda: g.remote_dma(ap(y), ap(x), T.sem[rs], T.sem.loc, pid, rid, msk), regs(x), [ln], sem="loc")
        _add(gr, "A", 2.5, None, [ln], regs(y), sem=(rs, len(en)))

    def mine(s, t):
        v = view(s); K, R = BK[s], BM[s]
        F2, ET, EB, EL = r(K, 128, 256), r(R, 0, 128), r(R, 128, 256), r(R, 256, 264)
        Z = r("Z%d%d" % (t, s)); rows = slice(64 * s, 64 * s + 64)
        tt(v("FS"), F2, v("MS"), A.mult)
        mm(group(ET, (v("FS"), BD_)) + group(EB, (BD_, v("FS"))))
        if t < V - 1:
            aff("SN%d" % s, r("SN%d%d" % (t, s)), F2); send("N", s, t)
        else:
            for q in range(2):
                act(v("YF", 64 * q, 64 * q + 64), r(K, 128 + q, 256, 2), F.Identity, 2048.0)
            for h in range(2):
                store("Y", T.yf[rows, H * h:H * h + H], v("YF", p0=64 * h, p1=64 * h + 64), 32768)
        tt(v("EM"), ET, RM, A.mult); aff("EC%d" % s, v("EC"), EB)
        mm(group(EL, (v("EM"), IND)))
        aff("YO%d" % s, v("YO"), EL, add=2048.0); aff("EL%d" % s, v("EL"), EL)
        act(v("YB"), v("X", 0, W), ix=v("YO"))
        mm(turned(r(K, 0, 128), (r("HALF"), Z, False), (r("NQ"), ONES, True), (r("HALF"), v("YB"), True)))
        if t < V - 1:
            ts(r("SZ%d%d" % (t, s)), r(K, 0, 128), 12582912.0, A.add, -12582912.0, A.add); send("Z", s, t)
        else:
            act(v("ZH"), r(K, 0, 128), F.Identity, 12582912.0)
            for q in range(2):
                act(v("YZ", 64 * q, 64 * q + 64), v("ZH", q, 128, 2), F.Identity, -12582912.0)
            for h in range(2):
                store("Y", T.yz[rows, H * h:H * h + H], v("YZ", p0=64 * h, p1=64 * h + 64), 16384)
        mm([x for h in range(2) for x in turned(r(K, 256 + 128 * h, 384 + 128 * h), (r("ND%d" % h), v("ZQ"), False), (r("DUP%d" % h), v("YB"), True))])
        act(v("NX"), r(K, 256, 512), F.Relu, 160.0)
        for c in range(8):
            ts(v("ED", H * c, H * c + H), v("EC"), v("EL", c, c + 1), A.is_equal, r("WT", 8 * t + c, 8 * t + c + 1), A.mult)
        mm(group(ET, (I_, r("NEG")), *[(v("ED", H * c, H * c + H), BD_) for c in range(8)]))
        act(v("DT"), ET, F.Sign, r("TH", t, t + 1))
        mm([x for h in range(2) for p in range(2) for x in group(r(R, 272 + 8 * h, 280 + 8 * h, p0=64 * p, p1=64 * p + 64),
            (cut(ONES, 0, 64), r("OFF8")), (v("EM", 64 * h, 64 * h + 64), IND), (v("DT", 64 * h, 64 * h + 64), r("CCB")))])
        tt(v("T1"), r(R, 272, 288), r("TRC"), A.min)
        aff("SO%d" % s, v("SO"), v("T1"), add=2048.0)
        for h in (1, 0):
            so, nx = v("SO", 8 * h, 8 * h + 8), v("NX", H * h, H * h + H)
            _add(gr, "V", 0.05 + H * SCATTER * CY, lambda so=so, nx=nx: vec.tensor_copy(out=src(v("X"), so), in_=ap(nx)), regs(so, nx), regs(v("X")))
        if t == V - 1:
            for h in range(2):
                store("YS"[h], T.yx[rows, 2048 * h:2048 * h + 2048], v("X", 2048 * h, 2048 * h + 2048, p0=64 * h, p1=64 * h + 64), 262144 * (1 + h))

    def limits():
        B = BT[1]
        mm(group(r(B, 0, 4), (ONES, r("MT0")), (ONES, r("MT1"))))
        for k in range(2):
            act(r("CN", 2, 6), r(B, 0, 4), acc=r("CN", k, k + 1))
        ts(r("EI", 0, 2), r("CN", 0, 2), 0.5, A.mult, 512.0, A.add); ts(r("EI", 2, 4), r("EI", 0, 2), 3, A.bitwise_and)
        tt(r("TOP"), r("EI", 2, 4), LF, A.add)

    numbers(0, 0)
    for o in gr["ops"]:
        o["lead"] = 1e3
    numbers(1, 0)
    late_constants()
    for t in range(V):
        for s in range(2):
            gr["bulk"] = 2 * t + s + 1
            scores(s, t)
            gr["bulk"] = False
            choose(s, t)
        for s in range(2):
            meet(s, t)
            if s == 1 and t < V - 1:
                limits()
            mine(s, t)
            if t < V - 1:
                numbers(s, t + 1)

    ops = gr["ops"]
    if not ORDER:
        ORDER.extend(_order(ops))
    seq, fin = ORDER
    eng = {"V": vec, "S": sca, "P": ten, "G": g, "Y": syn}
    cs = {"V": "cV", "S": "cS", "P": "cP", "G": "cG"}
    count = {q: 0 for q in eng}
    seen = {q: {} for q in eng}
    for c in seq:
        o = ops[c]; q = o["q"]
        if q == "A":
            o["key"] = o["sem"]; o["vc"] = {}
            continue
        S = seen[q]
        want = {}
        for d in o["deps"]:
            k = ops[d].get("key")
            if k is not None and S.get(k[0], 0) < k[1] and want.get(k[0], (0, None))[0] < k[1]:
                want[k[0]] = (k[1], d)
        for nm, (val, d) in sorted(want.items(), key=lambda kv: -fin[kv[1][1]]):
            if S.get(nm, 0) >= val:
                continue
            eng[q].wait_ge(T.sem[nm], val)
            S[nm] = max(S.get(nm, 0), val)
            for n2, v2 in ops[d]["vc"].items():
                S[n2] = max(S.get(n2, 0), v2)
        x = o["fn"]()
        o["vc"] = dict(S)
        if o["sem"] is None:
            count[q] += 1
            x.then_inc(T.sem[cs[q]], 1)
            o["key"] = (cs[q], count[q])
        elif o["sem"] != "loc":
            x.then_inc(T.sem[o["sem"]], 16)
            o["key"] = (o["sem"], 16)
    for q in "VSPG":
        if count[q]:
            g.wait_ge(T.sem[cs[q]], count[q])
    for k in range(dn[0]):
        g.wait_ge(T.sem["d%d" % k], 16)
    if NE:
        g.wait_ge(T.sem.loc, sum(NE))
